import numpy as np
import ml_dtypes


def mxq(x, axis, fmt="e4m3"):
    dtype, down = {"e4m3": (ml_dtypes.float8_e4m3fn, 7), "e5m2": (ml_dtypes.float8_e5m2, 14)}[fmt]
    v = np.moveaxis(np.asarray(x, np.float32).astype(ml_dtypes.bfloat16).astype(np.float64), axis, -1)
    blocks = v.reshape(v.shape[:-1] + (-1, 32))
    amax = np.abs(blocks).max(-1, keepdims=True)
    byte = np.maximum(np.where(amax > 0, np.frexp(amax)[1] - 1 + 127, 0) - down, 1)
    scale = np.exp2(byte - 127.0)
    codes = (blocks / scale).astype(np.float32).astype(dtype).astype(np.float64)
    return np.moveaxis((codes * scale).reshape(v.shape), -1, axis)


WIDE = False


def mx_kscale(k):
    if not WIDE:
        return np.ones(k)
    levels = np.array([10, -10, 5, -5, 0])
    if k % 512:
        return np.exp2(np.random.permutation(np.resize(levels, k // 32))).repeat(32)
    a = np.empty((k // 512, 16))
    for p in range(k // 512):
        a[p, :8] = np.random.permutation(np.resize(levels, 8))
        for g in range(8):
            far = levels[np.abs(levels - a[p, g]) >= 10]
            a[p, g + 8] = far[np.random.randint(len(far))]
    return np.exp2(a.ravel()).repeat(32)


def f64(x):
    return np.asarray(x).astype(np.float64)


def striped(idx):
    return np.tile(idx.reshape(-1, 16).T, (8, 1)).astype(np.uint16)


def unstriped(offs):
    return offs[:16].T.reshape(-1).astype(np.int64)


E2M1 = np.array([0.0, 0.5, 1.0, 1.5, 2.0, 3.0, 4.0, 6.0, -0.0, -0.5, -1.0, -1.5, -2.0, -3.0, -4.0, -6.0])


def pack_weight(w, fmt):
    k, n = w.shape
    w = f64(np.asarray(w, np.float32).astype(ml_dtypes.bfloat16)).reshape(k // 32, 32, n)
    amax = np.abs(w).max(1)
    if fmt == "e4m3":
        byte = np.frexp(amax)[1] - 1 + 127 - 7
    else:
        mant, ex = np.frexp(amax / 6.0)
        byte = np.where(mant > 0.5, ex, ex - 1) + 127
    byte = np.clip(np.where(amax > 0, byte, 1), 1, 254)
    scaled = (w * np.exp2(127.0 - byte)[:, None, :]).reshape(k, n).astype(np.float32)
    by_word = np.ascontiguousarray(scaled.reshape(k // 512, 128, 4, n).transpose(0, 1, 3, 2))
    if fmt == "e4m3":
        words = by_word.astype(ml_dtypes.float8_e4m3fn).view(np.uint8)
    else:
        c = by_word.astype(ml_dtypes.float4_e2m1fn).view(np.uint8) & 0xF
        words = (c[..., 0::2] | (c[..., 1::2] << 4)).reshape(k // 512, 128, 2 * n)
    return np.ascontiguousarray(words), np.ascontiguousarray(byte.astype(np.uint8).reshape(k // 512, 16, n))


def unpack_weight(words, scales, fmt):
    g, _, n = scales.shape
    words = np.ascontiguousarray(words).reshape(g, 128, n, -1)
    if fmt == "e4m3":
        vals = words.view(ml_dtypes.float8_e4m3fn).astype(np.float64)
    else:
        nib = np.empty((g, 128, n, 4), np.uint8)
        nib[..., 0::2] = words & 0xF
        nib[..., 1::2] = words >> 4
        vals = E2M1[nib]
    vals = vals * np.repeat(np.exp2(scales.astype(np.float64) - 127.0), 8, axis=1)[..., None]
    return vals.transpose(0, 1, 3, 2).reshape(g * 512, n)


K, T, E, C, N = 256, 768, 6, 256, 512


def by_expert(wq, xq):
    return np.concatenate([wq[e].T @ xq[:, e * C:(e + 1) * C] for e in range(E)], axis=1)


def setup_inputs():
    n = np.random.standard_normal
    v = mx_kscale(N)
    first = np.random.permutation(np.repeat(np.arange(E), T // E))
    second = (first + 1 + np.random.permutation(np.repeat(np.arange(E - 1), -(-T // (E - 1)))[:T])) % E
    while np.bincount(second, minlength=E).max() != T // E:
        load = np.bincount(second, minlength=E); hi, lo = int(load.argmax()), int(load.argmin())
        t = np.flatnonzero((second == hi) & (first != lo))[0]; second[t] = lo
    slot_token = np.empty(E * C, np.int64); pos = np.empty((2, T), np.int64); fill = np.zeros(E, np.int64)
    place = np.stack([np.random.permutation(C) for _ in range(E)])
    for r, deal in enumerate((first, second)):
        for t in np.random.permutation(T):
            e = deal[t]; j = e * C + place[e, fill[e]]; fill[e] += 1; slot_token[j] = t; pos[r, t] = j
    g = np.random.uniform(0.2, 0.8, T)
    w_slot = np.empty(E * C); w_slot[pos[0]] = g; w_slot[pos[1]] = 1.0 - g
    dq = pack_weight(n((N, T)) * v[:, None], "e4m3")
    dk = pack_weight(n((N, T)) * v[:, None], "e4m3")
    dv = pack_weight(n((N, T)) * v[:, None], "e4m3")
    wq = [pack_weight(m, "e2m1") for m in n((E, N, K)) / np.sqrt(N) / v[None, :, None]]
    wv = [pack_weight(m, "e2m1") for m in n((E, N, K)) / np.sqrt(N) / v[None, :, None]]
    return {
        "dq_words": dq[0],
        "dq_scales": dq[1],
        "dk_words": dk[0],
        "dk_scales": dk[1],
        "dv_words": dv[0],
        "dv_scales": dv[1],
        "wq_words": np.stack([m[0] for m in wq]),
        "wq_scales": np.stack([m[1] for m in wq]),
        "wk": (n((E, N, K)) / np.sqrt(N) / v[None, :, None]).astype(np.float32),
        "wv_words": np.stack([m[0] for m in wv]),
        "wv_scales": np.stack([m[1] for m in wv]),
        "gate": (np.tile(w_slot, (128, 1))).astype(np.float32),
        "offs": striped(slot_token),
        "pos1": striped(pos[0]),
        "pos2": striped(pos[1]),
    }


def reference(dq_words, dq_scales, dk_words, dk_scales, dv_words, dv_scales, wq_words, wq_scales, wk, wv_words, wv_scales, gate, offs, pos1, pos2):
    wq = np.stack([unpack_weight(wq_words[e], wq_scales[e], "e2m1") for e in range(E)])
    wkq = mxq(f64(wk), 1, "e4m3")
    wv = np.stack([unpack_weight(wv_words[e], wv_scales[e], "e2m1") for e in range(E)])
    idx = unstriped(offs)
    gq, gk, gv = [unpack_weight(w, s, "e4m3")[:, idx] for w, s in ((dq_words, dq_scales), (dk_words, dk_scales), (dv_words, dv_scales))]
    dx = f64(gate[:1]) * (by_expert(wq, gq) + by_expert(wkq, gk) + by_expert(wv, gv))
    out = dx[:, unstriped(pos1)] + dx[:, unstriped(pos2)]
    return out

@@ -1,0 +1,255 @@
+from contextlib import ExitStack
+
+import concourse.mybir as mybir
+from concourse.masks import make_identity
+
+K, T, E, C, N = 256, 768, 6, 256, 512
+S = E * C
+P = 128
+FLOPS = 2 * 3 * S * N * K
+
+F32 = mybir.dt.float32
+BF16 = mybir.dt.bfloat16
+I32 = mybir.dt.int32
+U32 = mybir.dt.uint32
+U16 = mybir.dt.uint16
+U8 = mybir.dt.uint8
+FP8X4 = mybir.dt.float8_e4m3fn_x4
+FP4X4 = mybir.dt.float4_e2m1fn_x4
+COPY = mybir.ActivationFunctionType.Copy
+MULT = mybir.AluOpType.mult
+ADD = mybir.AluOpType.add
+
+
+def tile_moe_qkb_kernel(
+    tc, dq_words, dq_scales, dk_words, dk_scales, dv_words, dv_scales,
+    wq_words, wq_scales, wk, wv_words, wv_scales, gate, offs, pos1, pos2, out,
+):
+    nc = tc.nc
+    with ExitStack() as ctx:
+        lists = ctx.enter_context(tc.tile_pool(name="lists", bufs=1))
+        sb = ctx.enter_context(tc.tile_pool(name="sb", bufs=1))
+        ps = ctx.enter_context(tc.psum_pool(name="ps", bufs=1))
+
+        def held(name, shape, dtype):
+            return sb.tile(shape, dtype, name=name, align_bytes=64)
+
+        offs_sb = lists.tile([P, S // 16], U16, name="offs_sb")
+        pos_sb = [lists.tile([P, T // 16], U16, name="pos%d_sb" % r) for r in (1, 2)]
+
+        names = ("q", "k", "v")
+        tok_words = {g: held("tok_words_" + g, [P, T], I32) for g in names}
+        tok_scales = {g: held("tok_scales_" + g, [P, T], U8) for g in names}
+        q_slot_words = held("slot_words_q", [P, S], U32)
+        slot_words = {}
+        slot_scales = {}
+        w4_words = {g: held("w4_words_" + g, [P, E, 2 * K], U8) for g in ("q", "v")}
+        w_scales = {g: held("w_scales_" + g, [P, E, K], U8) for g in names}
+        wk_words = held("wk_words", [P, E, K], U32)
+        wk_raw = [held("wk_raw%d" % e, [P, 4, K], F32) for e in range(E)]
+        wk_bf = held("wk_bf", [P, E, K, 4], BF16)
+        ident = held("ident", [P, P], F32)
+        gate_rows = held("gate_rows", [P, P], F32)
+        gate_cols = held("gate_cols", [P, 16], F32)
+        gate_last = held("gate_last", [P, C], F32)
+        dx = [held("dx%d" % h, [P, S], F32) for h in range(2)]
+        picked = [[held("picked%d%d" % (h, r), [P, T], F32) for r in range(2)] for h in range(2)]
+        summed = [held("summed%d" % h, [P, T], F32) for h in range(2)]
+
+        tok_words_hbm = {"q": dq_words, "k": dk_words, "v": dv_words}
+        tok_scales_hbm = {"q": dq_scales, "k": dk_scales, "v": dv_scales}
+        w4_words_hbm = {"q": wq_words, "v": wv_words}
+        w4_scales_hbm = {"q": wq_scales, "v": wv_scales}
+
+        def load_tok_scales(g):
+            rows = tok_scales_hbm[g][0].rearrange("(q r) t -> r q t", r=4)
+            for r in range(4):
+                nc.sync.dma_start(out=tok_scales[g][r:P:32, :].bitcast(I32), in_=rows[r].bitcast(I32))
+
+        def load_tok_words(g):
+            nc.sync.dma_start(out=tok_words[g][:], in_=tok_words_hbm[g][0].rearrange("p t d -> p (t d)").bitcast(I32))
+
+        def load_w4_scales(g):
+            rows = w4_scales_hbm[g].rearrange("e s (q r) c -> r q (e s) c", r=4)
+            for r in range(4):
+                nc.sync.dma_start(out=w_scales[g][r:P:32, :, :].bitcast(I32), in_=rows[r].bitcast(I32))
+
+        def load_w4_words(g):
+            nc.sync.dma_start(out=w4_words[g][:].bitcast(I32),
+                              in_=w4_words_hbm[g].rearrange("e s p b -> p (e s) b").bitcast(I32))
+
+        def load_wk(e):
+            nc.sync.dma_start(out=wk_raw[e][:], in_=wk[e].rearrange("(p j) c -> p j c", j=4))
+
+        def round_wk(e):
+            nc.scalar.copy(out=wk_bf[:, e].rearrange("p (c i) j -> p c j i", i=4),
+                           in_=wk_raw[e][:].rearrange("p j (c i) -> p c j i", i=4))
+
+        def quantize_wk(a, b):
+            nc.vector.quantize_mx(
+                out=wk_words[:, a:b, :].rearrange("p e c -> p (e c)").bitcast(FP8X4),
+                scales=w_scales["k"][:, a:b, :].rearrange("p e c -> p (e c)"),
+                in_=wk_bf[:, a:b].rearrange("p e c j -> p (e c j)"),
+            )
+
+        def new_slot_tiles(a, b):
+            for g in names:
+                scales = sb.tile([P, (b - a) * C], U8, name="slot_scales_" + g, bufs=2, align_bytes=64)
+                for e in range(a, b):
+                    slot_scales[g, e] = (scales, a * C)
+                if g == "q":
+                    for e in range(a, b):
+                        slot_words[g, e] = (q_slot_words, 0)
+                else:
+                    words = sb.tile([P, (b - a) * C], U32, name="slot_words_" + g, bufs=2, align_bytes=64)
+                    for e in range(a, b):
+                        slot_words[g, e] = (words, a * C)
+
+        def gather_scales(g, a, b):
+            dst, first = slot_scales[g, a // C]
+            nc.vector.tensor_copy(out=dst[:, a - first : b - first],
+                                  in_=tok_scales[g][:].indirect(offs_sb[:, a // 16 : b // 16]))
+
+        def gather_words(g, a, b):
+            dst, first = (q_slot_words, 0) if g == "q" else slot_words[g, a // C]
+            nc.vector.tensor_copy(out=dst[:, a - first : b - first],
+                                  in_=tok_words[g][:].bitcast(U32).indirect(offs_sb[:, a // 16 : b // 16]))
+
+        def weight_operand(g, e, h):
+            cols = slice(h * P, (h + 1) * P)
+            if g == "k":
+                return wk_words[:, e, cols].bitcast(FP8X4), w_scales[g][:, e, cols]
+            return w4_words[g][:, e, 2 * h * P : 2 * (h + 1) * P].bitcast(FP4X4), w_scales[g][:, e, cols]
+
+        def slot_operand(g, blk):
+            words, first_w = slot_words[g, blk // 2]
+            scales, first_s = slot_scales[g, blk // 2]
+            a = blk * P
+            return words[:, a - first_w : a - first_w + P].bitcast(FP8X4), scales[:, a - first_s : a - first_s + P]
+
+        def three_passes(acc, e, blk, h, slots_stationary):
+            for i, g in enumerate(names):
+                w, w_sc = weight_operand(g, e, h)
+                x, x_sc = slot_operand(g, blk)
+                if slots_stationary:
+                    nc.tensor.matmul_mx(out=acc, lhsT=x, lhsT_scale=x_sc, rhs=w, rhs_scale=w_sc,
+                                        start=(i == 0), stop=(i == 2))
+                else:
+                    nc.tensor.matmul_mx(out=acc, lhsT=w, lhsT_scale=w_sc, rhs=x, rhs_scale=x_sc,
+                                        start=(i == 0), stop=(i == 2))
+
+        def expert_turned(e, halves):
+            n = len(halves)
+            sums = ps.tile([P, 2, n * P], F32, name="sums", tag="sums", bufs=3)
+            gated = sb.tile([P, 2, n * P], F32, name="gated", tag="gated", bufs=3, align_bytes=64)
+            turned = ps.tile([P, n, C], F32, name="turned", tag="turned", bufs=2)
+            for u in range(2):
+                for i, h in enumerate(halves):
+                    three_passes(sums[:, u, i * P : (i + 1) * P], e, 2 * e + u, h, True)
+            for u in range(2):
+                nc.scalar.activation(out=gated[:, u, :], in_=sums[:, u, :], func=COPY,
+                                     scale=gate_cols[:, 2 * e + u : 2 * e + u + 1])
+            for i, h in enumerate(halves):
+                for u in range(2):
+                    nc.tensor.transpose(out=turned[:, i, u * P : (u + 1) * P],
+                                        in_=gated[:, u, i * P : (i + 1) * P], identity=ident[:])
+            for i, h in enumerate(halves):
+                nc.scalar.copy(out=dx[h][:, e * C : (e + 1) * C], in_=turned[:, i, :])
+
+        def pick(h, r, a, b):
+            nc.vector.tensor_copy(out=picked[h][r][:, a:b], in_=dx[h][:].indirect(pos_sb[r][:, a // 16 : b // 16]))
+
+        def add_and_store(h, a, b):
+            nc.vector.tensor_tensor(out=summed[h][:, a:b], in0=picked[h][0][:, a:b], in1=picked[h][1][:, a:b], op=ADD)
+            nc.sync.dma_start(out=out[h * P : (h + 1) * P, a:b], in_=summed[h][:, a:b])
+
+        for g in ("q", "k"):
+            nc.gpsimd.memset(tok_scales[g][:].bitcast(I32), 0)
+        make_identity(nc, ident[:])
+        nc.vector.memset(tok_scales["v"][:].bitcast(I32), 0)
+        for g in ("q", "v"):
+            nc.vector.memset(w_scales[g][:].bitcast(I32), 0)
+
+        nc.sync.dma_start(out=offs_sb[:], in_=offs)
+        load_tok_words("q")
+        load_tok_scales("q")
+        load_tok_words("k")
+        load_tok_scales("k")
+        load_wk(0)
+        load_wk(1)
+        load_tok_scales("v")
+        load_w4_scales("q")
+        load_w4_scales("v")
+        load_wk(2)
+        load_tok_words("v")
+        load_w4_words("q")
+        load_w4_words("v")
+        nc.sync.dma_start(out=gate_rows[:], in_=gate.rearrange("p (a b) -> (p a) b", b=P)[0:P, :])
+        load_wk(3)
+        load_wk(4)
+        load_wk(5)
+        nc.sync.dma_start(out=gate_last[:], in_=gate[:, S - C : S])
+        nc.sync.dma_start(out=pos_sb[0][:], in_=pos1)
+        nc.sync.dma_start(out=pos_sb[1][:], in_=pos2)
+
+        for e in range(3):
+            round_wk(e)
+        gate_bank = ps.tile([P, P], F32, name="gate_bank")
+        nc.tensor.transpose(out=gate_bank[:], in_=gate_rows[:], identity=ident[:])
+        nc.scalar.copy(out=gate_cols[:], in_=gate_bank[:, 0:16])
+        for e in range(3, E):
+            round_wk(e)
+
+        for a in range(0, S, 512):
+            gather_words("q", a, a + 512)
+
+        def gather_rest(a, b):
+            gather_scales("q", a, b)
+            gather_words("k", a, b)
+            gather_scales("k", a, b)
+            gather_scales("v", a, b)
+            gather_words("v", a, b)
+
+        new_slot_tiles(0, 1)
+        new_slot_tiles(1, 3)
+        quantize_wk(0, 2)
+        gather_rest(0, C)
+        expert_turned(0, (0, 1))
+        gather_rest(C, 3 * C)
+        quantize_wk(2, 3)
+        expert_turned(1, (0, 1))
+        expert_turned(2, (0, 1))
+        new_slot_tiles(3, 4)
+        gather_rest(3 * C, 4 * C)
+        quantize_wk(3, 4)
+        expert_turned(3, (0, 1))
+        new_slot_tiles(4, 5)
+        quantize_wk(4, 6)
+        gather_rest(4 * C, 5 * C)
+        expert_turned(4, (0, 1))
+
+        new_slot_tiles(5, 6)
+        a, b = 5 * C, 6 * C
+        gather_scales("q", a, b)
+        gather_words("k", a, b)
+        gather_scales("k", a, b)
+        gather_words("v", a, b)
+        direct = [ps.tile([P, P], F32, name="direct%d" % u) for u in range(2)]
+        for u in range(2):
+            gather_scales("v", a + u * P, a + (u + 1) * P)
+            three_passes(direct[u][:], 5, 10 + u, 0, False)
+        expert_turned(5, (1,))
+        for u in range(2):
+            nc.vector.tensor_tensor(out=dx[0][:, a + u * P : a + (u + 1) * P], in0=direct[u][:],
+                                    in1=gate_last[:, u * P : (u + 1) * P], op=MULT)
+
+        pick(0, 0, 0, T)
+        pick(0, 1, 0, T)
+        pick(1, 0, 0, T)
+        add_and_store(0, 0, T)
+        pick(1, 1, 0, 384)
+        pick(1, 1, 384, 576)
+        add_and_store(1, 0, 384)
+        pick(1, 1, 576, T)
+        add_and_store(1, 384, 576)
+        add_and_store(1, 576, T)

@@ -40,7 +40,6 @@ def tile_moe_qkb_kernel(
         names = ("q", "k", "v")
         tok_words = {g: held("tok_words_" + g, [P, T], I32) for g in names}
         tok_scales = {g: held("tok_scales_" + g, [P, T], U8) for g in names}
-        q_slot_words = held("slot_words_q", [P, S], U32)
         slot_words = {}
         slot_scales = {}
         w4_words = {g: held("w4_words_" + g, [P, E, 2 * K], U8) for g in ("q", "v")}
@@ -61,17 +60,17 @@ def tile_moe_qkb_kernel(
         w4_words_hbm = {"q": wq_words, "v": wv_words}
         w4_scales_hbm = {"q": wq_scales, "v": wv_scales}
 
-        def load_tok_scales(g):
+        def load_tok_scales(g, rs):
             rows = tok_scales_hbm[g][0].rearrange("(q r) t -> r q t", r=4)
-            for r in range(4):
+            for r in rs:
                 nc.sync.dma_start(out=tok_scales[g][r:P:32, :].bitcast(I32), in_=rows[r].bitcast(I32))
 
         def load_tok_words(g):
             nc.sync.dma_start(out=tok_words[g][:], in_=tok_words_hbm[g][0].rearrange("p t d -> p (t d)").bitcast(I32))
 
-        def load_w4_scales(g):
+        def load_w4_scales(g, rs):
             rows = w4_scales_hbm[g].rearrange("e s (q r) c -> r q (e s) c", r=4)
-            for r in range(4):
+            for r in rs:
                 nc.sync.dma_start(out=w_scales[g][r:P:32, :, :].bitcast(I32), in_=rows[r].bitcast(I32))
 
         def load_w4_words(g):
@@ -92,28 +91,18 @@ def tile_moe_qkb_kernel(
                 in_=wk_bf[:, a:b].rearrange("p e c j -> p (e c j)"),
             )
 
-        def new_slot_tiles(a, b):
-            for g in names:
-                scales = sb.tile([P, (b - a) * C], U8, name="slot_scales_" + g, bufs=2, align_bytes=64)
-                for e in range(a, b):
-                    slot_scales[g, e] = (scales, a * C)
-                if g == "q":
-                    for e in range(a, b):
-                        slot_words[g, e] = (q_slot_words, 0)
-                else:
-                    words = sb.tile([P, (b - a) * C], U32, name="slot_words_" + g, bufs=2, align_bytes=64)
-                    for e in range(a, b):
-                        slot_words[g, e] = (words, a * C)
+        def new_slot_tiles(g, e):
+            depth = 4 if g == "v" else 3
+            slot_words[g, e] = sb.tile([P, C], U32, name="slot_words_" + g, bufs=depth, align_bytes=64)
+            slot_scales[g, e] = sb.tile([P, C], U8, name="slot_scales_" + g, bufs=depth, align_bytes=64)
 
-        def gather_scales(g, a, b):
-            dst, first = slot_scales[g, a // C]
-            nc.vector.tensor_copy(out=dst[:, a - first : b - first],
-                                  in_=tok_scales[g][:].indirect(offs_sb[:, a // 16 : b // 16]))
+        def gather_scales(g, e, a, b):
+            nc.vector.tensor_copy(out=slot_scales[g, e][:, a:b],
+                                  in_=tok_scales[g][:].indirect(offs_sb[:, (e * C + a) // 16 : (e * C + b) // 16]))
 
-        def gather_words(g, a, b):
-            dst, first = (q_slot_words, 0) if g == "q" else slot_words[g, a // C]
-            nc.vector.tensor_copy(out=dst[:, a - first : b - first],
-                                  in_=tok_words[g][:].bitcast(U32).indirect(offs_sb[:, a // 16 : b // 16]))
+        def gather_words(g, e):
+            nc.vector.tensor_copy(out=slot_words[g, e][:],
+                                  in_=tok_words[g][:].bitcast(U32).indirect(offs_sb[:, e * C // 16 : (e + 1) * C // 16]))
 
         def weight_operand(g, e, h):
             cols = slice(h * P, (h + 1) * P)
@@ -122,13 +111,11 @@ def tile_moe_qkb_kernel(
             return w4_words[g][:, e, 2 * h * P : 2 * (h + 1) * P].bitcast(FP4X4), w_scales[g][:, e, cols]
 
         def slot_operand(g, blk):
-            words, first_w = slot_words[g, blk // 2]
-            scales, first_s = slot_scales[g, blk // 2]
-            a = blk * P
-            return words[:, a - first_w : a - first_w + P].bitcast(FP8X4), scales[:, a - first_s : a - first_s + P]
+            cols = slice(blk % 2 * P, (blk % 2 + 1) * P)
+            return slot_words[g, blk // 2][:, cols].bitcast(FP8X4), slot_scales[g, blk // 2][:, cols]
 
         def three_passes(acc, e, blk, h, slots_stationary):
-            for i, g in enumerate(names):
+            for i, g in enumerate(("v", "q", "k") if e == E - 1 else names):
                 w, w_sc = weight_operand(g, e, h)
                 x, x_sc = slot_operand(g, blk)
                 if slots_stationary:
@@ -140,27 +127,25 @@ def tile_moe_qkb_kernel(
 
         def expert_turned(e, halves):
             n = len(halves)
-            sums = ps.tile([P, 2, n * P], F32, name="sums", tag="sums", bufs=3)
-            gated = sb.tile([P, 2, n * P], F32, name="gated", tag="gated", bufs=3, align_bytes=64)
             turned = ps.tile([P, n, C], F32, name="turned", tag="turned", bufs=2)
             for u in range(2):
+                blk = 2 * e + u
+                sums = ps.tile([P, n * P], F32, name="sums", bufs=4)
+                gated = sb.tile([P, n * P], F32, name="gated", bufs=4, align_bytes=64)
                 for i, h in enumerate(halves):
-                    three_passes(sums[:, u, i * P : (i + 1) * P], e, 2 * e + u, h, True)
-            for u in range(2):
-                nc.scalar.activation(out=gated[:, u, :], in_=sums[:, u, :], func=COPY,
-                                     scale=gate_cols[:, 2 * e + u : 2 * e + u + 1])
-            for i, h in enumerate(halves):
-                for u in range(2):
+                    three_passes(sums[:, i * P : (i + 1) * P], e, blk, h, True)
+                nc.scalar.activation(out=gated[:], in_=sums[:], func=COPY, scale=gate_cols[:, blk : blk + 1])
+                for i, h in enumerate(halves):
                     nc.tensor.transpose(out=turned[:, i, u * P : (u + 1) * P],
-                                        in_=gated[:, u, i * P : (i + 1) * P], identity=ident[:])
+                                        in_=gated[:, i * P : (i + 1) * P], identity=ident[:])
             for i, h in enumerate(halves):
                 nc.scalar.copy(out=dx[h][:, e * C : (e + 1) * C], in_=turned[:, i, :])
 
         def pick(h, r, a, b):
             nc.vector.tensor_copy(out=picked[h][r][:, a:b], in_=dx[h][:].indirect(pos_sb[r][:, a // 16 : b // 16]))
 
-        def add_and_store(h, a, b):
-            nc.vector.tensor_tensor(out=summed[h][:, a:b], in0=picked[h][0][:, a:b], in1=picked[h][1][:, a:b], op=ADD)
+        def add_and_store(engine, h, a, b):
+            engine.tensor_tensor(out=summed[h][:, a:b], in0=picked[h][0][:, a:b], in1=picked[h][1][:, a:b], op=ADD)
             nc.sync.dma_start(out=out[h * P : (h + 1) * P, a:b], in_=summed[h][:, a:b])
 
         for g in ("q", "k"):
@@ -171,72 +156,55 @@ def tile_moe_qkb_kernel(
             nc.vector.memset(w_scales[g][:].bitcast(I32), 0)
 
         nc.sync.dma_start(out=offs_sb[:], in_=offs)
+        load_tok_scales("q", (0, 1, 2, 3))
         load_tok_words("q")
-        load_tok_scales("q")
-        load_tok_words("k")
-        load_tok_scales("k")
         load_wk(0)
+        load_tok_scales("k", (0, 1))
         load_wk(1)
-        load_tok_scales("v")
-        load_w4_scales("q")
-        load_w4_scales("v")
+        load_tok_scales("k", (2, 3))
+        load_tok_words("k")
+        load_tok_scales("v", (0, 1))
         load_wk(2)
+        load_tok_scales("v", (2, 3))
         load_tok_words("v")
+        load_w4_scales("q", (0, 1))
+        load_wk(3)
+        load_w4_scales("q", (2, 3))
+        load_wk(4)
+        load_w4_scales("v", (0, 1))
+        load_wk(5)
+        load_w4_scales("v", (2, 3))
         load_w4_words("q")
         load_w4_words("v")
         nc.sync.dma_start(out=gate_rows[:], in_=gate.rearrange("p (a b) -> (p a) b", b=P)[0:P, :])
-        load_wk(3)
-        load_wk(4)
-        load_wk(5)
         nc.sync.dma_start(out=gate_last[:], in_=gate[:, S - C : S])
         nc.sync.dma_start(out=pos_sb[0][:], in_=pos1)
         nc.sync.dma_start(out=pos_sb[1][:], in_=pos2)
 
-        for e in range(3):
+        for e in range(E):
             round_wk(e)
-        gate_bank = ps.tile([P, P], F32, name="gate_bank")
-        nc.tensor.transpose(out=gate_bank[:], in_=gate_rows[:], identity=ident[:])
-        nc.scalar.copy(out=gate_cols[:], in_=gate_bank[:, 0:16])
-        for e in range(3, E):
-            round_wk(e)
+        gate_bank = ps.tile([P, 2, C], F32, name="gate_bank", tag="turned", bufs=2)
+        nc.tensor.transpose(out=gate_bank[:, 0, 0:P], in_=gate_rows[:], identity=ident[:])
+        nc.scalar.copy(out=gate_cols[:], in_=gate_bank[:, 0, 0:16])
 
-        for a in range(0, S, 512):
-            gather_words("q", a, a + 512)
+        for e in range(0, E, 2):
+            quantize_wk(e, e + 2)
+        for e in range(E - 1):
+            for g in names:
+                new_slot_tiles(g, e)
+                gather_scales(g, e, 0, C)
+                gather_words(g, e)
+            expert_turned(e, (0, 1))
 
-        def gather_rest(a, b):
-            gather_scales("q", a, b)
-            gather_words("k", a, b)
-            gather_scales("k", a, b)
-            gather_scales("v", a, b)
-            gather_words("v", a, b)
-
-        new_slot_tiles(0, 1)
-        new_slot_tiles(1, 3)
-        quantize_wk(0, 2)
-        gather_rest(0, C)
-        expert_turned(0, (0, 1))
-        gather_rest(C, 3 * C)
-        quantize_wk(2, 3)
-        expert_turned(1, (0, 1))
-        expert_turned(2, (0, 1))
-        new_slot_tiles(3, 4)
-        gather_rest(3 * C, 4 * C)
-        quantize_wk(3, 4)
-        expert_turned(3, (0, 1))
-        new_slot_tiles(4, 5)
-        quantize_wk(4, 6)
-        gather_rest(4 * C, 5 * C)
-        expert_turned(4, (0, 1))
-
-        new_slot_tiles(5, 6)
-        a, b = 5 * C, 6 * C
-        gather_scales("q", a, b)
-        gather_words("k", a, b)
-        gather_scales("k", a, b)
-        gather_words("v", a, b)
+        for g in ("v", "q", "k"):
+            new_slot_tiles(g, 5)
+            gather_words(g, 5)
+            if g != "k":
+                gather_scales(g, 5, 0, C)
+        a = 5 * C
         direct = [ps.tile([P, P], F32, name="direct%d" % u) for u in range(2)]
         for u in range(2):
-            gather_scales("v", a + u * P, a + (u + 1) * P)
+            gather_scales("k", 5, u * P, (u + 1) * P)
             three_passes(direct[u][:], 5, 10 + u, 0, False)
         expert_turned(5, (1,))
         for u in range(2):
@@ -245,11 +213,9 @@ def tile_moe_qkb_kernel(
 
         pick(0, 0, 0, T)
         pick(0, 1, 0, T)
+        add_and_store(nc.gpsimd, 0, 0, T)
         pick(1, 0, 0, T)
-        add_and_store(0, 0, T)
         pick(1, 1, 0, 384)
-        pick(1, 1, 384, 576)
-        add_and_store(1, 0, 384)
-        pick(1, 1, 576, T)
-        add_and_store(1, 384, 576)
-        add_and_store(1, 576, T)
+        add_and_store(nc.gpsimd, 1, 0, 384)
+        pick(1, 1, 384, T)
+        add_and_store(nc.vector, 1, 384, T)

@@ -1,12 +1,16 @@
 from contextlib import ExitStack
 
 import concourse.mybir as mybir
-from concourse.masks import make_identity
 
 K, T, E, C, N = 256, 768, 6, 256, 512
 S = E * C
 P = 128
+PER_COLUMN = 16
 FLOPS = 2 * 3 * S * N * K
+
+SUM_BANKS = 6
+STAGED_TILES = 4
+TOKEN_CUT = 480
 
 F32 = mybir.dt.float32
 BF16 = mybir.dt.bfloat16
@@ -16,7 +20,6 @@ U16 = mybir.dt.uint16
 U8 = mybir.dt.uint8
 FP8X4 = mybir.dt.float8_e4m3fn_x4
 FP4X4 = mybir.dt.float4_e2m1fn_x4
-COPY = mybir.ActivationFunctionType.Copy
 MULT = mybir.AluOpType.mult
 ADD = mybir.AluOpType.add
 
@@ -34,23 +37,20 @@ def tile_moe_qkb_kernel(
         def held(name, shape, dtype):
             return sb.tile(shape, dtype, name=name, align_bytes=64)
 
-        offs_sb = lists.tile([P, S // 16], U16, name="offs_sb")
-        pos_sb = [lists.tile([P, T // 16], U16, name="pos%d_sb" % r) for r in (1, 2)]
+        offs_sb = lists.tile([P, S // PER_COLUMN], U16, name="offs_sb")
+        pos_sb = [lists.tile([P, T // PER_COLUMN], U16, name="pos%d_sb" % r) for r in (1, 2)]
 
-        names = ("q", "k", "v")
-        tok_words = {g: held("tok_words_" + g, [P, T], I32) for g in names}
-        tok_scales = {g: held("tok_scales_" + g, [P, T], U8) for g in names}
+        projections = ("q", "k", "v")
+        tok_words = {g: held("tok_words_" + g, [P, T], I32) for g in projections}
+        tok_scales = {g: held("tok_scales_" + g, [P, T], U8) for g in projections}
         slot_words = {}
         slot_scales = {}
         w4_words = {g: held("w4_words_" + g, [P, E, 2 * K], U8) for g in ("q", "v")}
-        w_scales = {g: held("w_scales_" + g, [P, E, K], U8) for g in names}
+        w_scales = {g: held("w_scales_" + g, [P, E, K], U8) for g in projections}
         wk_words = held("wk_words", [P, E, K], U32)
         wk_raw = [held("wk_raw%d" % e, [P, 4, K], F32) for e in range(E)]
         wk_bf = held("wk_bf", [P, E, K, 4], BF16)
-        ident = held("ident", [P, P], F32)
-        gate_rows = held("gate_rows", [P, P], F32)
-        gate_cols = held("gate_cols", [P, 16], F32)
-        gate_last = held("gate_last", [P, C], F32)
+        gate_sb = held("gate_sb", [P, S], F32)
         dx = [held("dx%d" % h, [P, S], F32) for h in range(2)]
         picked = [[held("picked%d%d" % (h, r), [P, T], F32) for r in range(2)] for h in range(2)]
         summed = [held("summed%d" % h, [P, T], F32) for h in range(2)]
@@ -84,25 +84,34 @@ def tile_moe_qkb_kernel(
             nc.scalar.copy(out=wk_bf[:, e].rearrange("p (c i) j -> p c j i", i=4),
                            in_=wk_raw[e][:].rearrange("p j (c i) -> p c j i", i=4))
 
-        def quantize_wk(a, b):
+        def quantize_wk(first, last):
             nc.vector.quantize_mx(
-                out=wk_words[:, a:b, :].rearrange("p e c -> p (e c)").bitcast(FP8X4),
-                scales=w_scales["k"][:, a:b, :].rearrange("p e c -> p (e c)"),
-                in_=wk_bf[:, a:b].rearrange("p e c j -> p (e c j)"),
+                out=wk_words[:, first:last, :].rearrange("p e c -> p (e c)").bitcast(FP8X4),
+                scales=w_scales["k"][:, first:last, :].rearrange("p e c -> p (e c)"),
+                in_=wk_bf[:, first:last].rearrange("p e c j -> p (e c j)"),
             )
 
-        def new_slot_tiles(g, e):
-            depth = 4 if g == "v" else 3
-            slot_words[g, e] = sb.tile([P, C], U32, name="slot_words_" + g, bufs=depth, align_bytes=64)
-            slot_scales[g, e] = sb.tile([P, C], U8, name="slot_scales_" + g, bufs=depth, align_bytes=64)
+        def new_slot_tiles(g, first, last, place):
+            words = sb.tile([P, (last - first) * C], U32, name="slot_words_%s%s" % (g, place), align_bytes=64)
+            scales = sb.tile([P, (last - first) * C], U8, name="slot_scales_%s%s" % (g, place), align_bytes=64)
+            for e in range(first, last):
+                slot_words[g, e] = words[:, (e - first) * C : (e - first + 1) * C]
+                slot_scales[g, e] = scales[:, (e - first) * C : (e - first + 1) * C]
+            return words, scales
 
-        def gather_scales(g, e, a, b):
-            nc.vector.tensor_copy(out=slot_scales[g, e][:, a:b],
-                                  in_=tok_scales[g][:].indirect(offs_sb[:, (e * C + a) // 16 : (e * C + b) // 16]))
+        def entries(list_sb, a, b):
+            return list_sb[:, a // PER_COLUMN : b // PER_COLUMN]
 
-        def gather_words(g, e):
-            nc.vector.tensor_copy(out=slot_words[g, e][:],
-                                  in_=tok_words[g][:].bitcast(U32).indirect(offs_sb[:, e * C // 16 : (e + 1) * C // 16]))
+        def gather_scales(dst, g, a, b):
+            nc.vector.tensor_copy(out=dst, in_=tok_scales[g][:].indirect(entries(offs_sb, a, b)))
+
+        def gather_words(dst, g, a, b):
+            nc.vector.tensor_copy(out=dst, in_=tok_words[g][:].bitcast(U32).indirect(entries(offs_sb, a, b)))
+
+        def gather_experts(g, first, last, place):
+            words, scales = new_slot_tiles(g, first, last, place)
+            gather_scales(scales[:], g, first * C, last * C)
+            gather_words(words[:], g, first * C, last * C)
 
         def weight_operand(g, e, h):
             cols = slice(h * P, (h + 1) * P)
@@ -110,39 +119,25 @@ def tile_moe_qkb_kernel(
                 return wk_words[:, e, cols].bitcast(FP8X4), w_scales[g][:, e, cols]
             return w4_words[g][:, e, 2 * h * P : 2 * (h + 1) * P].bitcast(FP4X4), w_scales[g][:, e, cols]
 
-        def slot_operand(g, blk):
-            cols = slice(blk % 2 * P, (blk % 2 + 1) * P)
-            return slot_words[g, blk // 2][:, cols].bitcast(FP8X4), slot_scales[g, blk // 2][:, cols]
-
-        def three_passes(acc, e, blk, h, slots_stationary):
-            for i, g in enumerate(("v", "q", "k") if e == E - 1 else names):
+        def three_passes(acc, e, u, h, order):
+            cols = slice(u * P, (u + 1) * P)
+            for i, g in enumerate(order):
                 w, w_sc = weight_operand(g, e, h)
-                x, x_sc = slot_operand(g, blk)
-                if slots_stationary:
-                    nc.tensor.matmul_mx(out=acc, lhsT=x, lhsT_scale=x_sc, rhs=w, rhs_scale=w_sc,
-                                        start=(i == 0), stop=(i == 2))
-                else:
-                    nc.tensor.matmul_mx(out=acc, lhsT=w, lhsT_scale=w_sc, rhs=x, rhs_scale=x_sc,
-                                        start=(i == 0), stop=(i == 2))
+                nc.tensor.matmul_mx(out=acc, lhsT=w, lhsT_scale=w_sc,
+                                    rhs=slot_words[g, e][:, cols].bitcast(FP8X4), rhs_scale=slot_scales[g, e][:, cols],
+                                    start=(i == 0), stop=(i == len(order) - 1))
 
-        def expert_turned(e, halves):
-            n = len(halves)
-            turned = ps.tile([P, n, C], F32, name="turned", tag="turned", bufs=2)
+        def expert_half(e, h, order):
+            sums = ps.tile([P, C], F32, name="sums", bufs=SUM_BANKS)
+            staged = sb.tile([P, C], F32, name="staged", bufs=STAGED_TILES, align_bytes=64)
             for u in range(2):
-                blk = 2 * e + u
-                sums = ps.tile([P, n * P], F32, name="sums", bufs=4)
-                gated = sb.tile([P, n * P], F32, name="gated", bufs=4, align_bytes=64)
-                for i, h in enumerate(halves):
-                    three_passes(sums[:, i * P : (i + 1) * P], e, blk, h, True)
-                nc.scalar.activation(out=gated[:], in_=sums[:], func=COPY, scale=gate_cols[:, blk : blk + 1])
-                for i, h in enumerate(halves):
-                    nc.tensor.transpose(out=turned[:, i, u * P : (u + 1) * P],
-                                        in_=gated[:, i * P : (i + 1) * P], identity=ident[:])
-            for i, h in enumerate(halves):
-                nc.scalar.copy(out=dx[h][:, e * C : (e + 1) * C], in_=turned[:, i, :])
+                three_passes(sums[:, u * P : (u + 1) * P], e, u, h, order)
+            nc.scalar.copy(out=staged[:], in_=sums[:])
+            cols = slice(e * C, (e + 1) * C)
+            nc.gpsimd.tensor_tensor(out=dx[h][:, cols], in0=staged[:], in1=gate_sb[:, cols], op=MULT)
 
         def pick(h, r, a, b):
-            nc.vector.tensor_copy(out=picked[h][r][:, a:b], in_=dx[h][:].indirect(pos_sb[r][:, a // 16 : b // 16]))
+            nc.vector.tensor_copy(out=picked[h][r][:, a:b], in_=dx[h][:].indirect(entries(pos_sb[r], a, b)))
 
         def add_and_store(engine, h, a, b):
             engine.tensor_tensor(out=summed[h][:, a:b], in0=picked[h][0][:, a:b], in1=picked[h][1][:, a:b], op=ADD)
@@ -150,7 +145,6 @@ def tile_moe_qkb_kernel(
 
         for g in ("q", "k"):
             nc.gpsimd.memset(tok_scales[g][:].bitcast(I32), 0)
-        make_identity(nc, ident[:])
         nc.vector.memset(tok_scales["v"][:].bitcast(I32), 0)
         for g in ("q", "v"):
             nc.vector.memset(w_scales[g][:].bitcast(I32), 0)
@@ -176,46 +170,47 @@ def tile_moe_qkb_kernel(
         load_w4_scales("v", (2, 3))
         load_w4_words("q")
         load_w4_words("v")
-        nc.sync.dma_start(out=gate_rows[:], in_=gate.rearrange("p (a b) -> (p a) b", b=P)[0:P, :])
-        nc.sync.dma_start(out=gate_last[:], in_=gate[:, S - C : S])
+        nc.sync.dma_start(out=gate_sb[:, : S // 2], in_=gate[:, : S // 2])
+        nc.sync.dma_start(out=gate_sb[:, S // 2 :], in_=gate[:, S // 2 :])
         nc.sync.dma_start(out=pos_sb[0][:], in_=pos1)
         nc.sync.dma_start(out=pos_sb[1][:], in_=pos2)
 
         for e in range(E):
             round_wk(e)
-        gate_bank = ps.tile([P, 2, C], F32, name="gate_bank", tag="turned", bufs=2)
-        nc.tensor.transpose(out=gate_bank[:, 0, 0:P], in_=gate_rows[:], identity=ident[:])
-        nc.scalar.copy(out=gate_cols[:], in_=gate_bank[:, 0, 0:16])
-
         for e in range(0, E, 2):
             quantize_wk(e, e + 2)
-        for e in range(E - 1):
-            for g in names:
-                new_slot_tiles(g, e)
-                gather_scales(g, e, 0, C)
-                gather_words(g, e)
-            expert_turned(e, (0, 1))
 
-        for g in ("v", "q", "k"):
-            new_slot_tiles(g, 5)
-            gather_words(g, 5)
-            if g != "k":
-                gather_scales(g, 5, 0, C)
-        a = 5 * C
-        direct = [ps.tile([P, P], F32, name="direct%d" % u) for u in range(2)]
-        for u in range(2):
-            gather_scales("k", 5, u * P, (u + 1) * P)
-            three_passes(direct[u][:], 5, 10 + u, 0, False)
-        expert_turned(5, (1,))
-        for u in range(2):
-            nc.vector.tensor_tensor(out=dx[0][:, a + u * P : a + (u + 1) * P], in0=direct[u][:],
-                                    in1=gate_last[:, u * P : (u + 1) * P], op=MULT)
+        for first, last, place in ((0, 1, "a"), (1, 3, "b")):
+            for g in projections:
+                gather_experts(g, first, last, place)
+            for e in range(first, last):
+                for h in range(2):
+                    expert_half(e, h, projections)
 
-        pick(0, 0, 0, T)
-        pick(0, 1, 0, T)
-        add_and_store(nc.gpsimd, 0, 0, T)
-        pick(1, 0, 0, T)
-        pick(1, 1, 0, 384)
-        add_and_store(nc.gpsimd, 1, 0, 384)
-        pick(1, 1, 384, T)
-        add_and_store(nc.vector, 1, 384, T)
+        late_order = ("v", "q", "k")
+        gather_experts("v", 3, 5, "c")
+        gather_experts("q", 3, 5, "a")
+        gather_experts("k", 3, 5, "a")
+        for h in range(2):
+            for e in (3, 4):
+                expert_half(e, h, late_order)
+
+        last_expert = E - 1
+        first_slot = last_expert * C
+        gather_experts("v", last_expert, E, "b")
+        gather_experts("q", last_expert, E, "b")
+        last_words, last_scales = new_slot_tiles("k", last_expert, E, "b")
+        gather_words(last_words[:], "k", first_slot, S)
+        last_sums = [ps.tile([P, P], F32, name="last_sums%d" % u) for u in range(2)]
+        for u in range(2):
+            gather_scales(last_scales[:, u * P : (u + 1) * P], "k", first_slot + u * P, first_slot + (u + 1) * P)
+            three_passes(last_sums[u][:], last_expert, u, 0, late_order)
+        expert_half(last_expert, 1, late_order)
+        for u in range(2):
+            cols = slice(first_slot + u * P, first_slot + (u + 1) * P)
+            nc.vector.tensor_tensor(out=dx[0][:, cols], in0=last_sums[u][:], in1=gate_sb[:, cols], op=MULT)
+
+        for engine, h, a, b in ((nc.gpsimd, 0, 0, T), (nc.gpsimd, 1, 0, TOKEN_CUT), (nc.vector, 1, TOKEN_CUT, T)):
+            pick(h, 0, a, b)
+            pick(h, 1, a, b)
+            add_and_store(engine, h, a, b)

@@ -6,10 +6,9 @@ K, T, E, C, N = 256, 768, 6, 256, 512
 S = E * C
 P = 128
 PER_COLUMN = 16
+WIDE = 2048
+PAIR = 2 * C
 FLOPS = 2 * 3 * S * N * K
-
-SUM_BANKS = 6
-STAGED_TILES = 4
 TOKEN_CUT = 480
 
 F32 = mybir.dt.float32
@@ -40,38 +39,43 @@ def tile_moe_qkb_kernel(
         offs_sb = lists.tile([P, S // PER_COLUMN], U16, name="offs_sb")
         pos_sb = [lists.tile([P, T // PER_COLUMN], U16, name="pos%d_sb" % r) for r in (1, 2)]
 
-        projections = ("q", "k", "v")
-        tok_words = {g: held("tok_words_" + g, [P, T], I32) for g in projections}
-        tok_scales = {g: held("tok_scales_" + g, [P, T], U8) for g in projections}
-        slot_words = {}
+        projections = ("q", "v", "k")
+        tok_words = {g: held("tok_words_" + g, [P, WIDE], I32) for g in projections}
+        tok_scales = {g: held("tok_scales_" + g, [P, T if g == "k" else WIDE], U8) for g in projections}
+        slot_words = {g: held("slot_words_" + g, [P, S], U32) for g in projections}
         slot_scales = {}
         w4_words = {g: held("w4_words_" + g, [P, E, 2 * K], U8) for g in ("q", "v")}
-        w_scales = {g: held("w_scales_" + g, [P, E, K], U8) for g in projections}
-        wk_words = held("wk_words", [P, E, K], U32)
+        w4_scales = {g: held("w4_scales_" + g, [P, E, K], U8) for g in ("q", "v")}
+        calls = (((0, 0), (1, 0), (0, 1), (1, 1)), ((2, 0), (3, 0)), ((4, 0), (5, 0)), ((2, 1), (3, 1), (4, 1), (5, 1)))
+        wk_words = [held("wk_words%d" % a, [P, len(c), P], U32) for a, c in enumerate(calls)]
+        wk_scales = [held("wk_scales%d" % a, [P, len(c), P], U8) for a, c in enumerate(calls)]
+        wk_bf = [held("wk_bf%d" % a, [P, len(c), P, 4], BF16) for a, c in enumerate(calls)]
+        wk_place = {block: (a, i) for a, c in enumerate(calls) for i, block in enumerate(c)}
         wk_raw = [held("wk_raw%d" % e, [P, 4, K], F32) for e in range(E)]
-        wk_bf = held("wk_bf", [P, E, K, 4], BF16)
         gate_sb = held("gate_sb", [P, S], F32)
         dx = [held("dx%d" % h, [P, S], F32) for h in range(2)]
         picked = [[held("picked%d%d" % (h, r), [P, T], F32) for r in range(2)] for h in range(2)]
         summed = [held("summed%d" % h, [P, T], F32) for h in range(2)]
+        banks = {(a, h): ps.tile([P, PAIR], F32, name="bank%d%d" % (a, h)) for a in range(3) for h in range(2)}
 
         tok_words_hbm = {"q": dq_words, "k": dk_words, "v": dv_words}
         tok_scales_hbm = {"q": dq_scales, "k": dk_scales, "v": dv_scales}
         w4_words_hbm = {"q": wq_words, "v": wv_words}
         w4_scales_hbm = {"q": wq_scales, "v": wv_scales}
 
-        def load_tok_scales(g, rs):
+        def load_tok_scales(g):
             rows = tok_scales_hbm[g][0].rearrange("(q r) t -> r q t", r=4)
-            for r in rs:
-                nc.sync.dma_start(out=tok_scales[g][r:P:32, :].bitcast(I32), in_=rows[r].bitcast(I32))
+            for r in range(4):
+                nc.sync.dma_start(out=tok_scales[g][r:P:32, :T].bitcast(I32), in_=rows[r].bitcast(I32))
 
         def load_tok_words(g):
-            nc.sync.dma_start(out=tok_words[g][:], in_=tok_words_hbm[g][0].rearrange("p t d -> p (t d)").bitcast(I32))
+            nc.sync.dma_start(out=tok_words[g][:, :T],
+                              in_=tok_words_hbm[g][0].rearrange("p t d -> p (t d)").bitcast(I32))
 
-        def load_w4_scales(g, rs):
+        def load_w4_scales(g):
             rows = w4_scales_hbm[g].rearrange("e s (q r) c -> r q (e s) c", r=4)
-            for r in rs:
-                nc.sync.dma_start(out=w_scales[g][r:P:32, :, :].bitcast(I32), in_=rows[r].bitcast(I32))
+            for r in range(4):
+                nc.sync.dma_start(out=w4_scales[g][r:P:32, :, :].bitcast(I32), in_=rows[r].bitcast(I32))
 
         def load_w4_words(g):
             nc.sync.dma_start(out=w4_words[g][:].bitcast(I32),
@@ -81,60 +85,60 @@ def tile_moe_qkb_kernel(
             nc.sync.dma_start(out=wk_raw[e][:], in_=wk[e].rearrange("(p j) c -> p j c", j=4))
 
         def round_wk(e):
-            nc.scalar.copy(out=wk_bf[:, e].rearrange("p (c i) j -> p c j i", i=4),
-                           in_=wk_raw[e][:].rearrange("p j (c i) -> p c j i", i=4))
+            for h in range(2):
+                a, i = wk_place[e, h]
+                nc.scalar.copy(out=wk_bf[a][:, i].rearrange("p (c i) j -> p c j i", i=4),
+                               in_=wk_raw[e][:, :, h * P : (h + 1) * P].rearrange("p j (c i) -> p c j i", i=4))
 
-        def quantize_wk(first, last):
+        def quantize_wk(a):
             nc.vector.quantize_mx(
-                out=wk_words[:, first:last, :].rearrange("p e c -> p (e c)").bitcast(FP8X4),
-                scales=w_scales["k"][:, first:last, :].rearrange("p e c -> p (e c)"),
-                in_=wk_bf[:, first:last].rearrange("p e c j -> p (e c j)"),
+                out=wk_words[a][:].rearrange("p e c -> p (e c)").bitcast(FP8X4),
+                scales=wk_scales[a][:].rearrange("p e c -> p (e c)"),
+                in_=wk_bf[a][:].rearrange("p e c j -> p (e c j)"),
             )
-
-        def new_slot_tiles(g, first, last, place):
-            words = sb.tile([P, (last - first) * C], U32, name="slot_words_%s%s" % (g, place), align_bytes=64)
-            scales = sb.tile([P, (last - first) * C], U8, name="slot_scales_%s%s" % (g, place), align_bytes=64)
-            for e in range(first, last):
-                slot_words[g, e] = words[:, (e - first) * C : (e - first + 1) * C]
-                slot_scales[g, e] = scales[:, (e - first) * C : (e - first + 1) * C]
-            return words, scales
 
         def entries(list_sb, a, b):
             return list_sb[:, a // PER_COLUMN : b // PER_COLUMN]
 
-        def gather_scales(dst, g, a, b):
-            nc.vector.tensor_copy(out=dst, in_=tok_scales[g][:].indirect(entries(offs_sb, a, b)))
+        def gather_words(g):
+            nc.vector.tensor_copy(out=slot_words[g][:], in_=tok_words[g][:].bitcast(U32).indirect(offs_sb[:]))
 
-        def gather_words(dst, g, a, b):
-            nc.vector.tensor_copy(out=dst, in_=tok_words[g][:].bitcast(U32).indirect(entries(offs_sb, a, b)))
+        def gather_scales(g, first, last, name):
+            tile = held(name, [P, (last - first) * PAIR], U8)
+            nc.vector.tensor_copy(out=tile[:], in_=tok_scales[g][:].indirect(entries(offs_sb, first * PAIR, last * PAIR)))
+            for a in range(first, last):
+                slot_scales[g, a] = tile[:, (a - first) * PAIR : (a - first + 1) * PAIR]
 
-        def gather_experts(g, first, last, place):
-            words, scales = new_slot_tiles(g, first, last, place)
-            gather_scales(scales[:], g, first * C, last * C)
-            gather_words(words[:], g, first * C, last * C)
+        def packed_passes(g, a, h):
+            for i in range(PAIR // P):
+                e = 2 * a + i // 2
+                cols = slice(a * PAIR + i * P, a * PAIR + (i + 1) * P)
+                nc.tensor.matmul_mx(
+                    out=banks[a, h][:, i * P : (i + 1) * P],
+                    lhsT=w4_words[g][:, e, 2 * h * P : 2 * (h + 1) * P].bitcast(FP4X4),
+                    lhsT_scale=w4_scales[g][:, e, h * P : (h + 1) * P],
+                    rhs=slot_words[g][:, cols].bitcast(FP8X4), rhs_scale=slot_scales[g, a][:, i * P : (i + 1) * P],
+                    start=(g == "q" and i == 0), stop=False)
 
-        def weight_operand(g, e, h):
-            cols = slice(h * P, (h + 1) * P)
-            if g == "k":
-                return wk_words[:, e, cols].bitcast(FP8X4), w_scales[g][:, e, cols]
-            return w4_words[g][:, e, 2 * h * P : 2 * (h + 1) * P].bitcast(FP4X4), w_scales[g][:, e, cols]
+        def key_passes(a, h):
+            for i in range(2):
+                call, block = wk_place[2 * a + i, h]
+                cols = slice(a * PAIR + i * C, a * PAIR + (i + 1) * C)
+                nc.tensor.matmul_mx(
+                    out=banks[a, h][:, i * C : (i + 1) * C],
+                    lhsT=wk_words[call][:, block].bitcast(FP8X4), lhsT_scale=wk_scales[call][:, block],
+                    rhs=slot_words["k"][:, cols].bitcast(FP8X4), rhs_scale=slot_scales["k", a][:, i * C : (i + 1) * C],
+                    start=False, stop=(i == 1))
 
-        def three_passes(acc, e, u, h, order):
-            cols = slice(u * P, (u + 1) * P)
-            for i, g in enumerate(order):
-                w, w_sc = weight_operand(g, e, h)
-                nc.tensor.matmul_mx(out=acc, lhsT=w, lhsT_scale=w_sc,
-                                    rhs=slot_words[g, e][:, cols].bitcast(FP8X4), rhs_scale=slot_scales[g, e][:, cols],
-                                    start=(i == 0), stop=(i == len(order) - 1))
-
-        def expert_half(e, h, order):
-            sums = ps.tile([P, C], F32, name="sums", bufs=SUM_BANKS)
-            staged = sb.tile([P, C], F32, name="staged", bufs=STAGED_TILES, align_bytes=64)
-            for u in range(2):
-                three_passes(sums[:, u * P : (u + 1) * P], e, u, h, order)
-            nc.scalar.copy(out=staged[:], in_=sums[:])
-            cols = slice(e * C, (e + 1) * C)
+        def gate_by_gpsimd(a, h):
+            cols = slice(a * PAIR, (a + 1) * PAIR)
+            staged = held("staged%d%d" % (a, h), [P, PAIR], F32)
+            nc.scalar.copy(out=staged[:], in_=banks[a, h][:])
             nc.gpsimd.tensor_tensor(out=dx[h][:, cols], in0=staged[:], in1=gate_sb[:, cols], op=MULT)
+
+        def gate_by_vector(a, h):
+            cols = slice(a * PAIR, (a + 1) * PAIR)
+            nc.vector.tensor_tensor(out=dx[h][:, cols], in0=banks[a, h][:], in1=gate_sb[:, cols], op=MULT)
 
         def pick(h, r, a, b):
             nc.vector.tensor_copy(out=picked[h][r][:, a:b], in_=dx[h][:].indirect(entries(pos_sb[r], a, b)))
@@ -143,72 +147,68 @@ def tile_moe_qkb_kernel(
             engine.tensor_tensor(out=summed[h][:, a:b], in0=picked[h][0][:, a:b], in1=picked[h][1][:, a:b], op=ADD)
             nc.sync.dma_start(out=out[h * P : (h + 1) * P, a:b], in_=summed[h][:, a:b])
 
-        for g in ("q", "k"):
-            nc.gpsimd.memset(tok_scales[g][:].bitcast(I32), 0)
-        nc.vector.memset(tok_scales["v"][:].bitcast(I32), 0)
+        nc.gpsimd.memset(tok_scales["q"][:, :T].bitcast(I32), 0)
+        nc.vector.memset(tok_scales["q"][:, T:].bitcast(I32), 0)
+        nc.vector.memset(tok_words["q"][:, T:], 0)
+        for g in ("v", "k"):
+            nc.gpsimd.memset(tok_scales[g][:, :T].bitcast(I32), 0)
         for g in ("q", "v"):
-            nc.vector.memset(w_scales[g][:].bitcast(I32), 0)
+            nc.gpsimd.memset(w4_scales[g][:].bitcast(I32), 0)
+        nc.gpsimd.memset(tok_words["v"][:, T:], 0)
+        nc.gpsimd.memset(tok_scales["v"][:, T:].bitcast(I32), 0)
+        nc.gpsimd.memset(tok_words["k"][:, T:], 0)
 
         nc.sync.dma_start(out=offs_sb[:], in_=offs)
-        load_tok_scales("q", (0, 1, 2, 3))
+        load_tok_scales("q")
         load_tok_words("q")
-        load_wk(0)
-        load_tok_scales("k", (0, 1))
-        load_wk(1)
-        load_tok_scales("k", (2, 3))
-        load_tok_words("k")
-        load_tok_scales("v", (0, 1))
-        load_wk(2)
-        load_tok_scales("v", (2, 3))
         load_tok_words("v")
-        load_w4_scales("q", (0, 1))
-        load_wk(3)
-        load_w4_scales("q", (2, 3))
-        load_wk(4)
-        load_w4_scales("v", (0, 1))
-        load_wk(5)
-        load_w4_scales("v", (2, 3))
+        load_tok_scales("v")
         load_w4_words("q")
+        load_tok_scales("k")
         load_w4_words("v")
-        nc.sync.dma_start(out=gate_sb[:, : S // 2], in_=gate[:, : S // 2])
-        nc.sync.dma_start(out=gate_sb[:, S // 2 :], in_=gate[:, S // 2 :])
+        load_w4_scales("q")
+        load_w4_scales("v")
+        load_tok_words("k")
+        for e in range(E):
+            load_wk(e)
+        nc.sync.dma_start(out=gate_sb[:], in_=gate)
         nc.sync.dma_start(out=pos_sb[0][:], in_=pos1)
         nc.sync.dma_start(out=pos_sb[1][:], in_=pos2)
 
         for e in range(E):
             round_wk(e)
-        for e in range(0, E, 2):
-            quantize_wk(e, e + 2)
 
-        for first, last, place in ((0, 1, "a"), (1, 3, "b")):
-            for g in projections:
-                gather_experts(g, first, last, place)
-            for e in range(first, last):
-                for h in range(2):
-                    expert_half(e, h, projections)
-
-        late_order = ("v", "q", "k")
-        gather_experts("v", 3, 5, "c")
-        gather_experts("q", 3, 5, "a")
-        gather_experts("k", 3, 5, "a")
+        gather_scales("q", 0, 3, "slot_scales_q")
+        gather_words("q")
+        gather_words("v")
+        gather_scales("v", 0, 2, "slot_scales_v")
+        gather_words("k")
         for h in range(2):
-            for e in (3, 4):
-                expert_half(e, h, late_order)
+            for a in range(3):
+                packed_passes("q", a, h)
+        for h in range(2):
+            for a in range(2):
+                packed_passes("v", a, h)
 
-        last_expert = E - 1
-        first_slot = last_expert * C
-        gather_experts("v", last_expert, E, "b")
-        gather_experts("q", last_expert, E, "b")
-        last_words, last_scales = new_slot_tiles("k", last_expert, E, "b")
-        gather_words(last_words[:], "k", first_slot, S)
-        last_sums = [ps.tile([P, P], F32, name="last_sums%d" % u) for u in range(2)]
-        for u in range(2):
-            gather_scales(last_scales[:, u * P : (u + 1) * P], "k", first_slot + u * P, first_slot + (u + 1) * P)
-            three_passes(last_sums[u][:], last_expert, u, 0, late_order)
-        expert_half(last_expert, 1, late_order)
-        for u in range(2):
-            cols = slice(first_slot + u * P, first_slot + (u + 1) * P)
-            nc.vector.tensor_tensor(out=dx[0][:, cols], in0=last_sums[u][:], in1=gate_sb[:, cols], op=MULT)
+        quantize_wk(0)
+        gather_scales("k", 0, 1, "wk_raw1")
+        quantize_wk(1)
+        gather_scales("k", 1, 2, "wk_raw3")
+        gather_scales("v", 2, 3, "wk_raw4")
+        quantize_wk(2)
+        gather_scales("k", 2, 3, "wk_raw5")
+        quantize_wk(3)
+
+        for a, h in ((0, 0), (1, 0), (0, 1)):
+            key_passes(a, h)
+            gate_by_gpsimd(a, h)
+        for h in range(2):
+            packed_passes("v", 2, h)
+        key_passes(2, 0)
+        gate_by_vector(2, 0)
+        for a in (1, 2):
+            key_passes(a, 1)
+            gate_by_gpsimd(a, 1)
 
         for engine, h, a, b in ((nc.gpsimd, 0, 0, T), (nc.gpsimd, 1, 0, TOKEN_CUT), (nc.vector, 1, TOKEN_CUT, T)):
             pick(h, 0, a, b)

@@ -42,11 +42,11 @@ def tile_moe_qkb_kernel(
         projections = ("q", "v", "k")
         tok_words = {g: held("tok_words_" + g, [P, WIDE], I32) for g in projections}
         tok_scales = {g: held("tok_scales_" + g, [P, T if g == "k" else WIDE], U8) for g in projections}
-        slot_words = {g: held("slot_words_" + g, [P, S], U32) for g in projections}
+        slot_words = {}
         slot_scales = {}
         w4_words = {g: held("w4_words_" + g, [P, E, 2 * K], U8) for g in ("q", "v")}
         w4_scales = {g: held("w4_scales_" + g, [P, E, K], U8) for g in ("q", "v")}
-        calls = (((0, 0), (1, 0), (0, 1), (1, 1)), ((2, 0), (3, 0)), ((4, 0), (5, 0)), ((2, 1), (3, 1), (4, 1), (5, 1)))
+        calls = (((0, 0), (1, 0), (2, 0), (2, 1), (3, 0), (3, 1), (4, 0), (4, 1)), ((0, 1), (1, 1), (5, 0), (5, 1)))
         wk_words = [held("wk_words%d" % a, [P, len(c), P], U32) for a, c in enumerate(calls)]
         wk_scales = [held("wk_scales%d" % a, [P, len(c), P], U8) for a, c in enumerate(calls)]
         wk_bf = [held("wk_bf%d" % a, [P, len(c), P, 4], BF16) for a, c in enumerate(calls)]
@@ -100,8 +100,12 @@ def tile_moe_qkb_kernel(
         def entries(list_sb, a, b):
             return list_sb[:, a // PER_COLUMN : b // PER_COLUMN]
 
-        def gather_words(g):
-            nc.vector.tensor_copy(out=slot_words[g][:], in_=tok_words[g][:].bitcast(U32).indirect(offs_sb[:]))
+        def gather_words(g, first, last, name):
+            tile = held(name, [P, (last - first) * PAIR], U32)
+            nc.vector.tensor_copy(
+                out=tile[:], in_=tok_words[g][:].bitcast(U32).indirect(entries(offs_sb, first * PAIR, last * PAIR)))
+            for a in range(first, last):
+                slot_words[g, a] = tile[:, (a - first) * PAIR : (a - first + 1) * PAIR]
 
         def gather_scales(g, first, last, name):
             tile = held(name, [P, (last - first) * PAIR], U8)
@@ -112,22 +116,20 @@ def tile_moe_qkb_kernel(
         def packed_passes(g, a, h):
             for i in range(PAIR // P):
                 e = 2 * a + i // 2
-                cols = slice(a * PAIR + i * P, a * PAIR + (i + 1) * P)
                 nc.tensor.matmul_mx(
                     out=banks[a, h][:, i * P : (i + 1) * P],
                     lhsT=w4_words[g][:, e, 2 * h * P : 2 * (h + 1) * P].bitcast(FP4X4),
                     lhsT_scale=w4_scales[g][:, e, h * P : (h + 1) * P],
-                    rhs=slot_words[g][:, cols].bitcast(FP8X4), rhs_scale=slot_scales[g, a][:, i * P : (i + 1) * P],
+                    rhs=slot_words[g, a][:, i * P : (i + 1) * P].bitcast(FP8X4), rhs_scale=slot_scales[g, a][:, i * P : (i + 1) * P],
                     start=(g == "q" and i == 0), stop=False)
 
         def key_passes(a, h):
             for i in range(2):
                 call, block = wk_place[2 * a + i, h]
-                cols = slice(a * PAIR + i * C, a * PAIR + (i + 1) * C)
                 nc.tensor.matmul_mx(
                     out=banks[a, h][:, i * C : (i + 1) * C],
                     lhsT=wk_words[call][:, block].bitcast(FP8X4), lhsT_scale=wk_scales[call][:, block],
-                    rhs=slot_words["k"][:, cols].bitcast(FP8X4), rhs_scale=slot_scales["k", a][:, i * C : (i + 1) * C],
+                    rhs=slot_words["k", a][:, i * C : (i + 1) * C].bitcast(FP8X4), rhs_scale=slot_scales["k", a][:, i * C : (i + 1) * C],
                     start=False, stop=(i == 1))
 
         def gate_by_gpsimd(a, h):
@@ -149,11 +151,11 @@ def tile_moe_qkb_kernel(
 
         nc.gpsimd.memset(tok_scales["q"][:, :T].bitcast(I32), 0)
         nc.vector.memset(tok_scales["q"][:, T:].bitcast(I32), 0)
-        nc.vector.memset(tok_words["q"][:, T:], 0)
         for g in ("v", "k"):
             nc.gpsimd.memset(tok_scales[g][:, :T].bitcast(I32), 0)
         for g in ("q", "v"):
             nc.gpsimd.memset(w4_scales[g][:].bitcast(I32), 0)
+        nc.gpsimd.memset(tok_words["q"][:, T:], 0)
         nc.gpsimd.memset(tok_words["v"][:, T:], 0)
         nc.gpsimd.memset(tok_scales["v"][:, T:].bitcast(I32), 0)
         nc.gpsimd.memset(tok_words["k"][:, T:], 0)
@@ -163,14 +165,18 @@ def tile_moe_qkb_kernel(
         load_tok_words("q")
         load_tok_words("v")
         load_tok_scales("v")
+        load_wk(0)
         load_w4_words("q")
-        load_tok_scales("k")
-        load_w4_words("v")
         load_w4_scales("q")
+        load_wk(1)
+        load_tok_scales("k")
+        load_wk(2)
+        load_w4_words("v")
         load_w4_scales("v")
+        load_wk(3)
         load_tok_words("k")
-        for e in range(E):
-            load_wk(e)
+        load_wk(4)
+        load_wk(5)
         nc.sync.dma_start(out=gate_sb[:], in_=gate)
         nc.sync.dma_start(out=pos_sb[0][:], in_=pos1)
         nc.sync.dma_start(out=pos_sb[1][:], in_=pos2)
@@ -178,32 +184,27 @@ def tile_moe_qkb_kernel(
         for e in range(E):
             round_wk(e)
 
-        gather_scales("q", 0, 3, "slot_scales_q")
-        gather_words("q")
-        gather_words("v")
-        gather_scales("v", 0, 2, "slot_scales_v")
-        gather_words("k")
-        for h in range(2):
-            for a in range(3):
-                packed_passes("q", a, h)
-        for h in range(2):
-            for a in range(2):
-                packed_passes("v", a, h)
+        for g in ("q", "v"):
+            gather_scales(g, 0, 3, "slot_scales_" + g)
+            gather_words(g, 0, 3, "slot_words_" + g)
+        gather_words("k", 0, 2, "slot_words_k")
+        for g in ("q", "v"):
+            for h in range(2):
+                for a in range(3):
+                    packed_passes(g, a, h)
 
         quantize_wk(0)
-        gather_scales("k", 0, 1, "wk_raw1")
+        gather_scales("k", 0, 1, "wk_raw4")
         quantize_wk(1)
-        gather_scales("k", 1, 2, "wk_raw3")
-        gather_scales("v", 2, 3, "wk_raw4")
-        quantize_wk(2)
-        gather_scales("k", 2, 3, "wk_raw5")
-        quantize_wk(3)
+        gather_scales("k", 1, 2, "wk_raw5")
+        gather_scales("k", 2, 3, "wk_bf1")
 
-        for a, h in ((0, 0), (1, 0), (0, 1)):
-            key_passes(a, h)
-            gate_by_gpsimd(a, h)
-        for h in range(2):
-            packed_passes("v", 2, h)
+        for a in (0, 1):
+            key_passes(a, 0)
+            gate_by_gpsimd(a, 0)
+        key_passes(0, 1)
+        gather_words("k", 2, 3, "wk_raw4")
+        gate_by_vector(0, 1)
         key_passes(2, 0)
         gate_by_vector(2, 0)
         for a in (1, 2):

@@ -6,10 +6,11 @@ K, T, E, C, N = 256, 768, 6, 256, 512
 S = E * C
 P = 128
 PER_COLUMN = 16
-WIDE = 2048
+WIDE = 1024
+WIDE_K = 1376
 PAIR = 2 * C
 FLOPS = 2 * 3 * S * N * K
-TOKEN_CUT = 480
+TOKEN_CUT = 576
 
 F32 = mybir.dt.float32
 BF16 = mybir.dt.bfloat16
@@ -40,7 +41,7 @@ def tile_moe_qkb_kernel(
         pos_sb = [lists.tile([P, T // PER_COLUMN], U16, name="pos%d_sb" % r) for r in (1, 2)]
 
         projections = ("q", "v", "k")
-        tok_words = {g: held("tok_words_" + g, [P, WIDE], I32) for g in projections}
+        tok_words = {g: held("tok_words_" + g, [P, WIDE_K if g == "k" else WIDE], I32) for g in projections}
         tok_scales = {g: held("tok_scales_" + g, [P, T if g == "k" else WIDE], U8) for g in projections}
         slot_words = {}
         slot_scales = {}
@@ -100,16 +101,24 @@ def tile_moe_qkb_kernel(
         def entries(list_sb, a, b):
             return list_sb[:, a // PER_COLUMN : b // PER_COLUMN]
 
+        def pieces(first, last):
+            if last - first == 3:
+                return ((0, S // 2), (S // 2, S))
+            return ((first * PAIR, last * PAIR),)
+
         def gather_words(g, first, last, name):
             tile = held(name, [P, (last - first) * PAIR], U32)
-            nc.vector.tensor_copy(
-                out=tile[:], in_=tok_words[g][:].bitcast(U32).indirect(entries(offs_sb, first * PAIR, last * PAIR)))
+            for a, b in pieces(first, last):
+                nc.vector.tensor_copy(out=tile[:, a - first * PAIR : b - first * PAIR],
+                                      in_=tok_words[g][:].bitcast(U32).indirect(entries(offs_sb, a, b)))
             for a in range(first, last):
                 slot_words[g, a] = tile[:, (a - first) * PAIR : (a - first + 1) * PAIR]
 
         def gather_scales(g, first, last, name):
             tile = held(name, [P, (last - first) * PAIR], U8)
-            nc.vector.tensor_copy(out=tile[:], in_=tok_scales[g][:].indirect(entries(offs_sb, first * PAIR, last * PAIR)))
+            for a, b in pieces(first, last):
+                nc.vector.tensor_copy(out=tile[:, a - first * PAIR : b - first * PAIR],
+                                      in_=tok_scales[g][:].indirect(entries(offs_sb, a, b)))
             for a in range(first, last):
                 slot_scales[g, a] = tile[:, (a - first) * PAIR : (a - first + 1) * PAIR]
 
@@ -149,16 +158,13 @@ def tile_moe_qkb_kernel(
             engine.tensor_tensor(out=summed[h][:, a:b], in0=picked[h][0][:, a:b], in1=picked[h][1][:, a:b], op=ADD)
             nc.sync.dma_start(out=out[h * P : (h + 1) * P, a:b], in_=summed[h][:, a:b])
 
-        nc.gpsimd.memset(tok_scales["q"][:, :T].bitcast(I32), 0)
-        nc.vector.memset(tok_scales["q"][:, T:].bitcast(I32), 0)
+        nc.gpsimd.memset(tok_scales["q"][:].bitcast(I32), 0)
         for g in ("v", "k"):
-            nc.gpsimd.memset(tok_scales[g][:, :T].bitcast(I32), 0)
+            nc.vector.memset(tok_scales[g][:].bitcast(I32), 0)
         for g in ("q", "v"):
-            nc.gpsimd.memset(w4_scales[g][:].bitcast(I32), 0)
-        nc.gpsimd.memset(tok_words["q"][:, T:], 0)
-        nc.gpsimd.memset(tok_words["v"][:, T:], 0)
-        nc.gpsimd.memset(tok_scales["v"][:, T:].bitcast(I32), 0)
-        nc.gpsimd.memset(tok_words["k"][:, T:], 0)
+            nc.vector.memset(w4_scales[g][:].bitcast(I32), 0)
+        for g in projections:
+            nc.vector.memset(tok_words[g][:, T:], 0)
 
         nc.sync.dma_start(out=offs_sb[:], in_=offs)
         load_tok_scales("q")
@@ -211,7 +217,11 @@ def tile_moe_qkb_kernel(
             key_passes(a, 1)
             gate_by_gpsimd(a, 1)
 
-        for engine, h, a, b in ((nc.gpsimd, 0, 0, T), (nc.gpsimd, 1, 0, TOKEN_CUT), (nc.vector, 1, TOKEN_CUT, T)):
-            pick(h, 0, a, b)
-            pick(h, 1, a, b)
-            add_and_store(engine, h, a, b)
+        pick(0, 0, 0, T)
+        pick(0, 1, 0, T)
+        add_and_store(nc.gpsimd, 0, 0, T)
+        pick(1, 0, 0, T)
+        for a, b in ((0, TOKEN_CUT), (TOKEN_CUT, T)):
+            nc.vector.tensor_tensor(out=summed[1][:, a:b], in0=dx[1][:].indirect(entries(pos_sb[1], a, b)),
+                                    in1=picked[1][0][:, a:b], op=ADD)
+            nc.sync.dma_start(out=out[P:, a:b], in_=summed[1][:, a:b])

@@ -7,7 +7,7 @@ S = E * C
 P = 128
 PER_COLUMN = 16
 WIDE = 1024
-WIDE_K = 1376
+WIDE_SCALES = 2048
 PAIR = 2 * C
 FLOPS = 2 * 3 * S * N * K
 TOKEN_CUT = 576
@@ -41,13 +41,13 @@ def tile_moe_qkb_kernel(
         pos_sb = [lists.tile([P, T // PER_COLUMN], U16, name="pos%d_sb" % r) for r in (1, 2)]
 
         projections = ("q", "v", "k")
-        tok_words = {g: held("tok_words_" + g, [P, WIDE_K if g == "k" else WIDE], I32) for g in projections}
-        tok_scales = {g: held("tok_scales_" + g, [P, T if g == "k" else WIDE], U8) for g in projections}
+        tok_words = {g: held("tok_words_" + g, [P, T if g == "k" else WIDE], I32) for g in projections}
+        tok_scales = {g: held("tok_scales_" + g, [P, T if g == "k" else WIDE_SCALES], U8) for g in projections}
         slot_words = {}
         slot_scales = {}
         w4_words = {g: held("w4_words_" + g, [P, E, 2 * K], U8) for g in ("q", "v")}
         w4_scales = {g: held("w4_scales_" + g, [P, E, K], U8) for g in ("q", "v")}
-        calls = (((0, 0), (1, 0), (2, 0), (2, 1), (3, 0), (3, 1), (4, 0), (4, 1)), ((0, 1), (1, 1), (5, 0), (5, 1)))
+        calls = (((0, 0), (1, 0), (0, 1), (1, 1), (2, 0), (3, 0), (4, 0), (4, 1)), ((2, 1), (3, 1), (5, 0), (5, 1)))
         wk_words = [held("wk_words%d" % a, [P, len(c), P], U32) for a, c in enumerate(calls)]
         wk_scales = [held("wk_scales%d" % a, [P, len(c), P], U8) for a, c in enumerate(calls)]
         wk_bf = [held("wk_bf%d" % a, [P, len(c), P, 4], BF16) for a, c in enumerate(calls)]
@@ -57,7 +57,9 @@ def tile_moe_qkb_kernel(
         dx = [held("dx%d" % h, [P, S], F32) for h in range(2)]
         picked = [[held("picked%d%d" % (h, r), [P, T], F32) for r in range(2)] for h in range(2)]
         summed = [held("summed%d" % h, [P, T], F32) for h in range(2)]
-        banks = {(a, h): ps.tile([P, PAIR], F32, name="bank%d%d" % (a, h)) for a in range(3) for h in range(2)}
+        spans = [(h, a, a + PAIR) for h in range(2) for a in range(0, S, PAIR)]
+        spans[2:3] = [(0, 2 * PAIR, S - P), (0, S - P, S)]
+        banks = {span: ps.tile([P, span[2] - span[1]], F32, name="bank%d" % i) for i, span in enumerate(spans)}
 
         tok_words_hbm = {"q": dq_words, "k": dk_words, "v": dv_words}
         tok_scales_hbm = {"q": dq_scales, "k": dk_scales, "v": dv_scales}
@@ -67,7 +69,8 @@ def tile_moe_qkb_kernel(
         def load_tok_scales(g):
             rows = tok_scales_hbm[g][0].rearrange("(q r) t -> r q t", r=4)
             for r in range(4):
-                nc.sync.dma_start(out=tok_scales[g][r:P:32, :T].bitcast(I32), in_=rows[r].bitcast(I32))
+                queue = nc.scalar if g == "q" and r >= 2 else nc.sync
+                queue.dma_start(out=tok_scales[g][r:P:32, :T].bitcast(I32), in_=rows[r].bitcast(I32))
 
         def load_tok_words(g):
             nc.sync.dma_start(out=tok_words[g][:, :T],
@@ -116,40 +119,46 @@ def tile_moe_qkb_kernel(
 
         def gather_scales(g, first, last, name):
             tile = held(name, [P, (last - first) * PAIR], U8)
-            for a, b in pieces(first, last):
-                nc.vector.tensor_copy(out=tile[:, a - first * PAIR : b - first * PAIR],
-                                      in_=tok_scales[g][:].indirect(entries(offs_sb, a, b)))
+            nc.vector.tensor_copy(out=tile[:], in_=tok_scales[g][:].indirect(entries(offs_sb, first * PAIR, last * PAIR)))
             for a in range(first, last):
                 slot_scales[g, a] = tile[:, (a - first) * PAIR : (a - first + 1) * PAIR]
 
-        def packed_passes(g, a, h):
-            for i in range(PAIR // P):
-                e = 2 * a + i // 2
+        def slot_operand(g, a, b):
+            pair = a // PAIR
+            cols = slice(a - pair * PAIR, b - pair * PAIR)
+            return slot_words[g, pair][:, cols].bitcast(FP8X4), slot_scales[g, pair][:, cols]
+
+        def packed_passes(g, span):
+            h, first, last = span
+            for a in range(first, last, P):
+                e = a // C
+                words, scales = slot_operand(g, a, a + P)
                 nc.tensor.matmul_mx(
-                    out=banks[a, h][:, i * P : (i + 1) * P],
+                    out=banks[span][:, a - first : a - first + P],
                     lhsT=w4_words[g][:, e, 2 * h * P : 2 * (h + 1) * P].bitcast(FP4X4),
                     lhsT_scale=w4_scales[g][:, e, h * P : (h + 1) * P],
-                    rhs=slot_words[g, a][:, i * P : (i + 1) * P].bitcast(FP8X4), rhs_scale=slot_scales[g, a][:, i * P : (i + 1) * P],
-                    start=(g == "q" and i == 0), stop=False)
+                    rhs=words, rhs_scale=scales, start=(g == "q" and a == first), stop=False)
 
-        def key_passes(a, h):
-            for i in range(2):
-                call, block = wk_place[2 * a + i, h]
+        def key_passes(span):
+            h, first, last = span
+            for a in range(first, last, C):
+                b = min(a + C, last)
+                call, block = wk_place[a // C, h]
+                words, scales = slot_operand("k", a, b)
                 nc.tensor.matmul_mx(
-                    out=banks[a, h][:, i * C : (i + 1) * C],
+                    out=banks[span][:, a - first : b - first],
                     lhsT=wk_words[call][:, block].bitcast(FP8X4), lhsT_scale=wk_scales[call][:, block],
-                    rhs=slot_words["k", a][:, i * C : (i + 1) * C].bitcast(FP8X4), rhs_scale=slot_scales["k", a][:, i * C : (i + 1) * C],
-                    start=False, stop=(i == 1))
+                    rhs=words, rhs_scale=scales, start=False, stop=(b == last))
 
-        def gate_by_gpsimd(a, h):
-            cols = slice(a * PAIR, (a + 1) * PAIR)
-            staged = held("staged%d%d" % (a, h), [P, PAIR], F32)
-            nc.scalar.copy(out=staged[:], in_=banks[a, h][:])
-            nc.gpsimd.tensor_tensor(out=dx[h][:, cols], in0=staged[:], in1=gate_sb[:, cols], op=MULT)
+        def gate_by_gpsimd(span):
+            h, a, b = span
+            staged = held("staged%d_%d" % (h, a), [P, b - a], F32)
+            nc.scalar.copy(out=staged[:], in_=banks[span][:])
+            nc.gpsimd.tensor_tensor(out=dx[h][:, a:b], in0=staged[:], in1=gate_sb[:, a:b], op=MULT)
 
-        def gate_by_vector(a, h):
-            cols = slice(a * PAIR, (a + 1) * PAIR)
-            nc.vector.tensor_tensor(out=dx[h][:, cols], in0=banks[a, h][:], in1=gate_sb[:, cols], op=MULT)
+        def gate_by_vector(span):
+            h, a, b = span
+            nc.vector.tensor_tensor(out=dx[h][:, a:b], in0=banks[span][:], in1=gate_sb[:, a:b], op=MULT)
 
         def pick(h, r, a, b):
             nc.vector.tensor_copy(out=picked[h][r][:, a:b], in_=dx[h][:].indirect(entries(pos_sb[r], a, b)))
@@ -158,12 +167,13 @@ def tile_moe_qkb_kernel(
             engine.tensor_tensor(out=summed[h][:, a:b], in0=picked[h][0][:, a:b], in1=picked[h][1][:, a:b], op=ADD)
             nc.sync.dma_start(out=out[h * P : (h + 1) * P, a:b], in_=summed[h][:, a:b])
 
-        nc.gpsimd.memset(tok_scales["q"][:].bitcast(I32), 0)
+        nc.gpsimd.memset(tok_scales["q"][:, :T].bitcast(I32), 0)
+        nc.gpsimd.memset(tok_scales["q"][:, T:].bitcast(I32), 0)
         for g in ("v", "k"):
             nc.vector.memset(tok_scales[g][:].bitcast(I32), 0)
         for g in ("q", "v"):
             nc.vector.memset(w4_scales[g][:].bitcast(I32), 0)
-        for g in projections:
+        for g in ("q", "v"):
             nc.vector.memset(tok_words[g][:, T:], 0)
 
         nc.sync.dma_start(out=offs_sb[:], in_=offs)
@@ -193,34 +203,39 @@ def tile_moe_qkb_kernel(
         for g in ("q", "v"):
             gather_scales(g, 0, 3, "slot_scales_" + g)
             gather_words(g, 0, 3, "slot_words_" + g)
-        gather_words("k", 0, 2, "slot_words_k")
+        gather_words("k", 0, 1, "slot_words_k")
         for g in ("q", "v"):
-            for h in range(2):
-                for a in range(3):
-                    packed_passes(g, a, h)
+            for span in spans:
+                packed_passes(g, span)
 
         quantize_wk(0)
         gather_scales("k", 0, 1, "wk_raw4")
         quantize_wk(1)
-        gather_scales("k", 1, 2, "wk_raw5")
-        gather_scales("k", 2, 3, "wk_bf1")
+        gather_words("k", 1, 2, "wk_raw5")
+        gather_scales("k", 1, 2, "wk_bf1")
 
-        for a in (0, 1):
-            key_passes(a, 0)
-            gate_by_gpsimd(a, 0)
-        key_passes(0, 1)
-        gather_words("k", 2, 3, "wk_raw4")
-        gate_by_vector(0, 1)
-        key_passes(2, 0)
-        gate_by_vector(2, 0)
-        for a in (1, 2):
-            key_passes(a, 1)
-            gate_by_gpsimd(a, 1)
+        for span in (spans[0], spans[4], spans[1]):
+            key_passes(span)
+            gate_by_gpsimd(span)
+        gather_scales("k", 2, 3, "wk_raw4")
+        last_words = held("slot_words_k", [P, PAIR], U32)
+        slot_words["k", 2] = last_words
+        for span in spans[2:4]:
+            h, a, b = span
+            nc.vector.tensor_copy(out=last_words[:, a - 2 * PAIR : b - 2 * PAIR],
+                                  in_=tok_words["k"][:, :T].bitcast(U32).indirect(entries(offs_sb, a, b)))
+        for span in spans[2:4]:
+            key_passes(span)
+            gate_by_vector(span)
+        for span in spans[5:]:
+            key_passes(span)
+            gate_by_gpsimd(span)
 
         pick(0, 0, 0, T)
         pick(0, 1, 0, T)
         add_and_store(nc.gpsimd, 0, 0, T)
-        pick(1, 0, 0, T)
+        pick(1, 0, 0, TOKEN_CUT)
+        pick(1, 0, TOKEN_CUT, T)
         for a, b in ((0, TOKEN_CUT), (TOKEN_CUT, T)):
             nc.vector.tensor_tensor(out=summed[1][:, a:b], in0=dx[1][:].indirect(entries(pos_sb[1], a, b)),
                                     in1=picked[1][0][:, a:b], op=ADD)

@@ -7,7 +7,7 @@ S = E * C
 P = 128
 PER_COLUMN = 16
 WIDE = 1024
-WIDE_SCALES = 2048
+WIDE_V = 1376
 PAIR = 2 * C
 FLOPS = 2 * 3 * S * N * K
 TOKEN_CUT = 576
@@ -42,7 +42,7 @@ def tile_moe_qkb_kernel(
 
         projections = ("q", "v", "k")
         tok_words = {g: held("tok_words_" + g, [P, T if g == "k" else WIDE], I32) for g in projections}
-        tok_scales = {g: held("tok_scales_" + g, [P, T if g == "k" else WIDE_SCALES], U8) for g in projections}
+        tok_scales = {g: held("tok_scales_" + g, [P, {"q": WIDE, "v": WIDE_V, "k": T}[g]], U8) for g in projections}
         slot_words = {}
         slot_scales = {}
         w4_words = {g: held("w4_words_" + g, [P, E, 2 * K], U8) for g in ("q", "v")}
@@ -55,10 +55,9 @@ def tile_moe_qkb_kernel(
         wk_raw = [held("wk_raw%d" % e, [P, 4, K], F32) for e in range(E)]
         gate_sb = held("gate_sb", [P, S], F32)
         dx = [held("dx%d" % h, [P, S], F32) for h in range(2)]
-        picked = [[held("picked%d%d" % (h, r), [P, T], F32) for r in range(2)] for h in range(2)]
-        summed = [held("summed%d" % h, [P, T], F32) for h in range(2)]
-        spans = [(h, a, a + PAIR) for h in range(2) for a in range(0, S, PAIR)]
-        spans[2:3] = [(0, 2 * PAIR, S - P), (0, S - P, S)]
+        picked = [held("picked%d" % h, [P, T], F32) for h in range(2)]
+        cuts = (0, PAIR, 2 * PAIR, S - P, S)
+        spans = [(h, cuts[i], cuts[i + 1]) for h in range(2) for i in range(4)]
         banks = {span: ps.tile([P, span[2] - span[1]], F32, name="bank%d" % i) for i, span in enumerate(spans)}
 
         tok_words_hbm = {"q": dq_words, "k": dk_words, "v": dv_words}
@@ -69,8 +68,7 @@ def tile_moe_qkb_kernel(
         def load_tok_scales(g):
             rows = tok_scales_hbm[g][0].rearrange("(q r) t -> r q t", r=4)
             for r in range(4):
-                queue = nc.scalar if g == "q" and r >= 2 else nc.sync
-                queue.dma_start(out=tok_scales[g][r:P:32, :T].bitcast(I32), in_=rows[r].bitcast(I32))
+                nc.sync.dma_start(out=tok_scales[g][r:P:32, :T].bitcast(I32), in_=rows[r].bitcast(I32))
 
         def load_tok_words(g):
             nc.sync.dma_start(out=tok_words[g][:, :T],
@@ -119,7 +117,9 @@ def tile_moe_qkb_kernel(
 
         def gather_scales(g, first, last, name):
             tile = held(name, [P, (last - first) * PAIR], U8)
-            nc.vector.tensor_copy(out=tile[:], in_=tok_scales[g][:].indirect(entries(offs_sb, first * PAIR, last * PAIR)))
+            for a, b in pieces(first, last):
+                nc.vector.tensor_copy(out=tile[:, a - first * PAIR : b - first * PAIR],
+                                      in_=tok_scales[g][:].indirect(entries(offs_sb, a, b)))
             for a in range(first, last):
                 slot_scales[g, a] = tile[:, (a - first) * PAIR : (a - first + 1) * PAIR]
 
@@ -160,15 +160,7 @@ def tile_moe_qkb_kernel(
             h, a, b = span
             nc.vector.tensor_tensor(out=dx[h][:, a:b], in0=banks[span][:], in1=gate_sb[:, a:b], op=MULT)
 
-        def pick(h, r, a, b):
-            nc.vector.tensor_copy(out=picked[h][r][:, a:b], in_=dx[h][:].indirect(entries(pos_sb[r], a, b)))
-
-        def add_and_store(engine, h, a, b):
-            engine.tensor_tensor(out=summed[h][:, a:b], in0=picked[h][0][:, a:b], in1=picked[h][1][:, a:b], op=ADD)
-            nc.sync.dma_start(out=out[h * P : (h + 1) * P, a:b], in_=summed[h][:, a:b])
-
-        nc.gpsimd.memset(tok_scales["q"][:, :T].bitcast(I32), 0)
-        nc.gpsimd.memset(tok_scales["q"][:, T:].bitcast(I32), 0)
+        nc.gpsimd.memset(tok_scales["q"][:].bitcast(I32), 0)
         for g in ("v", "k"):
             nc.vector.memset(tok_scales[g][:].bitcast(I32), 0)
         for g in ("q", "v"):
@@ -201,22 +193,26 @@ def tile_moe_qkb_kernel(
             round_wk(e)
 
         for g in ("q", "v"):
-            gather_scales(g, 0, 3, "slot_scales_" + g)
+            gather_scales(g, 0, 3 if g == "q" else 2, "slot_scales_" + g)
             gather_words(g, 0, 3, "slot_words_" + g)
         gather_words("k", 0, 1, "slot_words_k")
         for g in ("q", "v"):
             for span in spans:
-                packed_passes(g, span)
+                if g == "q" or span[1] < 2 * PAIR:
+                    packed_passes(g, span)
 
         quantize_wk(0)
         gather_scales("k", 0, 1, "wk_raw4")
         quantize_wk(1)
         gather_words("k", 1, 2, "wk_raw5")
         gather_scales("k", 1, 2, "wk_bf1")
+        gather_scales("v", 2, 3, "wk_bf0")
 
-        for span in (spans[0], spans[4], spans[1]):
+        for span in (spans[0], spans[4], spans[1], spans[5]):
             key_passes(span)
             gate_by_gpsimd(span)
+        for span in spans[2:4] + spans[6:]:
+            packed_passes("v", span)
         gather_scales("k", 2, 3, "wk_raw4")
         last_words = held("slot_words_k", [P, PAIR], U32)
         slot_words["k", 2] = last_words
@@ -224,19 +220,16 @@ def tile_moe_qkb_kernel(
             h, a, b = span
             nc.vector.tensor_copy(out=last_words[:, a - 2 * PAIR : b - 2 * PAIR],
                                   in_=tok_words["k"][:, :T].bitcast(U32).indirect(entries(offs_sb, a, b)))
-        for span in spans[2:4]:
-            key_passes(span)
-            gate_by_vector(span)
-        for span in spans[5:]:
-            key_passes(span)
-            gate_by_gpsimd(span)
+        for i in (2, 3):
+            key_passes(spans[i])
+            gate_by_vector(spans[i])
+            key_passes(spans[4 + i])
+            gate_by_gpsimd(spans[4 + i])
 
-        pick(0, 0, 0, T)
-        pick(0, 1, 0, T)
-        add_and_store(nc.gpsimd, 0, 0, T)
-        pick(1, 0, 0, TOKEN_CUT)
-        pick(1, 0, TOKEN_CUT, T)
-        for a, b in ((0, TOKEN_CUT), (TOKEN_CUT, T)):
-            nc.vector.tensor_tensor(out=summed[1][:, a:b], in0=dx[1][:].indirect(entries(pos_sb[1], a, b)),
-                                    in1=picked[1][0][:, a:b], op=ADD)
-            nc.sync.dma_start(out=out[P:, a:b], in_=summed[1][:, a:b])
+        for h in range(2):
+            nc.vector.tensor_copy(out=picked[h][:], in_=dx[h][:].indirect(pos_sb[0][:]))
+        summed = [held("staged1_%d" % (S - P), [P, T], F32), held("summed1", [P, T], F32)]
+        for h, a, b in ((0, 0, T), (1, 0, TOKEN_CUT), (1, TOKEN_CUT, T)):
+            nc.vector.tensor_tensor(out=summed[h][:, a:b], in0=dx[h][:].indirect(entries(pos_sb[1], a, b)),
+                                    in1=picked[h][:, a:b], op=ADD)
+            nc.sync.dma_start(out=out[h * P : (h + 1) * P, a:b], in_=summed[h][:, a:b])

@@ -6,10 +6,11 @@ K, T, E, C, N = 256, 768, 6, 256, 512
 S = E * C
 P = 128
 PER_COLUMN = 16
-WIDE = 1024
-WIDE_V = 1376
 PAIR = 2 * C
 FLOPS = 2 * 3 * S * N * K
+
+HALF_WINDOW = 1024
+TWO_PAIR_WINDOW = 1376
 TOKEN_CUT = 576
 
 F32 = mybir.dt.float32
@@ -40,43 +41,50 @@ def tile_moe_qkb_kernel(
         offs_sb = lists.tile([P, S // PER_COLUMN], U16, name="offs_sb")
         pos_sb = [lists.tile([P, T // PER_COLUMN], U16, name="pos%d_sb" % r) for r in (1, 2)]
 
-        projections = ("q", "v", "k")
-        tok_words = {g: held("tok_words_" + g, [P, T if g == "k" else WIDE], I32) for g in projections}
-        tok_scales = {g: held("tok_scales_" + g, [P, {"q": WIDE, "v": WIDE_V, "k": T}[g]], U8) for g in projections}
+        packed = ("q", "v")
+        word_columns = {"q": HALF_WINDOW, "v": HALF_WINDOW, "k": T}
+        scale_columns = {"q": HALF_WINDOW, "v": TWO_PAIR_WINDOW, "k": T}
+        tok_words = {g: held("tok_words_" + g, [P, width], I32) for g, width in word_columns.items()}
+        tok_scales = {g: held("tok_scales_" + g, [P, width], U8) for g, width in scale_columns.items()}
         slot_words = {}
         slot_scales = {}
-        w4_words = {g: held("w4_words_" + g, [P, E, 2 * K], U8) for g in ("q", "v")}
-        w4_scales = {g: held("w4_scales_" + g, [P, E, K], U8) for g in ("q", "v")}
-        calls = (((0, 0), (1, 0), (0, 1), (1, 1), (2, 0), (3, 0), (4, 0), (4, 1)), ((2, 1), (3, 1), (5, 0), (5, 1)))
-        wk_words = [held("wk_words%d" % a, [P, len(c), P], U32) for a, c in enumerate(calls)]
-        wk_scales = [held("wk_scales%d" % a, [P, len(c), P], U8) for a, c in enumerate(calls)]
-        wk_bf = [held("wk_bf%d" % a, [P, len(c), P, 4], BF16) for a, c in enumerate(calls)]
-        wk_place = {block: (a, i) for a, c in enumerate(calls) for i, block in enumerate(c)}
+        w4_words = {g: held("w4_words_" + g, [P, E, 2 * K], U8) for g in packed}
+        w4_scales = {g: held("w4_scales_" + g, [P, E, K], U8) for g in packed}
+
+        early_blocks = [(e, 0) for e in range(4)]
+        late_blocks = [(e, h) for e in range(E) for h in range(2) if (e, h) not in early_blocks]
+        calls = (early_blocks, late_blocks)
+        wk_words = [held("wk_words%d" % i, [P, len(blocks), P], U32) for i, blocks in enumerate(calls)]
+        wk_scales = [held("wk_scales%d" % i, [P, len(blocks), P], U8) for i, blocks in enumerate(calls)]
+        wk_bf = [held("wk_bf%d" % i, [P, len(blocks), P, 4], BF16) for i, blocks in enumerate(calls)]
+        wk_place = {block: (call, i) for call, blocks in enumerate(calls) for i, block in enumerate(blocks)}
         wk_raw = [held("wk_raw%d" % e, [P, 4, K], F32) for e in range(E)]
         gate_sb = held("gate_sb", [P, S], F32)
         dx = [held("dx%d" % h, [P, S], F32) for h in range(2)]
         picked = [held("picked%d" % h, [P, T], F32) for h in range(2)]
+
         cuts = (0, PAIR, 2 * PAIR, S - P, S)
-        spans = [(h, cuts[i], cuts[i + 1]) for h in range(2) for i in range(4)]
-        banks = {span: ps.tile([P, span[2] - span[1]], F32, name="bank%d" % i) for i, span in enumerate(spans)}
+        spans = [[(h, cuts[i], cuts[i + 1]) for h in range(2)] for i in range(len(cuts) - 1)]
+        banks = {run[h]: ps.tile([P, run[h][2] - run[h][1]], F32, name="bank%d_%d" % run[h][:2])
+                 for h in range(2) for run in spans}
 
         tok_words_hbm = {"q": dq_words, "k": dk_words, "v": dv_words}
         tok_scales_hbm = {"q": dq_scales, "k": dk_scales, "v": dv_scales}
         w4_words_hbm = {"q": wq_words, "v": wv_words}
         w4_scales_hbm = {"q": wq_scales, "v": wv_scales}
 
-        def load_tok_scales(g):
+        def load_tok_scales(g, rs):
             rows = tok_scales_hbm[g][0].rearrange("(q r) t -> r q t", r=4)
-            for r in range(4):
+            for r in rs:
                 nc.sync.dma_start(out=tok_scales[g][r:P:32, :T].bitcast(I32), in_=rows[r].bitcast(I32))
 
         def load_tok_words(g):
             nc.sync.dma_start(out=tok_words[g][:, :T],
                               in_=tok_words_hbm[g][0].rearrange("p t d -> p (t d)").bitcast(I32))
 
-        def load_w4_scales(g):
+        def load_w4_scales(g, rs):
             rows = w4_scales_hbm[g].rearrange("e s (q r) c -> r q (e s) c", r=4)
-            for r in range(4):
+            for r in rs:
                 nc.sync.dma_start(out=w4_scales[g][r:P:32, :, :].bitcast(I32), in_=rows[r].bitcast(I32))
 
         def load_w4_words(g):
@@ -88,40 +96,33 @@ def tile_moe_qkb_kernel(
 
         def round_wk(e):
             for h in range(2):
-                a, i = wk_place[e, h]
-                nc.scalar.copy(out=wk_bf[a][:, i].rearrange("p (c i) j -> p c j i", i=4),
+                call, i = wk_place[e, h]
+                nc.scalar.copy(out=wk_bf[call][:, i].rearrange("p (c i) j -> p c j i", i=4),
                                in_=wk_raw[e][:, :, h * P : (h + 1) * P].rearrange("p j (c i) -> p c j i", i=4))
 
-        def quantize_wk(a):
+        def quantize_wk(call):
             nc.vector.quantize_mx(
-                out=wk_words[a][:].rearrange("p e c -> p (e c)").bitcast(FP8X4),
-                scales=wk_scales[a][:].rearrange("p e c -> p (e c)"),
-                in_=wk_bf[a][:].rearrange("p e c j -> p (e c j)"),
+                out=wk_words[call][:].rearrange("p e c -> p (e c)").bitcast(FP8X4),
+                scales=wk_scales[call][:].rearrange("p e c -> p (e c)"),
+                in_=wk_bf[call][:].rearrange("p e c j -> p (e c j)"),
             )
 
         def entries(list_sb, a, b):
             return list_sb[:, a // PER_COLUMN : b // PER_COLUMN]
 
-        def pieces(first, last):
-            if last - first == 3:
-                return ((0, S // 2), (S // 2, S))
-            return ((first * PAIR, last * PAIR),)
+        def gather(window, dtype, views, g, name, bounds):
+            first = bounds[0]
+            tile = held(name, [P, bounds[-1] - first], dtype)
+            for a, b in zip(bounds[:-1], bounds[1:]):
+                nc.vector.tensor_copy(out=tile[:, a - first : b - first], in_=window.indirect(entries(offs_sb, a, b)))
+            for a in range(first, bounds[-1], PAIR):
+                views[g, a // PAIR] = tile[:, a - first : a - first + PAIR]
 
-        def gather_words(g, first, last, name):
-            tile = held(name, [P, (last - first) * PAIR], U32)
-            for a, b in pieces(first, last):
-                nc.vector.tensor_copy(out=tile[:, a - first * PAIR : b - first * PAIR],
-                                      in_=tok_words[g][:].bitcast(U32).indirect(entries(offs_sb, a, b)))
-            for a in range(first, last):
-                slot_words[g, a] = tile[:, (a - first) * PAIR : (a - first + 1) * PAIR]
+        def gather_words(g, name, bounds):
+            gather(tok_words[g][:].bitcast(U32), U32, slot_words, g, name, bounds)
 
-        def gather_scales(g, first, last, name):
-            tile = held(name, [P, (last - first) * PAIR], U8)
-            for a, b in pieces(first, last):
-                nc.vector.tensor_copy(out=tile[:, a - first * PAIR : b - first * PAIR],
-                                      in_=tok_scales[g][:].indirect(entries(offs_sb, a, b)))
-            for a in range(first, last):
-                slot_scales[g, a] = tile[:, (a - first) * PAIR : (a - first + 1) * PAIR]
+        def gather_scales(g, name, bounds):
+            gather(tok_scales[g][:], U8, slot_scales, g, name, bounds)
 
         def slot_operand(g, a, b):
             pair = a // PAIR
@@ -131,28 +132,30 @@ def tile_moe_qkb_kernel(
         def packed_passes(g, span):
             h, first, last = span
             for a in range(first, last, P):
-                e = a // C
                 words, scales = slot_operand(g, a, a + P)
                 nc.tensor.matmul_mx(
                     out=banks[span][:, a - first : a - first + P],
-                    lhsT=w4_words[g][:, e, 2 * h * P : 2 * (h + 1) * P].bitcast(FP4X4),
-                    lhsT_scale=w4_scales[g][:, e, h * P : (h + 1) * P],
+                    lhsT=w4_words[g][:, a // C, 2 * h * P : 2 * (h + 1) * P].bitcast(FP4X4),
+                    lhsT_scale=w4_scales[g][:, a // C, h * P : (h + 1) * P],
                     rhs=words, rhs_scale=scales, start=(g == "q" and a == first), stop=False)
 
         def key_passes(span):
             h, first, last = span
             for a in range(first, last, C):
                 b = min(a + C, last)
-                call, block = wk_place[a // C, h]
+                call, i = wk_place[a // C, h]
                 words, scales = slot_operand("k", a, b)
                 nc.tensor.matmul_mx(
                     out=banks[span][:, a - first : b - first],
-                    lhsT=wk_words[call][:, block].bitcast(FP8X4), lhsT_scale=wk_scales[call][:, block],
+                    lhsT=wk_words[call][:, i].bitcast(FP8X4), lhsT_scale=wk_scales[call][:, i],
                     rhs=words, rhs_scale=scales, start=False, stop=(b == last))
+
+        def staged_name(span):
+            return "staged%d_%d" % span[:2]
 
         def gate_by_gpsimd(span):
             h, a, b = span
-            staged = held("staged%d_%d" % (h, a), [P, b - a], F32)
+            staged = held(staged_name(span), [P, b - a], F32)
             nc.scalar.copy(out=staged[:], in_=banks[span][:])
             nc.gpsimd.tensor_tensor(out=dx[h][:, a:b], in0=staged[:], in1=gate_sb[:, a:b], op=MULT)
 
@@ -163,28 +166,32 @@ def tile_moe_qkb_kernel(
         nc.gpsimd.memset(tok_scales["q"][:].bitcast(I32), 0)
         for g in ("v", "k"):
             nc.vector.memset(tok_scales[g][:].bitcast(I32), 0)
-        for g in ("q", "v"):
+        for g in packed:
             nc.vector.memset(w4_scales[g][:].bitcast(I32), 0)
-        for g in ("q", "v"):
+        for g in packed:
             nc.vector.memset(tok_words[g][:, T:], 0)
 
         nc.sync.dma_start(out=offs_sb[:], in_=offs)
-        load_tok_scales("q")
+        load_tok_scales("q", range(4))
         load_tok_words("q")
-        load_tok_words("v")
-        load_tok_scales("v")
         load_wk(0)
-        load_w4_words("q")
-        load_w4_scales("q")
+        load_tok_scales("v", (0, 1))
+        load_tok_words("v")
+        load_tok_scales("v", (2, 3))
         load_wk(1)
-        load_tok_scales("k")
+        load_w4_scales("q", (0, 1))
+        load_w4_words("q")
+        load_w4_scales("q", (2, 3))
         load_wk(2)
-        load_w4_words("v")
-        load_w4_scales("v")
+        load_tok_scales("k", (0, 1))
         load_wk(3)
-        load_tok_words("k")
+        load_tok_scales("k", (2, 3))
         load_wk(4)
         load_wk(5)
+        load_tok_words("k")
+        load_w4_scales("v", (0, 1))
+        load_w4_words("v")
+        load_w4_scales("v", (2, 3))
         nc.sync.dma_start(out=gate_sb[:], in_=gate)
         nc.sync.dma_start(out=pos_sb[0][:], in_=pos1)
         nc.sync.dma_start(out=pos_sb[1][:], in_=pos2)
@@ -192,43 +199,43 @@ def tile_moe_qkb_kernel(
         for e in range(E):
             round_wk(e)
 
-        for g in ("q", "v"):
-            gather_scales(g, 0, 3 if g == "q" else 2, "slot_scales_" + g)
-            gather_words(g, 0, 3, "slot_words_" + g)
-        gather_words("k", 0, 1, "slot_words_k")
-        for g in ("q", "v"):
-            for span in spans:
-                if g == "q" or span[1] < 2 * PAIR:
-                    packed_passes(g, span)
-
+        gather_scales("q", "slot_scales_q", (0, S // 2, S))
+        gather_scales("v", "slot_scales_v", (0, 2 * PAIR))
+        gather_scales("k", "slot_scales_k", (0, PAIR))
+        for g in packed:
+            gather_words(g, "slot_words_" + g, (0, S // 2, S))
         quantize_wk(0)
-        gather_scales("k", 0, 1, "wk_raw4")
-        quantize_wk(1)
-        gather_words("k", 1, 2, "wk_raw5")
-        gather_scales("k", 1, 2, "wk_bf1")
-        gather_scales("v", 2, 3, "wk_bf0")
+        gather_words("k", "slot_words_k", (0, PAIR))
+        for h in range(2):
+            for run in spans:
+                packed_passes("q", run[h])
 
-        for span in (spans[0], spans[4], spans[1], spans[5]):
-            key_passes(span)
-            gate_by_gpsimd(span)
-        for span in spans[2:4] + spans[6:]:
-            packed_passes("v", span)
-        gather_scales("k", 2, 3, "wk_raw4")
-        last_words = held("slot_words_k", [P, PAIR], U32)
-        slot_words["k", 2] = last_words
-        for span in spans[2:4]:
-            h, a, b = span
-            nc.vector.tensor_copy(out=last_words[:, a - 2 * PAIR : b - 2 * PAIR],
-                                  in_=tok_words["k"][:, :T].bitcast(U32).indirect(entries(offs_sb, a, b)))
-        for i in (2, 3):
-            key_passes(spans[i])
-            gate_by_vector(spans[i])
-            key_passes(spans[4 + i])
-            gate_by_gpsimd(spans[4 + i])
+        quantize_wk(1)
+        gather_words("k", "wk_raw%d" % (E - 1), (PAIR, 2 * PAIR))
+        gather_scales("k", "wk_bf1", (PAIR, 2 * PAIR))
+        for run in spans[:2]:
+            for span in run:
+                packed_passes("v", span)
+            for span in run:
+                key_passes(span)
+                gate_by_gpsimd(span)
+
+        gather_scales("v", "slot_words_k", (2 * PAIR, S))
+        for h in range(2):
+            for run in spans[2:]:
+                packed_passes("v", run[h])
+        gather_scales("k", "slot_scales_k", (2 * PAIR, S))
+        gather_words("k", staged_name(spans[0][1]), cuts[2:])
+
+        for first_half, second_half in spans[2:]:
+            key_passes(first_half)
+            gate_by_vector(first_half)
+            key_passes(second_half)
+            gate_by_gpsimd(second_half)
 
         for h in range(2):
             nc.vector.tensor_copy(out=picked[h][:], in_=dx[h][:].indirect(pos_sb[0][:]))
-        summed = [held("staged1_%d" % (S - P), [P, T], F32), held("summed1", [P, T], F32)]
+        summed = [held(staged_name(spans[-1][1]), [P, T], F32), held("summed1", [P, T], F32)]
         for h, a, b in ((0, 0, T), (1, 0, TOKEN_CUT), (1, TOKEN_CUT, T)):
             nc.vector.tensor_tensor(out=summed[h][:, a:b], in0=dx[h][:].indirect(entries(pos_sb[1], a, b)),
                                     in1=picked[h][:, a:b], op=ADD)

@@ -9,7 +9,7 @@ PER_COLUMN = 16
 PAIR = 2 * C
 FLOPS = 2 * 3 * S * N * K
 
-HALF_WINDOW = 1024
+WHOLE_WINDOW = 2048
 TWO_PAIR_WINDOW = 1376
 TOKEN_CUT = 576
 
@@ -42,8 +42,8 @@ def tile_moe_qkb_kernel(
         pos_sb = [lists.tile([P, T // PER_COLUMN], U16, name="pos%d_sb" % r) for r in (1, 2)]
 
         packed = ("q", "v")
-        word_columns = {"q": HALF_WINDOW, "v": HALF_WINDOW, "k": T}
-        scale_columns = {"q": HALF_WINDOW, "v": TWO_PAIR_WINDOW, "k": T}
+        word_columns = {"q": WHOLE_WINDOW, "v": WHOLE_WINDOW, "k": T}
+        scale_columns = {"q": WHOLE_WINDOW, "v": TWO_PAIR_WINDOW, "k": TWO_PAIR_WINDOW}
         tok_words = {g: held("tok_words_" + g, [P, width], I32) for g, width in word_columns.items()}
         tok_scales = {g: held("tok_scales_" + g, [P, width], U8) for g, width in scale_columns.items()}
         slot_words = {}
@@ -73,10 +73,10 @@ def tile_moe_qkb_kernel(
         w4_words_hbm = {"q": wq_words, "v": wv_words}
         w4_scales_hbm = {"q": wq_scales, "v": wv_scales}
 
-        def load_tok_scales(g, rs):
+        def load_tok_scales(g, rs, queue=nc.sync):
             rows = tok_scales_hbm[g][0].rearrange("(q r) t -> r q t", r=4)
             for r in rs:
-                nc.sync.dma_start(out=tok_scales[g][r:P:32, :T].bitcast(I32), in_=rows[r].bitcast(I32))
+                queue.dma_start(out=tok_scales[g][r:P:32, :T].bitcast(I32), in_=rows[r].bitcast(I32))
 
         def load_tok_words(g):
             nc.sync.dma_start(out=tok_words[g][:, :T],
@@ -163,16 +163,15 @@ def tile_moe_qkb_kernel(
             h, a, b = span
             nc.vector.tensor_tensor(out=dx[h][:, a:b], in0=banks[span][:], in1=gate_sb[:, a:b], op=MULT)
 
-        nc.gpsimd.memset(tok_scales["q"][:].bitcast(I32), 0)
+        nc.gpsimd.memset(tok_scales["q"][:, :T].bitcast(I32), 0)
         for g in ("v", "k"):
-            nc.vector.memset(tok_scales[g][:].bitcast(I32), 0)
+            nc.vector.memset(tok_scales[g][:, :T].bitcast(I32), 0)
         for g in packed:
             nc.vector.memset(w4_scales[g][:].bitcast(I32), 0)
-        for g in packed:
-            nc.vector.memset(tok_words[g][:, T:], 0)
 
         nc.sync.dma_start(out=offs_sb[:], in_=offs)
-        load_tok_scales("q", range(4))
+        load_tok_scales("q", (0, 1))
+        load_tok_scales("q", (2, 3), nc.scalar)
         load_tok_words("q")
         load_wk(0)
         load_tok_scales("v", (0, 1))
@@ -199,11 +198,11 @@ def tile_moe_qkb_kernel(
         for e in range(E):
             round_wk(e)
 
-        gather_scales("q", "slot_scales_q", (0, S // 2, S))
+        gather_scales("q", "slot_scales_q", (0, S))
         gather_scales("v", "slot_scales_v", (0, 2 * PAIR))
-        gather_scales("k", "slot_scales_k", (0, PAIR))
+        gather_scales("k", "slot_scales_k", (0, 2 * PAIR))
         for g in packed:
-            gather_words(g, "slot_words_" + g, (0, S // 2, S))
+            gather_words(g, "slot_words_" + g, (0, S))
         quantize_wk(0)
         gather_words("k", "slot_words_k", (0, PAIR))
         for h in range(2):
@@ -212,7 +211,6 @@ def tile_moe_qkb_kernel(
 
         quantize_wk(1)
         gather_words("k", "wk_raw%d" % (E - 1), (PAIR, 2 * PAIR))
-        gather_scales("k", "wk_bf1", (PAIR, 2 * PAIR))
         for run in spans[:2]:
             for span in run:
                 packed_passes("v", span)
@@ -224,7 +222,7 @@ def tile_moe_qkb_kernel(
         for h in range(2):
             for run in spans[2:]:
                 packed_passes("v", run[h])
-        gather_scales("k", "slot_scales_k", (2 * PAIR, S))
+        gather_scales("k", staged_name(spans[0][0]), (2 * PAIR, S))
         gather_words("k", staged_name(spans[0][1]), cuts[2:])
 
         for first_half, second_half in spans[2:]:

@@ -5,6 +5,7 @@ import concourse.mybir as mybir
 K, T, E, C, N = 256, 768, 6, 256, 512
 S = E * C
 P = 128
+BLOCKS = N // 32
 PER_COLUMN = 16
 PAIR = 2 * C
 FLOPS = 2 * 3 * S * N * K
@@ -46,6 +47,8 @@ def tile_moe_qkb_kernel(
         scale_columns = {"q": WHOLE_WINDOW, "v": TWO_PAIR_WINDOW, "k": TWO_PAIR_WINDOW}
         tok_words = {g: held("tok_words_" + g, [P, width], I32) for g, width in word_columns.items()}
         tok_scales = {g: held("tok_scales_" + g, [P, width], U8) for g, width in scale_columns.items()}
+        slot_plane_q = held("slot_plane_q", [P, S], U8)
+        gathered = {}
         slot_words = {}
         slot_scales = {}
         w4_words = {g: held("w4_words_" + g, [P, E, 2 * K], U8) for g in packed}
@@ -73,10 +76,10 @@ def tile_moe_qkb_kernel(
         w4_words_hbm = {"q": wq_words, "v": wv_words}
         w4_scales_hbm = {"q": wq_scales, "v": wv_scales}
 
-        def load_tok_scales(g, rs, queue=nc.sync):
+        def load_tok_scales(g, rs):
             rows = tok_scales_hbm[g][0].rearrange("(q r) t -> r q t", r=4)
             for r in rs:
-                queue.dma_start(out=tok_scales[g][r:P:32, :T].bitcast(I32), in_=rows[r].bitcast(I32))
+                nc.sync.dma_start(out=tok_scales[g][r:P:32, :T].bitcast(I32), in_=rows[r].bitcast(I32))
 
         def load_tok_words(g):
             nc.sync.dma_start(out=tok_words[g][:, :T],
@@ -113,6 +116,7 @@ def tile_moe_qkb_kernel(
         def gather(window, dtype, views, g, name, bounds):
             first = bounds[0]
             tile = held(name, [P, bounds[-1] - first], dtype)
+            gathered[name] = tile
             for a, b in zip(bounds[:-1], bounds[1:]):
                 nc.vector.tensor_copy(out=tile[:, a - first : b - first], in_=window.indirect(entries(offs_sb, a, b)))
             for a in range(first, bounds[-1], PAIR):
@@ -168,10 +172,10 @@ def tile_moe_qkb_kernel(
             nc.vector.memset(tok_scales[g][:, :T].bitcast(I32), 0)
         for g in packed:
             nc.vector.memset(w4_scales[g][:].bitcast(I32), 0)
+        nc.vector.memset(slot_plane_q[:].bitcast(I32), 0)
 
         nc.sync.dma_start(out=offs_sb[:], in_=offs)
-        load_tok_scales("q", (0, 1))
-        load_tok_scales("q", (2, 3), nc.scalar)
+        nc.sync.dma_start(out=tok_scales["q"][:BLOCKS, :T].bitcast(I32), in_=dq_scales[0].bitcast(I32))
         load_tok_words("q")
         load_wk(0)
         load_tok_scales("v", (0, 1))
@@ -198,7 +202,12 @@ def tile_moe_qkb_kernel(
         for e in range(E):
             round_wk(e)
 
-        gather_scales("q", "slot_scales_q", (0, S))
+        gather_scales("q", "slot_rows_q", (0, S))
+        for q in range(4):
+            nc.gpsimd.dma_start(out=slot_plane_q[32 * q : 32 * q + 4, :].bitcast(I32),
+                                in_=gathered["slot_rows_q"][4 * q : 4 * q + 4, :].bitcast(I32))
+        for pair in range(S // PAIR):
+            slot_scales["q", pair] = slot_plane_q[:, pair * PAIR : (pair + 1) * PAIR]
         gather_scales("v", "slot_scales_v", (0, 2 * PAIR))
         gather_scales("k", "slot_scales_k", (0, 2 * PAIR))
         for g in packed:
@@ -229,11 +238,12 @@ def tile_moe_qkb_kernel(
             key_passes(first_half)
             gate_by_vector(first_half)
             key_passes(second_half)
-            gate_by_gpsimd(second_half)
+        gate_by_gpsimd(spans[2][1])
+        gate_by_vector(spans[3][1])
 
         for h in range(2):
             nc.vector.tensor_copy(out=picked[h][:], in_=dx[h][:].indirect(pos_sb[0][:]))
-        summed = [held(staged_name(spans[-1][1]), [P, T], F32), held("summed1", [P, T], F32)]
+        summed = [held(staged_name(spans[2][1]), [P, T], F32), held("summed1", [P, T], F32)]
         for h, a, b in ((0, 0, T), (1, 0, TOKEN_CUT), (1, TOKEN_CUT, T)):
             nc.vector.tensor_tensor(out=summed[h][:, a:b], in0=dx[h][:].indirect(entries(pos_sb[1], a, b)),
                                     in1=picked[h][:, a:b], op=ADD)

@@ -12,7 +12,6 @@ FLOPS = 2 * 3 * S * N * K
 
 WHOLE_WINDOW = 2048
 TWO_PAIR_WINDOW = 1376
-TOKEN_CUT = 576
 
 F32 = mybir.dt.float32
 BF16 = mybir.dt.bfloat16
@@ -244,7 +243,7 @@ def tile_moe_qkb_kernel(
         for h in range(2):
             nc.vector.tensor_copy(out=picked[h][:], in_=dx[h][:].indirect(pos_sb[0][:]))
         summed = [held(staged_name(spans[2][1]), [P, T], F32), held("summed1", [P, T], F32)]
-        for h, a, b in ((0, 0, T), (1, 0, TOKEN_CUT), (1, TOKEN_CUT, T)):
+        for h, a, b in ((0, 0, T), (1, 0, T // 2), (1, T // 2, T - P), (1, T - P, T)):
             nc.vector.tensor_tensor(out=summed[h][:, a:b], in0=dx[h][:].indirect(entries(pos_sb[1], a, b)),
                                     in1=picked[h][:, a:b], op=ADD)
             nc.sync.dma_start(out=out[h * P : (h + 1) * P, a:b], in_=summed[h][:, a:b])

@@ -12,6 +12,7 @@ FLOPS = 2 * 3 * S * N * K
 
 WHOLE_WINDOW = 2048
 TWO_PAIR_WINDOW = 1376
+TOKEN_CUTS = (0, T // 2, T - P, T)
 
 F32 = mybir.dt.float32
 BF16 = mybir.dt.bfloat16
@@ -33,9 +34,14 @@ def tile_moe_qkb_kernel(
     with ExitStack() as ctx:
         lists = ctx.enter_context(tc.tile_pool(name="lists", bufs=1))
         sb = ctx.enter_context(tc.tile_pool(name="sb", bufs=1))
+        late = ctx.enter_context(tc.tile_pool(name="late", bufs=1))
         ps = ctx.enter_context(tc.psum_pool(name="ps", bufs=1))
 
+        late_offsets = {"wk_bf1": 0, "late_scales_v": 0, "late_scales_k": PAIR, "late_words_k": 2 * PAIR}
+
         def held(name, shape, dtype):
+            if name in late_offsets:
+                return late.tile(shape, dtype, name=name, align_bytes=64, offset=late_offsets[name])
             return sb.tile(shape, dtype, name=name, align_bytes=64)
 
         offs_sb = lists.tile([P, S // PER_COLUMN], U16, name="offs_sb")
@@ -46,8 +52,7 @@ def tile_moe_qkb_kernel(
         scale_columns = {"q": WHOLE_WINDOW, "v": TWO_PAIR_WINDOW, "k": TWO_PAIR_WINDOW}
         tok_words = {g: held("tok_words_" + g, [P, width], I32) for g, width in word_columns.items()}
         tok_scales = {g: held("tok_scales_" + g, [P, width], U8) for g, width in scale_columns.items()}
-        slot_plane_q = held("slot_plane_q", [P, S], U8)
-        gathered = {}
+        slot_scales_q = held("slot_plane_q", [P, S], U8)
         slot_words = {}
         slot_scales = {}
         w4_words = {g: held("w4_words_" + g, [P, E, 2 * K], U8) for g in packed}
@@ -112,20 +117,24 @@ def tile_moe_qkb_kernel(
         def entries(list_sb, a, b):
             return list_sb[:, a // PER_COLUMN : b // PER_COLUMN]
 
-        def gather(window, dtype, views, g, name, bounds):
+        def gather(window, dtype, name, bounds):
             first = bounds[0]
             tile = held(name, [P, bounds[-1] - first], dtype)
-            gathered[name] = tile
             for a, b in zip(bounds[:-1], bounds[1:]):
                 nc.vector.tensor_copy(out=tile[:, a - first : b - first], in_=window.indirect(entries(offs_sb, a, b)))
-            for a in range(first, bounds[-1], PAIR):
+            return tile
+
+        def file_by_pair(views, g, tile, first, last):
+            for a in range(first, last, PAIR):
                 views[g, a // PAIR] = tile[:, a - first : a - first + PAIR]
 
         def gather_words(g, name, bounds):
-            gather(tok_words[g][:].bitcast(U32), U32, slot_words, g, name, bounds)
+            tile = gather(tok_words[g][:].bitcast(U32), U32, name, bounds)
+            file_by_pair(slot_words, g, tile, bounds[0], bounds[-1])
 
         def gather_scales(g, name, bounds):
-            gather(tok_scales[g][:], U8, slot_scales, g, name, bounds)
+            tile = gather(tok_scales[g][:], U8, name, bounds)
+            file_by_pair(slot_scales, g, tile, bounds[0], bounds[-1])
 
         def slot_operand(g, a, b):
             pair = a // PAIR
@@ -166,34 +175,34 @@ def tile_moe_qkb_kernel(
             h, a, b = span
             nc.vector.tensor_tensor(out=dx[h][:, a:b], in0=banks[span][:], in1=gate_sb[:, a:b], op=MULT)
 
-        nc.gpsimd.memset(tok_scales["q"][:, :T].bitcast(I32), 0)
+        for first, last in ((32, 64), (64, P)):
+            nc.gpsimd.memset(tok_scales["q"][first:last, :T].bitcast(I32), 0)
         for g in ("v", "k"):
             nc.vector.memset(tok_scales[g][:, :T].bitcast(I32), 0)
         for g in packed:
             nc.vector.memset(w4_scales[g][:].bitcast(I32), 0)
-        nc.vector.memset(slot_plane_q[:].bitcast(I32), 0)
+        nc.vector.memset(slot_scales_q[:].bitcast(I32), 0)
 
         nc.sync.dma_start(out=offs_sb[:], in_=offs)
-        nc.sync.dma_start(out=tok_scales["q"][:BLOCKS, :T].bitcast(I32), in_=dq_scales[0].bitcast(I32))
+        nc.sync.dma_start(out=tok_scales["q"][: 2 * BLOCKS, :T].bitcast(I32),
+                          in_=dq_scales[0].bitcast(I32).unsqueeze(1).to_broadcast([BLOCKS, 2, T // 4]))
         load_tok_words("q")
-        load_wk(0)
-        load_tok_scales("v", (0, 1))
+        load_tok_scales("v", range(4))
         load_tok_words("v")
-        load_tok_scales("v", (2, 3))
-        load_wk(1)
-        load_w4_scales("q", (0, 1))
-        load_w4_words("q")
-        load_w4_scales("q", (2, 3))
-        load_wk(2)
-        load_tok_scales("k", (0, 1))
-        load_wk(3)
-        load_tok_scales("k", (2, 3))
-        load_wk(4)
-        load_wk(5)
+        load_wk(0)
+        load_tok_scales("k", range(4))
         load_tok_words("k")
+        load_wk(1)
+        load_wk(2)
+        load_w4_scales("q", (0, 1))
+        load_wk(3)
+        load_w4_scales("q", (2, 3))
+        load_wk(4)
         load_w4_scales("v", (0, 1))
-        load_w4_words("v")
+        load_wk(5)
         load_w4_scales("v", (2, 3))
+        load_w4_words("q")
+        load_w4_words("v")
         nc.sync.dma_start(out=gate_sb[:], in_=gate)
         nc.sync.dma_start(out=pos_sb[0][:], in_=pos1)
         nc.sync.dma_start(out=pos_sb[1][:], in_=pos2)
@@ -201,12 +210,11 @@ def tile_moe_qkb_kernel(
         for e in range(E):
             round_wk(e)
 
-        gather_scales("q", "slot_rows_q", (0, S))
+        slot_rows_q = gather(tok_scales["q"][:], U8, "slot_rows_q", (0, S))
         for q in range(4):
-            nc.gpsimd.dma_start(out=slot_plane_q[32 * q : 32 * q + 4, :].bitcast(I32),
-                                in_=gathered["slot_rows_q"][4 * q : 4 * q + 4, :].bitcast(I32))
-        for pair in range(S // PAIR):
-            slot_scales["q", pair] = slot_plane_q[:, pair * PAIR : (pair + 1) * PAIR]
+            nc.gpsimd.dma_start(out=slot_scales_q[32 * q : 32 * q + 4, :].bitcast(I32),
+                                in_=slot_rows_q[8 * q : 8 * q + 8 : 2, :].bitcast(I32))
+        file_by_pair(slot_scales, "q", slot_scales_q, 0, S)
         gather_scales("v", "slot_scales_v", (0, 2 * PAIR))
         gather_scales("k", "slot_scales_k", (0, 2 * PAIR))
         for g in packed:
@@ -226,12 +234,12 @@ def tile_moe_qkb_kernel(
                 key_passes(span)
                 gate_by_gpsimd(span)
 
-        gather_scales("v", "slot_words_k", (2 * PAIR, S))
+        gather_scales("v", "late_scales_v", (2 * PAIR, S))
         for h in range(2):
             for run in spans[2:]:
                 packed_passes("v", run[h])
-        gather_scales("k", staged_name(spans[0][0]), (2 * PAIR, S))
-        gather_words("k", staged_name(spans[0][1]), cuts[2:])
+        gather_scales("k", "late_scales_k", (2 * PAIR, S))
+        gather_words("k", "late_words_k", cuts[2:])
 
         for first_half, second_half in spans[2:]:
             key_passes(first_half)
@@ -243,7 +251,7 @@ def tile_moe_qkb_kernel(
         for h in range(2):
             nc.vector.tensor_copy(out=picked[h][:], in_=dx[h][:].indirect(pos_sb[0][:]))
         summed = [held(staged_name(spans[2][1]), [P, T], F32), held("summed1", [P, T], F32)]
-        for h, a, b in ((0, 0, T), (1, 0, T // 2), (1, T // 2, T - P), (1, T - P, T)):
+        for h, a, b in [(0, 0, T)] + [(1, a, b) for a, b in zip(TOKEN_CUTS[:-1], TOKEN_CUTS[1:])]:
             nc.vector.tensor_tensor(out=summed[h][:, a:b], in0=dx[h][:].indirect(entries(pos_sb[1], a, b)),
                                     in1=picked[h][:, a:b], op=ADD)
             nc.sync.dma_start(out=out[h * P : (h + 1) * P, a:b], in_=summed[h][:, a:b])

@@ -11,7 +11,10 @@ PAIR = 2 * C
 FLOPS = 2 * 3 * S * N * K
 
 WHOLE_WINDOW = 2048
-TWO_PAIR_WINDOW = 1376
+LATE = S - 3 * P
+EARLY_WINDOW = 1536
+SECOND_WINDOW = 896
+FILL_END = PAIR + 3 * P
 TOKEN_CUTS = (0, T // 2, T - P, T)
 
 F32 = mybir.dt.float32
@@ -48,8 +51,8 @@ def tile_moe_qkb_kernel(
         pos_sb = [lists.tile([P, T // PER_COLUMN], U16, name="pos%d_sb" % r) for r in (1, 2)]
 
         packed = ("q", "v")
-        word_columns = {"q": WHOLE_WINDOW, "v": WHOLE_WINDOW, "k": T}
-        scale_columns = {"q": WHOLE_WINDOW, "v": TWO_PAIR_WINDOW, "k": TWO_PAIR_WINDOW}
+        word_columns = {"q": WHOLE_WINDOW, "v": WHOLE_WINDOW, "k": SECOND_WINDOW}
+        scale_columns = {"q": WHOLE_WINDOW, "v": EARLY_WINDOW, "k": EARLY_WINDOW}
         tok_words = {g: held("tok_words_" + g, [P, width], I32) for g, width in word_columns.items()}
         tok_scales = {g: held("tok_scales_" + g, [P, width], U8) for g, width in scale_columns.items()}
         slot_scales_q = held("slot_plane_q", [P, S], U8)
@@ -70,10 +73,20 @@ def tile_moe_qkb_kernel(
         dx = [held("dx%d" % h, [P, S], F32) for h in range(2)]
         picked = [held("picked%d" % h, [P, T], F32) for h in range(2)]
 
-        cuts = (0, PAIR, 2 * PAIR, S - P, S)
-        spans = [[(h, cuts[i], cuts[i + 1]) for h in range(2)] for i in range(len(cuts) - 1)]
-        banks = {run[h]: ps.tile([P, run[h][2] - run[h][1]], F32, name="bank%d_%d" % run[h][:2])
-                 for h in range(2) for run in spans}
+        first0, first1 = (0, 0, PAIR), (1, 0, PAIR)
+        second0, second1 = (0, PAIR, 2 * PAIR), (1, PAIR, FILL_END)
+        rest0, rest1 = (0, 2 * PAIR, LATE), (1, FILL_END, LATE)
+        third0, last0, last1 = (0, LATE, S - P), (0, S - P, S), (1, LATE, S)
+        groups = [[first0], [first1], [second0], [rest0, rest1], [second1], [third0], [last0], [last1]]
+        sums = {}
+        for group in groups:
+            bank = ps.tile([P, sum(b - a for h, a, b in group)], F32, name="bank%d_%d" % group[0][:2])
+            column = 0
+            for h, a, b in group:
+                sums[h, a, b] = bank[:, column : column + b - a]
+                column = column + b - a
+        opens = [group[0] for group in groups]
+        closes = [group[-1] for group in groups]
 
         tok_words_hbm = {"q": dq_words, "k": dk_words, "v": dv_words}
         tok_scales_hbm = {"q": dq_scales, "k": dk_scales, "v": dv_scales}
@@ -125,8 +138,8 @@ def tile_moe_qkb_kernel(
             return tile
 
         def file_by_pair(views, g, tile, first, last):
-            for a in range(first, last, PAIR):
-                views[g, a // PAIR] = tile[:, a - first : a - first + PAIR]
+            for a in range(first, last, P):
+                views[g, a // P] = (tile, first)
 
         def gather_words(g, name, bounds):
             tile = gather(tok_words[g][:].bitcast(U32), U32, name, bounds)
@@ -137,43 +150,43 @@ def tile_moe_qkb_kernel(
             file_by_pair(slot_scales, g, tile, bounds[0], bounds[-1])
 
         def slot_operand(g, a, b):
-            pair = a // PAIR
-            cols = slice(a - pair * PAIR, b - pair * PAIR)
-            return slot_words[g, pair][:, cols].bitcast(FP8X4), slot_scales[g, pair][:, cols]
+            (words, first_word), (scales, first_scale) = slot_words[g, a // P], slot_scales[g, a // P]
+            return words[:, a - first_word : b - first_word].bitcast(FP8X4), scales[:, a - first_scale : b - first_scale]
 
         def packed_passes(g, span):
             h, first, last = span
             for a in range(first, last, P):
                 words, scales = slot_operand(g, a, a + P)
                 nc.tensor.matmul_mx(
-                    out=banks[span][:, a - first : a - first + P],
+                    out=sums[span][:, a - first : a - first + P],
                     lhsT=w4_words[g][:, a // C, 2 * h * P : 2 * (h + 1) * P].bitcast(FP4X4),
                     lhsT_scale=w4_scales[g][:, a // C, h * P : (h + 1) * P],
-                    rhs=words, rhs_scale=scales, start=(g == "q" and a == first), stop=False)
+                    rhs=words, rhs_scale=scales, start=(g == "q" and a == first and span in opens), stop=False)
 
         def key_passes(span):
             h, first, last = span
-            for a in range(first, last, C):
-                b = min(a + C, last)
+            bounds = [first] + list(range((first // C + 1) * C, last, C)) + [last]
+            for a, b in zip(bounds[:-1], bounds[1:]):
                 call, i = wk_place[a // C, h]
                 words, scales = slot_operand("k", a, b)
                 nc.tensor.matmul_mx(
-                    out=banks[span][:, a - first : b - first],
+                    out=sums[span][:, a - first : b - first],
                     lhsT=wk_words[call][:, i].bitcast(FP8X4), lhsT_scale=wk_scales[call][:, i],
-                    rhs=words, rhs_scale=scales, start=False, stop=(b == last))
+                    rhs=words, rhs_scale=scales, start=False, stop=(b == last and span in closes))
 
         def staged_name(span):
             return "staged%d_%d" % span[:2]
 
-        def gate_by_gpsimd(span):
-            h, a, b = span
-            staged = held(staged_name(span), [P, b - a], F32)
-            nc.scalar.copy(out=staged[:], in_=banks[span][:])
-            nc.gpsimd.tensor_tensor(out=dx[h][:, a:b], in0=staged[:], in1=gate_sb[:, a:b], op=MULT)
+        def gate_by_gpsimd(*parts):
+            h, first, last = parts[0][0], parts[0][1], parts[-1][2]
+            staged = held(staged_name(parts[0]), [P, last - first], F32)
+            for span in parts:
+                nc.scalar.copy(out=staged[:, span[1] - first : span[2] - first], in_=sums[span])
+            nc.gpsimd.tensor_tensor(out=dx[h][:, first:last], in0=staged[:], in1=gate_sb[:, first:last], op=MULT)
 
         def gate_by_vector(span):
             h, a, b = span
-            nc.vector.tensor_tensor(out=dx[h][:, a:b], in0=banks[span][:], in1=gate_sb[:, a:b], op=MULT)
+            nc.vector.tensor_tensor(out=dx[h][:, a:b], in0=sums[span], in1=gate_sb[:, a:b], op=MULT)
 
         for first, last in ((32, 64), (64, P)):
             nc.gpsimd.memset(tok_scales["q"][first:last, :T].bitcast(I32), 0)
@@ -215,42 +228,44 @@ def tile_moe_qkb_kernel(
             nc.gpsimd.dma_start(out=slot_scales_q[32 * q : 32 * q + 4, :].bitcast(I32),
                                 in_=slot_rows_q[8 * q : 8 * q + 8 : 2, :].bitcast(I32))
         file_by_pair(slot_scales, "q", slot_scales_q, 0, S)
-        gather_scales("v", "slot_scales_v", (0, 2 * PAIR))
-        gather_scales("k", "slot_scales_k", (0, 2 * PAIR))
+        gather_scales("v", "slot_scales_v", (0, LATE))
+        gather_scales("k", "slot_scales_k", (0, LATE))
         for g in packed:
             gather_words(g, "slot_words_" + g, (0, S))
         quantize_wk(0)
         gather_words("k", "slot_words_k", (0, PAIR))
-        for h in range(2):
-            for run in spans:
-                packed_passes("q", run[h])
+        for group in groups:
+            for span in group:
+                packed_passes("q", span)
 
         quantize_wk(1)
-        gather_words("k", "wk_raw%d" % (E - 1), (PAIR, 2 * PAIR))
-        for run in spans[:2]:
-            for span in run:
-                packed_passes("v", span)
-            for span in run:
-                key_passes(span)
-                gate_by_gpsimd(span)
+        gather_words("k", "wk_raw%d" % (E - 1), (PAIR, LATE))
+        for span in (first0, first1):
+            packed_passes("v", span)
+        for span in (first0, first1):
+            key_passes(span)
+            gate_by_gpsimd(span)
+        for span in (second0, rest0, rest1, second1):
+            packed_passes("v", span)
+        for span in (second0, rest0, rest1, second1):
+            key_passes(span)
+        gate_by_gpsimd(second0, rest0)
+        gate_by_gpsimd(rest1)
 
-        gather_scales("v", "late_scales_v", (2 * PAIR, S))
-        for h in range(2):
-            for run in spans[2:]:
-                packed_passes("v", run[h])
-        gather_scales("k", "late_scales_k", (2 * PAIR, S))
-        gather_words("k", "late_words_k", cuts[2:])
+        gather_scales("v", "late_scales_v", (LATE, S))
+        for span in (third0, last0, last1):
+            packed_passes("v", span)
+        gather_scales("k", "late_scales_k", (LATE, S))
+        gather_words("k", "late_words_k", (LATE, S - P, S))
 
-        for first_half, second_half in spans[2:]:
-            key_passes(first_half)
-            gate_by_vector(first_half)
-            key_passes(second_half)
-        gate_by_gpsimd(spans[2][1])
-        gate_by_vector(spans[3][1])
+        gate_by_vector(second1)
+        for span in (third0, last0, last1):
+            key_passes(span)
+            gate_by_vector(span)
 
         for h in range(2):
             nc.vector.tensor_copy(out=picked[h][:], in_=dx[h][:].indirect(pos_sb[0][:]))
-        summed = [held(staged_name(spans[2][1]), [P, T], F32), held("summed1", [P, T], F32)]
+        summed = [held(staged_name(rest1), [P, T], F32), held("summed1", [P, T], F32)]
         for h, a, b in [(0, 0, T)] + [(1, a, b) for a, b in zip(TOKEN_CUTS[:-1], TOKEN_CUTS[1:])]:
             nc.vector.tensor_tensor(out=summed[h][:, a:b], in0=dx[h][:].indirect(entries(pos_sb[1], a, b)),
                                     in1=picked[h][:, a:b], op=ADD)

@@ -40,7 +40,7 @@ def tile_moe_qkb_kernel(
         late = ctx.enter_context(tc.tile_pool(name="late", bufs=1))
         ps = ctx.enter_context(tc.psum_pool(name="ps", bufs=1))
 
-        late_offsets = {"wk_bf1": 0, "late_scales_v": 0, "late_scales_k": PAIR, "late_words_k": 2 * PAIR}
+        late_offsets = {"wk_bf1": 0, "late_scales_k": 0, "late_words_k": PAIR}
 
         def held(name, shape, dtype):
             if name in late_offsets:
@@ -52,7 +52,7 @@ def tile_moe_qkb_kernel(
 
         packed = ("q", "v")
         word_columns = {"q": WHOLE_WINDOW, "v": WHOLE_WINDOW, "k": SECOND_WINDOW}
-        scale_columns = {"q": WHOLE_WINDOW, "v": EARLY_WINDOW, "k": EARLY_WINDOW}
+        scale_columns = {"q": WHOLE_WINDOW, "v": WHOLE_WINDOW, "k": EARLY_WINDOW}
         tok_words = {g: held("tok_words_" + g, [P, width], I32) for g, width in word_columns.items()}
         tok_scales = {g: held("tok_scales_" + g, [P, width], U8) for g, width in scale_columns.items()}
         slot_scales_q = held("slot_plane_q", [P, S], U8)
@@ -74,10 +74,10 @@ def tile_moe_qkb_kernel(
         picked = [held("picked%d" % h, [P, T], F32) for h in range(2)]
 
         first0, first1 = (0, 0, PAIR), (1, 0, PAIR)
-        second0, second1 = (0, PAIR, 2 * PAIR), (1, PAIR, FILL_END)
-        rest0, rest1 = (0, 2 * PAIR, LATE), (1, FILL_END, LATE)
+        second0, second1 = (0, PAIR, FILL_END), (1, PAIR, 2 * PAIR)
+        rest0, rest1 = (0, FILL_END, LATE), (1, 2 * PAIR, LATE)
         third0, last0, last1 = (0, LATE, S - P), (0, S - P, S), (1, LATE, S)
-        groups = [[first0], [first1], [second0], [rest0, rest1], [second1], [third0], [last0], [last1]]
+        groups = [[first0], [first1], [rest0, rest1], [second1], [second0], [third0], [last0], [last1]]
         sums = {}
         for group in groups:
             bank = ps.tile([P, sum(b - a for h, a, b in group)], F32, name="bank%d_%d" % group[0][:2])
@@ -228,7 +228,7 @@ def tile_moe_qkb_kernel(
             nc.gpsimd.dma_start(out=slot_scales_q[32 * q : 32 * q + 4, :].bitcast(I32),
                                 in_=slot_rows_q[8 * q : 8 * q + 8 : 2, :].bitcast(I32))
         file_by_pair(slot_scales, "q", slot_scales_q, 0, S)
-        gather_scales("v", "slot_scales_v", (0, LATE))
+        gather_scales("v", "slot_scales_v", (0, S))
         gather_scales("k", "slot_scales_k", (0, LATE))
         for g in packed:
             gather_words(g, "slot_words_" + g, (0, S))
@@ -245,27 +245,26 @@ def tile_moe_qkb_kernel(
         for span in (first0, first1):
             key_passes(span)
             gate_by_gpsimd(span)
-        for span in (second0, rest0, rest1, second1):
+        for span in (rest0, rest1, second1, second0):
             packed_passes("v", span)
-        for span in (second0, rest0, rest1, second1):
+        for span in (rest0, rest1, second1, second0):
             key_passes(span)
-        gate_by_gpsimd(second0, rest0)
-        gate_by_gpsimd(rest1)
+        gate_by_gpsimd(rest0)
+        gate_by_gpsimd(second1, rest1)
 
-        gather_scales("v", "late_scales_v", (LATE, S))
         for span in (third0, last0, last1):
             packed_passes("v", span)
         gather_scales("k", "late_scales_k", (LATE, S))
         gather_words("k", "late_words_k", (LATE, S - P, S))
 
-        gate_by_vector(second1)
+        gate_by_vector(second0)
         for span in (third0, last0, last1):
             key_passes(span)
             gate_by_vector(span)
 
         for h in range(2):
             nc.vector.tensor_copy(out=picked[h][:], in_=dx[h][:].indirect(pos_sb[0][:]))
-        summed = [held(staged_name(rest1), [P, T], F32), held("summed1", [P, T], F32)]
+        summed = [held(staged_name(second1), [P, T], F32), held("summed1", [P, T], F32)]
         for h, a, b in [(0, 0, T)] + [(1, a, b) for a, b in zip(TOKEN_CUTS[:-1], TOKEN_CUTS[1:])]:
             nc.vector.tensor_tensor(out=summed[h][:, a:b], in0=dx[h][:].indirect(entries(pos_sb[1], a, b)),
                                     in1=picked[h][:, a:b], op=ADD)

@@ -76,17 +76,22 @@ def tile_moe_qkb_kernel(
         first0, first1 = (0, 0, PAIR), (1, 0, PAIR)
         second0, second1 = (0, PAIR, FILL_END), (1, PAIR, 2 * PAIR)
         rest0, rest1 = (0, FILL_END, LATE), (1, 2 * PAIR, LATE)
-        third0, last0, last1 = (0, LATE, S - P), (0, S - P, S), (1, LATE, S)
+        third0, third1 = (0, LATE, S - P), (1, LATE, S - C)
+        last0, last1 = (0, S - P, S), (1, S - C, S)
         groups = [[first0], [first1], [rest0, rest1], [second1], [second0], [third0], [last0], [last1]]
         sums = {}
-        for group in groups:
-            bank = ps.tile([P, sum(b - a for h, a, b in group)], F32, name="bank%d_%d" % group[0][:2])
+
+        def take_bank(group, name):
+            bank = ps.tile([P, sum(b - a for h, a, b in group)], F32, name=name)
             column = 0
             for h, a, b in group:
                 sums[h, a, b] = bank[:, column : column + b - a]
                 column = column + b - a
-        opens = [group[0] for group in groups]
-        closes = [group[-1] for group in groups]
+
+        for i, group in enumerate(groups):
+            take_bank(group, "bank%d" % i)
+        opens = [group[0] for group in groups] + [third1]
+        closes = [group[-1] for group in groups] + [third1]
 
         tok_words_hbm = {"q": dq_words, "k": dk_words, "v": dv_words}
         tok_scales_hbm = {"q": dq_scales, "k": dk_scales, "v": dv_scales}
@@ -251,8 +256,10 @@ def tile_moe_qkb_kernel(
             key_passes(span)
         gate_by_gpsimd(rest0)
         gate_by_gpsimd(second1, rest1)
+        take_bank([third1], "bank0")
+        packed_passes("q", third1)
 
-        for span in (third0, last0, last1):
+        for span in (third0, third1, last0, last1):
             packed_passes("v", span)
         gather_scales("k", "late_scales_k", (LATE, S))
         gather_words("k", "late_words_k", (LATE, S - P, S))
@@ -261,10 +268,12 @@ def tile_moe_qkb_kernel(
         for span in (third0, last0, last1):
             key_passes(span)
             gate_by_vector(span)
+        key_passes(third1)
+        gate_by_gpsimd(third1)
 
         for h in range(2):
             nc.vector.tensor_copy(out=picked[h][:], in_=dx[h][:].indirect(pos_sb[0][:]))
-        summed = [held(staged_name(second1), [P, T], F32), held("summed1", [P, T], F32)]
+        summed = [held(staged_name(third1), [P, T], F32), held("summed1", [P, T], F32)]
         for h, a, b in [(0, 0, T)] + [(1, a, b) for a, b in zip(TOKEN_CUTS[:-1], TOKEN_CUTS[1:])]:
             nc.vector.tensor_tensor(out=summed[h][:, a:b], in0=dx[h][:].indirect(entries(pos_sb[1], a, b)),
                                     in1=picked[h][:, a:b], op=ADD)

@@ -10,11 +10,11 @@ PER_COLUMN = 16
 PAIR = 2 * C
 FLOPS = 2 * 3 * S * N * K
 
-WHOLE_WINDOW = 2048
 LATE = S - 3 * P
+FILL_END = PAIR + 3 * P
+WHOLE_WINDOW = 2048
 EARLY_WINDOW = 1536
 SECOND_WINDOW = 896
-FILL_END = PAIR + 3 * P
 TOKEN_CUTS = (0, T // 2, T - P, T)
 
 F32 = mybir.dt.float32
@@ -61,13 +61,13 @@ def tile_moe_qkb_kernel(
         w4_words = {g: held("w4_words_" + g, [P, E, 2 * K], U8) for g in packed}
         w4_scales = {g: held("w4_scales_" + g, [P, E, K], U8) for g in packed}
 
-        early_blocks = [(e, 0) for e in range(4)]
-        late_blocks = [(e, h) for e in range(E) for h in range(2) if (e, h) not in early_blocks]
-        calls = (early_blocks, late_blocks)
-        wk_words = [held("wk_words%d" % i, [P, len(blocks), P], U32) for i, blocks in enumerate(calls)]
-        wk_scales = [held("wk_scales%d" % i, [P, len(blocks), P], U8) for i, blocks in enumerate(calls)]
-        wk_bf = [held("wk_bf%d" % i, [P, len(blocks), P, 4], BF16) for i, blocks in enumerate(calls)]
-        wk_place = {block: (call, i) for call, blocks in enumerate(calls) for i, block in enumerate(blocks)}
+        early_panels = [(e, h) for e in range(2) for h in range(2)]
+        late_panels = [(e, h) for e in range(E) for h in range(2) if (e, h) not in early_panels]
+        calls = (early_panels, late_panels)
+        wk_words = [held("wk_words%d" % i, [P, len(panels), P], U32) for i, panels in enumerate(calls)]
+        wk_scales = [held("wk_scales%d" % i, [P, len(panels), P], U8) for i, panels in enumerate(calls)]
+        wk_bf = [held("wk_bf%d" % i, [P, len(panels), P, 4], BF16) for i, panels in enumerate(calls)]
+        wk_place = {panel: (call, i) for call, panels in enumerate(calls) for i, panel in enumerate(panels)}
         wk_raw = [held("wk_raw%d" % e, [P, 4, K], F32) for e in range(E)]
         gate_sb = held("gate_sb", [P, S], F32)
         dx = [held("dx%d" % h, [P, S], F32) for h in range(2)]
@@ -99,7 +99,7 @@ def tile_moe_qkb_kernel(
         w4_scales_hbm = {"q": wq_scales, "v": wv_scales}
 
         def load_tok_scales(g, rs):
-            rows = tok_scales_hbm[g][0].rearrange("(q r) t -> r q t", r=4)
+            rows = tok_scales_hbm[g][0].rearrange("(m r) t -> r m t", r=4)
             for r in rs:
                 nc.sync.dma_start(out=tok_scales[g][r:P:32, :T].bitcast(I32), in_=rows[r].bitcast(I32))
 
@@ -108,7 +108,7 @@ def tile_moe_qkb_kernel(
                               in_=tok_words_hbm[g][0].rearrange("p t d -> p (t d)").bitcast(I32))
 
         def load_w4_scales(g, rs):
-            rows = w4_scales_hbm[g].rearrange("e s (q r) c -> r q (e s) c", r=4)
+            rows = w4_scales_hbm[g].rearrange("e s (m r) c -> r m (e s) c", r=4)
             for r in rs:
                 nc.sync.dma_start(out=w4_scales[g][r:P:32, :, :].bitcast(I32), in_=rows[r].bitcast(I32))
 
@@ -142,17 +142,17 @@ def tile_moe_qkb_kernel(
                 nc.vector.tensor_copy(out=tile[:, a - first : b - first], in_=window.indirect(entries(offs_sb, a, b)))
             return tile
 
-        def file_by_pair(views, g, tile, first, last):
+        def file_slots(places, g, tile, first, last):
             for a in range(first, last, P):
-                views[g, a // P] = (tile, first)
+                places[g, a // P] = (tile, first)
 
         def gather_words(g, name, bounds):
             tile = gather(tok_words[g][:].bitcast(U32), U32, name, bounds)
-            file_by_pair(slot_words, g, tile, bounds[0], bounds[-1])
+            file_slots(slot_words, g, tile, bounds[0], bounds[-1])
 
         def gather_scales(g, name, bounds):
             tile = gather(tok_scales[g][:], U8, name, bounds)
-            file_by_pair(slot_scales, g, tile, bounds[0], bounds[-1])
+            file_slots(slot_scales, g, tile, bounds[0], bounds[-1])
 
         def slot_operand(g, a, b):
             (words, first_word), (scales, first_scale) = slot_words[g, a // P], slot_scales[g, a // P]
@@ -229,10 +229,10 @@ def tile_moe_qkb_kernel(
             round_wk(e)
 
         slot_rows_q = gather(tok_scales["q"][:], U8, "slot_rows_q", (0, S))
-        for q in range(4):
-            nc.gpsimd.dma_start(out=slot_scales_q[32 * q : 32 * q + 4, :].bitcast(I32),
-                                in_=slot_rows_q[8 * q : 8 * q + 8 : 2, :].bitcast(I32))
-        file_by_pair(slot_scales, "q", slot_scales_q, 0, S)
+        for quadrant in range(4):
+            nc.gpsimd.dma_start(out=slot_scales_q[32 * quadrant : 32 * quadrant + 4, :].bitcast(I32),
+                                in_=slot_rows_q[8 * quadrant : 8 * quadrant + 8 : 2, :].bitcast(I32))
+        file_slots(slot_scales, "q", slot_scales_q, 0, S)
         gather_scales("v", "slot_scales_v", (0, S))
         gather_scales("k", "slot_scales_k", (0, LATE))
         for g in packed:
@@ -261,6 +261,7 @@ def tile_moe_qkb_kernel(
 
         for span in (third0, third1, last0, last1):
             packed_passes("v", span)
+
         gather_scales("k", "late_scales_k", (LATE, S))
         gather_words("k", "late_words_k", (LATE, S - P, S))
 

@@ -8,14 +8,14 @@ P = 128
 BLOCKS = N // 32
 PER_COLUMN = 16
 PAIR = 2 * C
+LATE = 2 * PAIR
 FLOPS = 2 * 3 * S * N * K
 
-LATE = S - 3 * P
-FILL_END = PAIR + 3 * P
 WHOLE_WINDOW = 2048
-EARLY_WINDOW = 1536
-SECOND_WINDOW = 896
-TOKEN_CUTS = (0, T // 2, T - P, T)
+EARLY_WINDOW = 1408
+HALF = T // 2
+FUSED_END = 256
+PLAIN_CUTS = (FUSED_END, 512, T)
 
 F32 = mybir.dt.float32
 BF16 = mybir.dt.bfloat16
@@ -27,6 +27,11 @@ FP8X4 = mybir.dt.float8_e4m3fn_x4
 FP4X4 = mybir.dt.float4_e2m1fn_x4
 MULT = mybir.AluOpType.mult
 ADD = mybir.AluOpType.add
+COPY = mybir.ActivationFunctionType.Copy
+
+
+def pieces(cuts):
+    return list(zip(cuts[:-1], cuts[1:]))
 
 
 def tile_moe_qkb_kernel(
@@ -40,7 +45,11 @@ def tile_moe_qkb_kernel(
         late = ctx.enter_context(tc.tile_pool(name="late", bufs=1))
         ps = ctx.enter_context(tc.psum_pool(name="ps", bufs=1))
 
-        late_offsets = {"wk_bf1": 0, "late_scales_k": 0, "late_words_k": PAIR}
+        words_bytes = 4 * PAIR
+        late_offsets = {
+            "wk_raw%d" % (E - 1): 0, "second_words_k": 0, "late_words_v": words_bytes,
+            "wk_bf1": 2 * words_bytes, "late_words_k": 2 * words_bytes, "late_scales_k": 3 * words_bytes,
+        }
 
         def held(name, shape, dtype):
             if name in late_offsets:
@@ -51,7 +60,7 @@ def tile_moe_qkb_kernel(
         pos_sb = [lists.tile([P, T // PER_COLUMN], U16, name="pos%d_sb" % r) for r in (1, 2)]
 
         packed = ("q", "v")
-        word_columns = {"q": WHOLE_WINDOW, "v": WHOLE_WINDOW, "k": SECOND_WINDOW}
+        word_columns = {"q": WHOLE_WINDOW, "v": EARLY_WINDOW, "k": T}
         scale_columns = {"q": WHOLE_WINDOW, "v": WHOLE_WINDOW, "k": EARLY_WINDOW}
         tok_words = {g: held("tok_words_" + g, [P, width], I32) for g, width in word_columns.items()}
         tok_scales = {g: held("tok_scales_" + g, [P, width], U8) for g, width in scale_columns.items()}
@@ -61,9 +70,7 @@ def tile_moe_qkb_kernel(
         w4_words = {g: held("w4_words_" + g, [P, E, 2 * K], U8) for g in packed}
         w4_scales = {g: held("w4_scales_" + g, [P, E, K], U8) for g in packed}
 
-        early_panels = [(e, h) for e in range(2) for h in range(2)]
-        late_panels = [(e, h) for e in range(E) for h in range(2) if (e, h) not in early_panels]
-        calls = (early_panels, late_panels)
+        calls = [[(e, h) for e in experts for h in range(2)] for experts in (range(4), range(4, E))]
         wk_words = [held("wk_words%d" % i, [P, len(panels), P], U32) for i, panels in enumerate(calls)]
         wk_scales = [held("wk_scales%d" % i, [P, len(panels), P], U8) for i, panels in enumerate(calls)]
         wk_bf = [held("wk_bf%d" % i, [P, len(panels), P, 4], BF16) for i, panels in enumerate(calls)]
@@ -73,25 +80,11 @@ def tile_moe_qkb_kernel(
         dx = [held("dx%d" % h, [P, S], F32) for h in range(2)]
         picked = [held("picked%d" % h, [P, T], F32) for h in range(2)]
 
-        first0, first1 = (0, 0, PAIR), (1, 0, PAIR)
-        second0, second1 = (0, PAIR, FILL_END), (1, PAIR, 2 * PAIR)
-        rest0, rest1 = (0, FILL_END, LATE), (1, 2 * PAIR, LATE)
-        third0, third1 = (0, LATE, S - P), (1, LATE, S - C)
-        last0, last1 = (0, S - P, S), (1, S - C, S)
-        groups = [[first0], [first1], [rest0, rest1], [second1], [second0], [third0], [last0], [last1]]
-        sums = {}
-
-        def take_bank(group, name):
-            bank = ps.tile([P, sum(b - a for h, a, b in group)], F32, name=name)
-            column = 0
-            for h, a, b in group:
-                sums[h, a, b] = bank[:, column : column + b - a]
-                column = column + b - a
-
-        for i, group in enumerate(groups):
-            take_bank(group, "bank%d" % i)
-        opens = [group[0] for group in groups] + [third1]
-        closes = [group[-1] for group in groups] + [third1]
+        first_spans = [(h, 0, PAIR) for h in range(2)]
+        second_spans = [(h, PAIR, LATE) for h in range(2)]
+        late_spans = [(0, LATE, S - P), (0, S - P, S), (1, LATE, S)]
+        spans = first_spans + second_spans + late_spans
+        sums = {span: ps.tile([P, span[2] - span[1]], F32, name="bank%d" % i) for i, span in enumerate(spans)}
 
         tok_words_hbm = {"q": dq_words, "k": dk_words, "v": dv_words}
         tok_scales_hbm = {"q": dq_scales, "k": dk_scales, "v": dv_scales}
@@ -135,10 +128,10 @@ def tile_moe_qkb_kernel(
         def entries(list_sb, a, b):
             return list_sb[:, a // PER_COLUMN : b // PER_COLUMN]
 
-        def gather(window, dtype, name, bounds):
-            first = bounds[0]
-            tile = held(name, [P, bounds[-1] - first], dtype)
-            for a, b in zip(bounds[:-1], bounds[1:]):
+        def gather(window, dtype, name, cuts):
+            first = cuts[0]
+            tile = held(name, [P, cuts[-1] - first], dtype)
+            for a, b in pieces(cuts):
                 nc.vector.tensor_copy(out=tile[:, a - first : b - first], in_=window.indirect(entries(offs_sb, a, b)))
             return tile
 
@@ -146,52 +139,41 @@ def tile_moe_qkb_kernel(
             for a in range(first, last, P):
                 places[g, a // P] = (tile, first)
 
-        def gather_words(g, name, bounds):
-            tile = gather(tok_words[g][:].bitcast(U32), U32, name, bounds)
-            file_slots(slot_words, g, tile, bounds[0], bounds[-1])
+        def gather_words(g, name, cuts):
+            file_slots(slot_words, g, gather(tok_words[g][:].bitcast(U32), U32, name, cuts), cuts[0], cuts[-1])
 
-        def gather_scales(g, name, bounds):
-            tile = gather(tok_scales[g][:], U8, name, bounds)
-            file_slots(slot_scales, g, tile, bounds[0], bounds[-1])
+        def gather_scales(g, name, cuts):
+            file_slots(slot_scales, g, gather(tok_scales[g][:], U8, name, cuts), cuts[0], cuts[-1])
 
-        def slot_operand(g, a, b):
-            (words, first_word), (scales, first_scale) = slot_words[g, a // P], slot_scales[g, a // P]
-            return words[:, a - first_word : b - first_word].bitcast(FP8X4), scales[:, a - first_scale : b - first_scale]
+        def weights(g, e, h):
+            if g in packed:
+                return w4_words[g][:, e, 2 * h * P : 2 * (h + 1) * P].bitcast(FP4X4), w4_scales[g][:, e, h * P : (h + 1) * P]
+            call, i = wk_place[e, h]
+            return wk_words[call][:, i].bitcast(FP8X4), wk_scales[call][:, i]
 
-        def packed_passes(g, span):
+        def passes(g, span):
             h, first, last = span
-            for a in range(first, last, P):
-                words, scales = slot_operand(g, a, a + P)
+            for a, b in pieces([first] + list(range((first // C + 1) * C, last, C)) + [last]):
+                (words, first_word), (scales, first_scale) = slot_words[g, a // P], slot_scales[g, a // P]
+                lhs, lhs_scale = weights(g, a // C, h)
                 nc.tensor.matmul_mx(
-                    out=sums[span][:, a - first : a - first + P],
-                    lhsT=w4_words[g][:, a // C, 2 * h * P : 2 * (h + 1) * P].bitcast(FP4X4),
-                    lhsT_scale=w4_scales[g][:, a // C, h * P : (h + 1) * P],
-                    rhs=words, rhs_scale=scales, start=(g == "q" and a == first and span in opens), stop=False)
-
-        def key_passes(span):
-            h, first, last = span
-            bounds = [first] + list(range((first // C + 1) * C, last, C)) + [last]
-            for a, b in zip(bounds[:-1], bounds[1:]):
-                call, i = wk_place[a // C, h]
-                words, scales = slot_operand("k", a, b)
-                nc.tensor.matmul_mx(
-                    out=sums[span][:, a - first : b - first],
-                    lhsT=wk_words[call][:, i].bitcast(FP8X4), lhsT_scale=wk_scales[call][:, i],
-                    rhs=words, rhs_scale=scales, start=False, stop=(b == last and span in closes))
+                    out=sums[span][:, a - first : b - first], lhsT=lhs, lhsT_scale=lhs_scale,
+                    rhs=words[:, a - first_word : b - first_word].bitcast(FP8X4),
+                    rhs_scale=scales[:, a - first_scale : b - first_scale],
+                    start=(g == "q" and a == first), stop=(g == "k" and b == last))
 
         def staged_name(span):
             return "staged%d_%d" % span[:2]
 
-        def gate_by_gpsimd(*parts):
-            h, first, last = parts[0][0], parts[0][1], parts[-1][2]
-            staged = held(staged_name(parts[0]), [P, last - first], F32)
-            for span in parts:
-                nc.scalar.copy(out=staged[:, span[1] - first : span[2] - first], in_=sums[span])
-            nc.gpsimd.tensor_tensor(out=dx[h][:, first:last], in0=staged[:], in1=gate_sb[:, first:last], op=MULT)
+        def gate_by_gpsimd(span):
+            h, a, b = span
+            staged = held(staged_name(span), [P, b - a], F32)
+            nc.scalar.copy(out=staged[:], in_=sums[span][:])
+            nc.gpsimd.tensor_tensor(out=dx[h][:, a:b], in0=staged[:], in1=gate_sb[:, a:b], op=MULT)
 
         def gate_by_vector(span):
             h, a, b = span
-            nc.vector.tensor_tensor(out=dx[h][:, a:b], in0=sums[span], in1=gate_sb[:, a:b], op=MULT)
+            nc.vector.tensor_tensor(out=dx[h][:, a:b], in0=sums[span][:], in1=gate_sb[:, a:b], op=MULT)
 
         for first, last in ((32, 64), (64, P)):
             nc.gpsimd.memset(tok_scales["q"][first:last, :T].bitcast(I32), 0)
@@ -233,49 +215,57 @@ def tile_moe_qkb_kernel(
             nc.gpsimd.dma_start(out=slot_scales_q[32 * quadrant : 32 * quadrant + 4, :].bitcast(I32),
                                 in_=slot_rows_q[8 * quadrant : 8 * quadrant + 8 : 2, :].bitcast(I32))
         file_slots(slot_scales, "q", slot_scales_q, 0, S)
+        gather_words("q", "slot_words_q", (0, S))
         gather_scales("v", "slot_scales_v", (0, S))
-        gather_scales("k", "slot_scales_k", (0, LATE))
-        for g in packed:
-            gather_words(g, "slot_words_" + g, (0, S))
+        gather_words("v", "early_words_v", (0, LATE))
+        gather_scales("k", "early_scales_k", (0, LATE))
         quantize_wk(0)
-        gather_words("k", "slot_words_k", (0, PAIR))
-        for group in groups:
-            for span in group:
-                packed_passes("q", span)
-
+        gather_words("k", "wk_raw3", (0, PAIR))
         quantize_wk(1)
-        gather_words("k", "wk_raw%d" % (E - 1), (PAIR, LATE))
-        for span in (first0, first1):
-            packed_passes("v", span)
-        for span in (first0, first1):
-            key_passes(span)
-            gate_by_gpsimd(span)
-        for span in (rest0, rest1, second1, second0):
-            packed_passes("v", span)
-        for span in (rest0, rest1, second1, second0):
-            key_passes(span)
-        gate_by_gpsimd(rest0)
-        gate_by_gpsimd(second1, rest1)
-        take_bank([third1], "bank0")
-        packed_passes("q", third1)
-
-        for span in (third0, third1, last0, last1):
-            packed_passes("v", span)
-
+        gather_words("k", "second_words_k", (PAIR, LATE))
+        gather_words("v", "late_words_v", (LATE, S))
         gather_scales("k", "late_scales_k", (LATE, S))
         gather_words("k", "late_words_k", (LATE, S - P, S))
 
-        gate_by_vector(second0)
-        for span in (third0, last0, last1):
-            key_passes(span)
+        for run in (first_spans, second_spans):
+            for g in packed:
+                for span in run:
+                    passes(g, span)
+        for span in late_spans:
+            passes("q", span)
+        for span in first_spans + second_spans:
+            passes("k", span)
+            gate_by_gpsimd(span)
+        for span in late_spans:
+            passes("v", span)
+        for span in late_spans:
+            passes("k", span)
             gate_by_vector(span)
-        key_passes(third1)
-        gate_by_gpsimd(third1)
 
-        for h in range(2):
-            nc.vector.tensor_copy(out=picked[h][:], in_=dx[h][:].indirect(pos_sb[0][:]))
-        summed = [held(staged_name(third1), [P, T], F32), held("summed1", [P, T], F32)]
-        for h, a, b in [(0, 0, T)] + [(1, a, b) for a, b in zip(TOKEN_CUTS[:-1], TOKEN_CUTS[1:])]:
+        summed = [held(staged_name(second_spans[-1]), [P, T], F32), held("summed1", [P, T], F32)]
+        other = held("other", [P, T - FUSED_END], F32)
+
+        def pick_on_scalar(tile, h, r, a, b):
+            nc.scalar.activation(out=tile, in_=dx[h][:].indirect(entries(pos_sb[r], a, b)), func=COPY)
+
+        def pick_and_add(h, a, b):
             nc.vector.tensor_tensor(out=summed[h][:, a:b], in0=dx[h][:].indirect(entries(pos_sb[1], a, b)),
                                     in1=picked[h][:, a:b], op=ADD)
+
+        def store(h, a, b):
             nc.sync.dma_start(out=out[h * P : (h + 1) * P, a:b], in_=summed[h][:, a:b])
+
+        pick_on_scalar(picked[0][:, :HALF], 0, 0, 0, HALF)
+        nc.vector.tensor_copy(out=picked[0][:, HALF:], in_=dx[0][:].indirect(entries(pos_sb[0], HALF, T)))
+        pick_on_scalar(picked[1][:], 1, 0, 0, T)
+        for a, b in pieces(PLAIN_CUTS):
+            pick_on_scalar(other[:, a - FUSED_END : b - FUSED_END], 1, 1, a, b)
+        pick_and_add(0, 0, HALF)
+        pick_and_add(0, HALF, T)
+        store(0, 0, T)
+        pick_and_add(1, 0, FUSED_END)
+        store(1, 0, FUSED_END)
+        for a, b in pieces(PLAIN_CUTS):
+            nc.vector.tensor_tensor(out=summed[1][:, a:b], in0=other[:, a - FUSED_END : b - FUSED_END],
+                                    in1=picked[1][:, a:b], op=ADD)
+            store(1, a, b)

@@ -8,14 +8,15 @@ P = 128
 BLOCKS = N // 32
 PER_COLUMN = 16
 PAIR = 2 * C
-LATE = 2 * PAIR
+LATE = S - 3 * P
 FLOPS = 2 * 3 * S * N * K
 
 WHOLE_WINDOW = 2048
-EARLY_WINDOW = 1408
+SECOND_WINDOW = 896
+EARLY_WINDOW = 1536
 HALF = T // 2
-FUSED_END = 256
-PLAIN_CUTS = (FUSED_END, 512, T)
+FUSED_END = 320
+PLAIN_CUTS = (FUSED_END, T - P, T)
 
 F32 = mybir.dt.float32
 BF16 = mybir.dt.bfloat16
@@ -45,10 +46,10 @@ def tile_moe_qkb_kernel(
         late = ctx.enter_context(tc.tile_pool(name="late", bufs=1))
         ps = ctx.enter_context(tc.psum_pool(name="ps", bufs=1))
 
-        words_bytes = 4 * PAIR
+        raw_bytes = 4 * 4 * K
         late_offsets = {
-            "wk_raw%d" % (E - 1): 0, "second_words_k": 0, "late_words_v": words_bytes,
-            "wk_bf1": 2 * words_bytes, "late_words_k": 2 * words_bytes, "late_scales_k": 3 * words_bytes,
+            "wk_raw%d" % (E - 1): 0, "second_words_k": 0, "late_words_v": 4 * (LATE - PAIR),
+            "wk_bf1": raw_bytes, "late_words_k": raw_bytes, "late_scales_k": raw_bytes + 4 * (S - LATE),
         }
 
         def held(name, shape, dtype):
@@ -60,7 +61,7 @@ def tile_moe_qkb_kernel(
         pos_sb = [lists.tile([P, T // PER_COLUMN], U16, name="pos%d_sb" % r) for r in (1, 2)]
 
         packed = ("q", "v")
-        word_columns = {"q": WHOLE_WINDOW, "v": EARLY_WINDOW, "k": T}
+        word_columns = {"q": WHOLE_WINDOW, "v": EARLY_WINDOW, "k": SECOND_WINDOW}
         scale_columns = {"q": WHOLE_WINDOW, "v": WHOLE_WINDOW, "k": EARLY_WINDOW}
         tok_words = {g: held("tok_words_" + g, [P, width], I32) for g, width in word_columns.items()}
         tok_scales = {g: held("tok_scales_" + g, [P, width], U8) for g, width in scale_columns.items()}
@@ -81,8 +82,8 @@ def tile_moe_qkb_kernel(
         picked = [held("picked%d" % h, [P, T], F32) for h in range(2)]
 
         first_spans = [(h, 0, PAIR) for h in range(2)]
-        second_spans = [(h, PAIR, LATE) for h in range(2)]
-        late_spans = [(0, LATE, S - P), (0, S - P, S), (1, LATE, S)]
+        second_spans = [(0, PAIR, LATE - C), (0, LATE - C, LATE), (1, PAIR, 2 * PAIR)]
+        late_spans = [(0, LATE, S - P), (0, S - P, S), (1, 2 * PAIR, S)]
         spans = first_spans + second_spans + late_spans
         sums = {span: ps.tile([P, span[2] - span[1]], F32, name="bank%d" % i) for i, span in enumerate(spans)}
 
@@ -153,22 +154,25 @@ def tile_moe_qkb_kernel(
 
         def passes(g, span):
             h, first, last = span
-            for a, b in pieces([first] + list(range((first // C + 1) * C, last, C)) + [last]):
+            opener = "v" if span in late_spans else "q"
+            borders = set(range(0, S, C)) | {LATE}
+            for a, b in pieces([first] + sorted(x for x in borders if first < x < last) + [last]):
                 (words, first_word), (scales, first_scale) = slot_words[g, a // P], slot_scales[g, a // P]
                 lhs, lhs_scale = weights(g, a // C, h)
                 nc.tensor.matmul_mx(
                     out=sums[span][:, a - first : b - first], lhsT=lhs, lhsT_scale=lhs_scale,
                     rhs=words[:, a - first_word : b - first_word].bitcast(FP8X4),
                     rhs_scale=scales[:, a - first_scale : b - first_scale],
-                    start=(g == "q" and a == first), stop=(g == "k" and b == last))
+                    start=(g == opener and a == first), stop=(g == "k" and b == last))
 
         def staged_name(span):
             return "staged%d_%d" % span[:2]
 
-        def gate_by_gpsimd(span):
-            h, a, b = span
-            staged = held(staged_name(span), [P, b - a], F32)
-            nc.scalar.copy(out=staged[:], in_=sums[span][:])
+        def gate_by_gpsimd(*parts):
+            h, a, b = parts[0][0], parts[0][1], parts[-1][2]
+            staged = held(staged_name(parts[0]), [P, b - a], F32)
+            for span in parts:
+                nc.scalar.copy(out=staged[:, span[1] - a : span[2] - a], in_=sums[span][:])
             nc.gpsimd.tensor_tensor(out=dx[h][:, a:b], in0=staged[:], in1=gate_sb[:, a:b], op=MULT)
 
         def gate_by_vector(span):
@@ -231,13 +235,17 @@ def tile_moe_qkb_kernel(
             for g in packed:
                 for span in run:
                     passes(g, span)
-        for span in late_spans:
-            passes("q", span)
-        for span in first_spans + second_spans:
+        for span in first_spans:
             passes("k", span)
             gate_by_gpsimd(span)
-        for span in late_spans:
-            passes("v", span)
+        for span in second_spans:
+            passes("k", span)
+        gate_by_gpsimd(second_spans[0])
+        gate_by_gpsimd(second_spans[2])
+        for g in ("v", "q"):
+            for span in late_spans:
+                passes(g, span)
+        gate_by_vector(second_spans[1])
         for span in late_spans:
             passes("k", span)
             gate_by_vector(span)
@@ -260,9 +268,9 @@ def tile_moe_qkb_kernel(
         pick_on_scalar(picked[1][:], 1, 0, 0, T)
         for a, b in pieces(PLAIN_CUTS):
             pick_on_scalar(other[:, a - FUSED_END : b - FUSED_END], 1, 1, a, b)
-        pick_and_add(0, 0, HALF)
-        pick_and_add(0, HALF, T)
-        store(0, 0, T)
+        for a, b in pieces((0, HALF, T)):
+            pick_and_add(0, a, b)
+            store(0, a, b)
         pick_and_add(1, 0, FUSED_END)
         store(1, 0, FUSED_END)
         for a, b in pieces(PLAIN_CUTS):

@@ -180,16 +180,13 @@ def tile_moe_qkb_kernel(
             nc.vector.tensor_tensor(out=dx[h][:, a:b], in0=sums[span][:], in1=gate_sb[:, a:b], op=MULT)
 
         for first, last in ((32, 64), (64, P)):
-            nc.gpsimd.memset(tok_scales["q"][first:last, :T].bitcast(I32), 0)
+            nc.vector.memset(tok_scales["q"][first:last, :T].bitcast(I32), 0)
         for g in ("v", "k"):
             nc.vector.memset(tok_scales[g][:, :T].bitcast(I32), 0)
-        for g in packed:
-            nc.vector.memset(w4_scales[g][:].bitcast(I32), 0)
-        nc.vector.memset(slot_scales_q[:].bitcast(I32), 0)
 
-        nc.sync.dma_start(out=offs_sb[:], in_=offs)
         nc.sync.dma_start(out=tok_scales["q"][: 2 * BLOCKS, :T].bitcast(I32),
                           in_=dq_scales[0].bitcast(I32).unsqueeze(1).to_broadcast([BLOCKS, 2, T // 4]))
+        nc.sync.dma_start(out=offs_sb[:], in_=offs)
         load_tok_words("q")
         load_tok_scales("v", range(4))
         load_tok_words("v")

@@ -14,7 +14,7 @@ FLOPS = 2 * 3 * S * N * K
 WHOLE_WINDOW = 2048
 SECOND_WINDOW = 896
 EARLY_WINDOW = 1536
-HALF = T // 2
+HALF = 320
 FUSED_END = 320
 PLAIN_CUTS = (FUSED_END, T - P, T)
 
@@ -82,10 +82,18 @@ def tile_moe_qkb_kernel(
         picked = [held("picked%d" % h, [P, T], F32) for h in range(2)]
 
         first_spans = [(h, 0, PAIR) for h in range(2)]
-        second_spans = [(0, PAIR, LATE - C), (0, LATE - C, LATE), (1, PAIR, 2 * PAIR)]
-        late_spans = [(0, LATE, S - P), (0, S - P, S), (1, 2 * PAIR, S)]
-        spans = first_spans + second_spans + late_spans
-        sums = {span: ps.tile([P, span[2] - span[1]], F32, name="bank%d" % i) for i, span in enumerate(spans)}
+        second_spans = [(0, PAIR, LATE - C), (1, PAIR, 2 * PAIR), (0, LATE - C, LATE), (1, 2 * PAIR, LATE)]
+        late_spans = [(0, LATE, S - P), (0, S - P, S), (1, LATE, S)]
+        groups = [[span] for span in first_spans + second_spans[:3] + late_spans[0::2]] + [[second_spans[3], late_spans[1]]]
+        sums = {}
+        for i, group in enumerate(groups):
+            bank = ps.tile([P, sum(b - a for h, a, b in group)], F32, name="bank%d" % i)
+            column = 0
+            for h, a, b in group:
+                sums[h, a, b] = bank[:, column : column + b - a]
+                column = column + b - a
+        opens = [group[0] for group in groups]
+        closes = [group[-1] for group in groups]
 
         tok_words_hbm = {"q": dq_words, "k": dk_words, "v": dv_words}
         tok_scales_hbm = {"q": dq_scales, "k": dk_scales, "v": dv_scales}
@@ -154,8 +162,7 @@ def tile_moe_qkb_kernel(
 
         def passes(g, span):
             h, first, last = span
-            opener = "v" if span in late_spans else "q"
-            borders = set(range(0, S, C)) | {LATE}
+            borders = set(range(0, S, C)) | (set() if g == "q" else {LATE})
             for a, b in pieces([first] + sorted(x for x in borders if first < x < last) + [last]):
                 (words, first_word), (scales, first_scale) = slot_words[g, a // P], slot_scales[g, a // P]
                 lhs, lhs_scale = weights(g, a // C, h)
@@ -163,7 +170,8 @@ def tile_moe_qkb_kernel(
                     out=sums[span][:, a - first : b - first], lhsT=lhs, lhsT_scale=lhs_scale,
                     rhs=words[:, a - first_word : b - first_word].bitcast(FP8X4),
                     rhs_scale=scales[:, a - first_scale : b - first_scale],
-                    start=(g == opener and a == first), stop=(g == "k" and b == last))
+                    start=(g == "q" and a == first and span in opens),
+                    stop=(g == "k" and b == last and span in closes))
 
         def staged_name(span):
             return "staged%d_%d" % span[:2]
@@ -172,12 +180,12 @@ def tile_moe_qkb_kernel(
             h, a, b = parts[0][0], parts[0][1], parts[-1][2]
             staged = held(staged_name(parts[0]), [P, b - a], F32)
             for span in parts:
-                nc.scalar.copy(out=staged[:, span[1] - a : span[2] - a], in_=sums[span][:])
+                nc.scalar.copy(out=staged[:, span[1] - a : span[2] - a], in_=sums[span])
             nc.gpsimd.tensor_tensor(out=dx[h][:, a:b], in0=staged[:], in1=gate_sb[:, a:b], op=MULT)
 
         def gate_by_vector(span):
             h, a, b = span
-            nc.vector.tensor_tensor(out=dx[h][:, a:b], in0=sums[span][:], in1=gate_sb[:, a:b], op=MULT)
+            nc.vector.tensor_tensor(out=dx[h][:, a:b], in0=sums[span], in1=gate_sb[:, a:b], op=MULT)
 
         for first, last in ((32, 64), (64, P)):
             nc.vector.memset(tok_scales["q"][first:last, :T].bitcast(I32), 0)
@@ -235,19 +243,20 @@ def tile_moe_qkb_kernel(
         for span in first_spans:
             passes("k", span)
             gate_by_gpsimd(span)
+        for span in late_spans:
+            passes("q", span)
         for span in second_spans:
             passes("k", span)
         gate_by_gpsimd(second_spans[0])
-        gate_by_gpsimd(second_spans[2])
-        for g in ("v", "q"):
-            for span in late_spans:
-                passes(g, span)
-        gate_by_vector(second_spans[1])
+        gate_by_gpsimd(second_spans[1])
+        for span in late_spans:
+            passes("v", span)
         for span in late_spans:
             passes("k", span)
+        for span in (second_spans[2], late_spans[0], late_spans[1], second_spans[3], late_spans[2]):
             gate_by_vector(span)
 
-        summed = [held(staged_name(second_spans[-1]), [P, T], F32), held("summed1", [P, T], F32)]
+        summed = [held(staged_name(second_spans[1]), [P, T], F32), held("summed1", [P, T], F32)]
         other = held("other", [P, T - FUSED_END], F32)
 
         def pick_on_scalar(tile, h, r, a, b):

@@ -14,9 +14,9 @@ FLOPS = 2 * 3 * S * N * K
 WHOLE_WINDOW = 2048
 SECOND_WINDOW = 896
 EARLY_WINDOW = 1536
-HALF = 320
-FUSED_END = 320
-PLAIN_CUTS = (FUSED_END, T - P, T)
+HALF = 288
+FUSED_END = 288
+PLAIN_CUTS = (FUSED_END, 576, T)
 
 F32 = mybir.dt.float32
 BF16 = mybir.dt.bfloat16
@@ -71,7 +71,7 @@ def tile_moe_qkb_kernel(
         w4_words = {g: held("w4_words_" + g, [P, E, 2 * K], U8) for g in packed}
         w4_scales = {g: held("w4_scales_" + g, [P, E, K], U8) for g in packed}
 
-        calls = [[(e, h) for e in experts for h in range(2)] for experts in (range(4), range(4, E))]
+        calls = [[(e, h) for e in experts for h in range(2)] for experts in (range(2), range(2, E))]
         wk_words = [held("wk_words%d" % i, [P, len(panels), P], U32) for i, panels in enumerate(calls)]
         wk_scales = [held("wk_scales%d" % i, [P, len(panels), P], U8) for i, panels in enumerate(calls)]
         wk_bf = [held("wk_bf%d" % i, [P, len(panels), P, 4], BF16) for i, panels in enumerate(calls)]
@@ -83,8 +83,9 @@ def tile_moe_qkb_kernel(
 
         first_spans = [(h, 0, PAIR) for h in range(2)]
         second_spans = [(0, PAIR, LATE - C), (1, PAIR, 2 * PAIR), (0, LATE - C, LATE), (1, 2 * PAIR, LATE)]
-        late_spans = [(0, LATE, S - P), (0, S - P, S), (1, LATE, S)]
-        groups = [[span] for span in first_spans + second_spans[:3] + late_spans[0::2]] + [[second_spans[3], late_spans[1]]]
+        late_spans = [(0, LATE, S - P), (1, LATE, S - P), (0, S - P, S), (1, S - P, S)]
+        groups = [[span] for span in first_spans + second_spans[1:3] + late_spans[0::3]]
+        groups = groups + [second_spans[0::3], late_spans[1:3]]
         sums = {}
         for i, group in enumerate(groups):
             bank = ps.tile([P, sum(b - a for h, a, b in group)], F32, name="bank%d" % i)
@@ -229,31 +230,34 @@ def tile_moe_qkb_kernel(
         gather_words("v", "early_words_v", (0, LATE))
         gather_scales("k", "early_scales_k", (0, LATE))
         quantize_wk(0)
-        gather_words("k", "wk_raw3", (0, PAIR))
+        gather_words("k", "wk_raw1", (0, PAIR))
         quantize_wk(1)
         gather_words("k", "second_words_k", (PAIR, LATE))
         gather_words("v", "late_words_v", (LATE, S))
         gather_scales("k", "late_scales_k", (LATE, S))
         gather_words("k", "late_words_k", (LATE, S - P, S))
 
-        for run in (first_spans, second_spans):
-            for g in packed:
-                for span in run:
-                    passes(g, span)
+        for g in packed:
+            for span in first_spans:
+                passes(g, span)
+        for span in second_spans:
+            passes("q", span)
         for span in first_spans:
             passes("k", span)
             gate_by_gpsimd(span)
+        for span in second_spans:
+            passes("v", span)
         for span in late_spans:
             passes("q", span)
-        for span in second_spans:
+        for span in second_spans[0::3] + second_spans[1:3]:
             passes("k", span)
         gate_by_gpsimd(second_spans[0])
-        gate_by_gpsimd(second_spans[1])
+        gate_by_gpsimd(second_spans[1], second_spans[3])
         for span in late_spans:
             passes("v", span)
         for span in late_spans:
             passes("k", span)
-        for span in (second_spans[2], late_spans[0], late_spans[1], second_spans[3], late_spans[2]):
+        for span in (second_spans[2], late_spans[0], late_spans[2], late_spans[1], late_spans[3]):
             gate_by_vector(span)
 
         summed = [held(staged_name(second_spans[1]), [P, T], F32), held("summed1", [P, T], F32)]

@@ -1,20 +1,25 @@
 from contextlib import ExitStack
 
 import concourse.mybir as mybir
+from concourse.masks import make_identity
 
 K, T, E, C, N = 256, 768, 6, 256, 512
 S = E * C
 P = 128
 BLOCKS = N // 32
 PER_COLUMN = 16
-PAIR = 2 * C
-LATE = S - 3 * P
 FLOPS = 2 * 3 * S * N * K
 
+FIRST = 2 * C
+LATE = S - 3 * P
+TURNED = LATE - P
+FILLER = LATE - 3 * P
+LAST = S - P
+
 WHOLE_WINDOW = 2048
-SECOND_WINDOW = 896
 EARLY_WINDOW = 1536
-HALF = 288
+RUN_WINDOW = 896
+SCALAR_FIRST = 288
 FUSED_END = 288
 PLAIN_CUTS = (FUSED_END, 576, T)
 
@@ -43,25 +48,25 @@ def tile_moe_qkb_kernel(
     with ExitStack() as ctx:
         lists = ctx.enter_context(tc.tile_pool(name="lists", bufs=1))
         sb = ctx.enter_context(tc.tile_pool(name="sb", bufs=1))
-        late = ctx.enter_context(tc.tile_pool(name="late", bufs=1))
+        shared = ctx.enter_context(tc.tile_pool(name="shared", bufs=1))
         ps = ctx.enter_context(tc.psum_pool(name="ps", bufs=1))
 
         raw_bytes = 4 * 4 * K
-        late_offsets = {
-            "wk_raw%d" % (E - 1): 0, "second_words_k": 0, "late_words_v": 4 * (LATE - PAIR),
+        shared_offsets = {
+            "wk_raw%d" % (E - 1): 0, "second_words_k": 0,
             "wk_bf1": raw_bytes, "late_words_k": raw_bytes, "late_scales_k": raw_bytes + 4 * (S - LATE),
         }
 
         def held(name, shape, dtype):
-            if name in late_offsets:
-                return late.tile(shape, dtype, name=name, align_bytes=64, offset=late_offsets[name])
+            if name in shared_offsets:
+                return shared.tile(shape, dtype, name=name, align_bytes=64, offset=shared_offsets[name])
             return sb.tile(shape, dtype, name=name, align_bytes=64)
 
         offs_sb = lists.tile([P, S // PER_COLUMN], U16, name="offs_sb")
         pos_sb = [lists.tile([P, T // PER_COLUMN], U16, name="pos%d_sb" % r) for r in (1, 2)]
 
         packed = ("q", "v")
-        word_columns = {"q": WHOLE_WINDOW, "v": EARLY_WINDOW, "k": SECOND_WINDOW}
+        word_columns = {"q": WHOLE_WINDOW, "v": WHOLE_WINDOW, "k": RUN_WINDOW}
         scale_columns = {"q": WHOLE_WINDOW, "v": WHOLE_WINDOW, "k": EARLY_WINDOW}
         tok_words = {g: held("tok_words_" + g, [P, width], I32) for g, width in word_columns.items()}
         tok_scales = {g: held("tok_scales_" + g, [P, width], U8) for g, width in scale_columns.items()}
@@ -78,14 +83,19 @@ def tile_moe_qkb_kernel(
         wk_place = {panel: (call, i) for call, panels in enumerate(calls) for i, panel in enumerate(panels)}
         wk_raw = [held("wk_raw%d" % e, [P, 4, K], F32) for e in range(E)]
         gate_sb = held("gate_sb", [P, S], F32)
+        turned_blocks = list(range(TURNED, LATE, P))
+        gate_columns = held("gate_columns", [P, len(turned_blocks)], F32)
+        identity = held("identity", [P, P], F32)
         dx = [held("dx%d" % h, [P, S], F32) for h in range(2)]
         picked = [held("picked%d" % h, [P, T], F32) for h in range(2)]
 
-        first_spans = [(h, 0, PAIR) for h in range(2)]
-        second_spans = [(0, PAIR, LATE - C), (1, PAIR, 2 * PAIR), (0, LATE - C, LATE), (1, 2 * PAIR, LATE)]
-        late_spans = [(0, LATE, S - P), (1, LATE, S - P), (0, S - P, S), (1, S - P, S)]
-        groups = [[span] for span in first_spans + second_spans[1:3] + late_spans[0::3]]
-        groups = groups + [second_spans[0::3], late_spans[1:3]]
+        first_spans = [(h, 0, FIRST) for h in range(2)]
+        second_spans = [(0, FIRST, FILLER), (1, FIRST, TURNED)]
+        filler_span = (0, FILLER, LATE)
+        turned_spans = [(1, a, a + P) for a in turned_blocks]
+        late_spans = [(0, LATE, LAST), (1, LATE, LAST), (0, LAST, S), (1, LAST, S)]
+        groups = [[span] for span in first_spans + second_spans[1:] + late_spans[0::3]]
+        groups = groups + [turned_spans + second_spans[:1], late_spans[1:3], [filler_span]]
         sums = {}
         for i, group in enumerate(groups):
             bank = ps.tile([P, sum(b - a for h, a, b in group)], F32, name="bank%d" % i)
@@ -163,26 +173,29 @@ def tile_moe_qkb_kernel(
 
         def passes(g, span):
             h, first, last = span
-            borders = set(range(0, S, C)) | (set() if g == "q" else {LATE})
-            for a, b in pieces([first] + sorted(x for x in borders if first < x < last) + [last]):
+            for a, b in pieces([first] + [x for x in range(0, S, C) if first < x < last] + [last]):
                 (words, first_word), (scales, first_scale) = slot_words[g, a // P], slot_scales[g, a // P]
-                lhs, lhs_scale = weights(g, a // C, h)
+                tokens = (words[:, a - first_word : b - first_word].bitcast(FP8X4),
+                          scales[:, a - first_scale : b - first_scale])
+                matrix = weights(g, a // C, h)
+                still, moving = (tokens, matrix) if span in turned_spans else (matrix, tokens)
                 nc.tensor.matmul_mx(
-                    out=sums[span][:, a - first : b - first], lhsT=lhs, lhsT_scale=lhs_scale,
-                    rhs=words[:, a - first_word : b - first_word].bitcast(FP8X4),
-                    rhs_scale=scales[:, a - first_scale : b - first_scale],
+                    out=sums[span][:, a - first : b - first], lhsT=still[0], lhsT_scale=still[1],
+                    rhs=moving[0], rhs_scale=moving[1],
                     start=(g == "q" and a == first and span in opens),
                     stop=(g == "k" and b == last and span in closes))
 
         def staged_name(span):
             return "staged%d_%d" % span[:2]
 
-        def gate_by_gpsimd(*parts):
-            h, a, b = parts[0][0], parts[0][1], parts[-1][2]
-            staged = held(staged_name(parts[0]), [P, b - a], F32)
-            for span in parts:
-                nc.scalar.copy(out=staged[:, span[1] - a : span[2] - a], in_=sums[span])
-            nc.gpsimd.tensor_tensor(out=dx[h][:, a:b], in0=staged[:], in1=gate_sb[:, a:b], op=MULT)
+        def stage(span):
+            staged = held(staged_name(span), [P, span[2] - span[1]], F32)
+            nc.scalar.copy(out=staged[:], in_=sums[span])
+            return staged
+
+        def gate_by_gpsimd(span):
+            h, a, b = span
+            nc.gpsimd.tensor_tensor(out=dx[h][:, a:b], in0=stage(span)[:], in1=gate_sb[:, a:b], op=MULT)
 
         def gate_by_vector(span):
             h, a, b = span
@@ -192,6 +205,7 @@ def tile_moe_qkb_kernel(
             nc.vector.memset(tok_scales["q"][first:last, :T].bitcast(I32), 0)
         for g in ("v", "k"):
             nc.vector.memset(tok_scales[g][:, :T].bitcast(I32), 0)
+        make_identity(nc, identity[:])
 
         nc.sync.dma_start(out=tok_scales["q"][: 2 * BLOCKS, :T].bitcast(I32),
                           in_=dq_scales[0].bitcast(I32).unsqueeze(1).to_broadcast([BLOCKS, 2, T // 4]))
@@ -216,6 +230,8 @@ def tile_moe_qkb_kernel(
         nc.sync.dma_start(out=gate_sb[:], in_=gate)
         nc.sync.dma_start(out=pos_sb[0][:], in_=pos1)
         nc.sync.dma_start(out=pos_sb[1][:], in_=pos2)
+        with nc.allow_non_contiguous_dma(reason="one weight a partition"):
+            nc.sync.dma_start(out=gate_columns[:], in_=gate[0, TURNED:LATE].rearrange("(b p) -> p b", p=P))
 
         for e in range(E):
             round_wk(e)
@@ -227,40 +243,46 @@ def tile_moe_qkb_kernel(
         file_slots(slot_scales, "q", slot_scales_q, 0, S)
         gather_words("q", "slot_words_q", (0, S))
         gather_scales("v", "slot_scales_v", (0, S))
-        gather_words("v", "early_words_v", (0, LATE))
+        gather_words("v", "slot_words_v", (0, S))
         gather_scales("k", "early_scales_k", (0, LATE))
         quantize_wk(0)
-        gather_words("k", "wk_raw1", (0, PAIR))
+        gather_words("k", "wk_raw1", (0, FIRST))
         quantize_wk(1)
-        gather_words("k", "second_words_k", (PAIR, LATE))
-        gather_words("v", "late_words_v", (LATE, S))
+        gather_words("k", "second_words_k", (FIRST, LATE))
         gather_scales("k", "late_scales_k", (LATE, S))
-        gather_words("k", "late_words_k", (LATE, S - P, S))
+        gather_words("k", "late_words_k", (LATE, LAST, S))
 
+        middle_spans = turned_spans + second_spans + [filler_span]
         for g in packed:
             for span in first_spans:
                 passes(g, span)
-        for span in second_spans:
+        for span in middle_spans:
             passes("q", span)
         for span in first_spans:
             passes("k", span)
             gate_by_gpsimd(span)
-        for span in second_spans:
+        for span in middle_spans:
             passes("v", span)
-        for span in late_spans:
-            passes("q", span)
-        for span in second_spans[0::3] + second_spans[1:3]:
+        for g in packed:
+            for span in late_spans:
+                passes(g, span)
+        for span in middle_spans:
             passes("k", span)
+        gated = held("gated", [P, len(turned_spans), P], F32)
+        for i, span in enumerate(turned_spans):
+            nc.scalar.activation(out=gated[:, i], in_=sums[span], func=COPY, scale=gate_columns[:, i : i + 1])
         gate_by_gpsimd(second_spans[0])
-        gate_by_gpsimd(second_spans[1], second_spans[3])
-        for span in late_spans:
-            passes("v", span)
+        gate_by_gpsimd(second_spans[1])
         for span in late_spans:
             passes("k", span)
-        for span in (second_spans[2], late_spans[0], late_spans[2], late_spans[1], late_spans[3]):
+        turned_back = ps.tile([P, len(turned_spans), P], F32, name="bank0")
+        for i in range(len(turned_spans)):
+            nc.tensor.transpose(turned_back[:, i], gated[:, i], identity[:])
+        nc.scalar.copy(out=dx[1][:, TURNED:LATE], in_=turned_back[:].rearrange("p b s -> p (b s)"))
+        for span in (filler_span, late_spans[0], late_spans[2], late_spans[1], late_spans[3]):
             gate_by_vector(span)
 
-        summed = [held(staged_name(second_spans[1]), [P, T], F32), held("summed1", [P, T], F32)]
+        summed = [held("summed%d" % h, [P, T], F32) for h in range(2)]
         other = held("other", [P, T - FUSED_END], F32)
 
         def pick_on_scalar(tile, h, r, a, b):
@@ -273,12 +295,12 @@ def tile_moe_qkb_kernel(
         def store(h, a, b):
             nc.sync.dma_start(out=out[h * P : (h + 1) * P, a:b], in_=summed[h][:, a:b])
 
-        pick_on_scalar(picked[0][:, :HALF], 0, 0, 0, HALF)
-        nc.vector.tensor_copy(out=picked[0][:, HALF:], in_=dx[0][:].indirect(entries(pos_sb[0], HALF, T)))
+        pick_on_scalar(picked[0][:, :SCALAR_FIRST], 0, 0, 0, SCALAR_FIRST)
+        nc.vector.tensor_copy(out=picked[0][:, SCALAR_FIRST:], in_=dx[0][:].indirect(entries(pos_sb[0], SCALAR_FIRST, T)))
         pick_on_scalar(picked[1][:], 1, 0, 0, T)
         for a, b in pieces(PLAIN_CUTS):
             pick_on_scalar(other[:, a - FUSED_END : b - FUSED_END], 1, 1, a, b)
-        for a, b in pieces((0, HALF, T)):
+        for a, b in pieces((0, SCALAR_FIRST, T)):
             pick_and_add(0, a, b)
             store(0, a, b)
         pick_and_add(1, 0, FUSED_END)

@@ -273,11 +273,12 @@ def tile_moe_qkb_kernel(
             nc.scalar.activation(out=gated[:, i], in_=sums[span], func=COPY, scale=gate_columns[:, i : i + 1])
         gate_by_gpsimd(second_spans[0])
         gate_by_gpsimd(second_spans[1])
-        for span in late_spans:
+        for span in late_spans[:3]:
             passes("k", span)
         turned_back = ps.tile([P, len(turned_spans), P], F32, name="bank0")
         for i in range(len(turned_spans)):
             nc.tensor.transpose(turned_back[:, i], gated[:, i], identity[:])
+        passes("k", late_spans[3])
         nc.scalar.copy(out=dx[1][:, TURNED:LATE], in_=turned_back[:].rearrange("p b s -> p (b s)"))
         for span in (filler_span, late_spans[0], late_spans[2], late_spans[1], late_spans[3]):
             gate_by_vector(span)

@@ -81,7 +81,8 @@ def tile_moe_qkb_kernel(
         wk_scales = [held("wk_scales%d" % i, [P, len(panels), P], U8) for i, panels in enumerate(calls)]
         wk_bf = [held("wk_bf%d" % i, [P, len(panels), P, 4], BF16) for i, panels in enumerate(calls)]
         wk_place = {panel: (call, i) for call, panels in enumerate(calls) for i, panel in enumerate(panels)}
-        wk_raw = [held("wk_raw%d" % e, [P, 4, K], F32) for e in range(E)]
+        wk_three = held("wk_three", [P, 3, 4, K], F32)
+        wk_raw = [wk_three[:, e - 2] if e in (2, 3, 4) else held("wk_raw%d" % e, [P, 4, K], F32)[:] for e in range(E)]
         gate_sb = held("gate_sb", [P, S], F32)
         turned_blocks = list(range(TURNED, LATE, P))
         gate_columns = held("gate_columns", [P, len(turned_blocks)], F32)
@@ -130,7 +131,7 @@ def tile_moe_qkb_kernel(
                               in_=w4_words_hbm[g].rearrange("e s p b -> p (e s) b").bitcast(I32))
 
         def load_wk(e):
-            nc.sync.dma_start(out=wk_raw[e][:], in_=wk[e].rearrange("(p j) c -> p j c", j=4))
+            nc.sync.dma_start(out=wk_raw[e], in_=wk[e].rearrange("(p j) c -> p j c", j=4))
 
         def round_wk(e):
             for h in range(2):
@@ -182,7 +183,7 @@ def tile_moe_qkb_kernel(
                 nc.tensor.matmul_mx(
                     out=sums[span][:, a - first : b - first], lhsT=still[0], lhsT_scale=still[1],
                     rhs=moving[0], rhs_scale=moving[1],
-                    start=(g == "q" and a == first and span in opens),
+                    start=(g == ("v" if span in first_spans else "q") and a == first and span in opens),
                     stop=(g == "k" and b == last and span in closes))
 
         def staged_name(span):
@@ -217,29 +218,25 @@ def tile_moe_qkb_kernel(
         load_tok_scales("k", range(4))
         load_tok_words("k")
         load_wk(1)
-        load_wk(2)
-        load_w4_scales("q", (0, 1))
-        load_wk(3)
-        load_w4_scales("q", (2, 3))
-        load_wk(4)
-        load_w4_scales("v", (0, 1))
+        nc.sync.dma_start(out=wk_three[:], in_=wk[2:5].rearrange("e (p j) c -> p e j c", j=4))
+        load_w4_scales("v", range(4))
         load_wk(5)
-        load_w4_scales("v", (2, 3))
-        load_w4_words("q")
+        load_w4_scales("q", range(4))
         load_w4_words("v")
-        nc.sync.dma_start(out=gate_sb[:], in_=gate)
-        nc.sync.dma_start(out=pos_sb[0][:], in_=pos1)
-        nc.sync.dma_start(out=pos_sb[1][:], in_=pos2)
-        with nc.allow_non_contiguous_dma(reason="one weight a partition"):
-            nc.sync.dma_start(out=gate_columns[:], in_=gate[0, TURNED:LATE].rearrange("(b p) -> p b", p=P))
+        load_w4_words("q")
 
         for e in range(E):
             round_wk(e)
 
         slot_rows_q = gather(tok_scales["q"][:], U8, "slot_rows_q", (0, S))
         for quadrant in range(4):
-            nc.gpsimd.dma_start(out=slot_scales_q[32 * quadrant : 32 * quadrant + 4, :].bitcast(I32),
-                                in_=slot_rows_q[8 * quadrant : 8 * quadrant + 8 : 2, :].bitcast(I32))
+            nc.sync.dma_start(out=slot_scales_q[32 * quadrant : 32 * quadrant + 4, :].bitcast(I32),
+                              in_=slot_rows_q[8 * quadrant : 8 * quadrant + 8 : 2, :].bitcast(I32))
+        nc.sync.dma_start(out=gate_sb[:], in_=gate)
+        nc.sync.dma_start(out=pos_sb[0][:], in_=pos1)
+        nc.sync.dma_start(out=pos_sb[1][:], in_=pos2)
+        with nc.allow_non_contiguous_dma(reason="one weight a partition"):
+            nc.sync.dma_start(out=gate_columns[:], in_=gate[0, TURNED:LATE].rearrange("(b p) -> p b", p=P))
         file_slots(slot_scales, "q", slot_scales_q, 0, S)
         gather_words("q", "slot_words_q", (0, S))
         gather_scales("v", "slot_scales_v", (0, S))
@@ -253,7 +250,7 @@ def tile_moe_qkb_kernel(
         gather_words("k", "late_words_k", (LATE, LAST, S))
 
         middle_spans = turned_spans + second_spans + [filler_span]
-        for g in packed:
+        for g in packed[::-1]:
             for span in first_spans:
                 passes(g, span)
         for span in middle_spans:

from contextlib import ExitStack

import concourse.mybir as mybir
from concourse.masks import make_identity

K, T, E, C, N = 256, 768, 6, 256, 512
S = E * C
P = 128
BLOCKS = N // 32
PER_COLUMN = 16
FLOPS = 2 * 3 * S * N * K

FIRST = 2 * C
LATE = S - 3 * P
TURNED = LATE - P
FILLER = LATE - 3 * P
LAST = S - P

WHOLE_WINDOW = 2048
EARLY_WINDOW = 1536
RUN_WINDOW = 896
SCALAR_FIRST = 288
FUSED_END = 288
PLAIN_CUTS = (FUSED_END, 576, T)

F32 = mybir.dt.float32
BF16 = mybir.dt.bfloat16
I32 = mybir.dt.int32
U32 = mybir.dt.uint32
U16 = mybir.dt.uint16
U8 = mybir.dt.uint8
FP8X4 = mybir.dt.float8_e4m3fn_x4
FP4X4 = mybir.dt.float4_e2m1fn_x4
MULT = mybir.AluOpType.mult
ADD = mybir.AluOpType.add
COPY = mybir.ActivationFunctionType.Copy


def pieces(cuts):
    return list(zip(cuts[:-1], cuts[1:]))


def tile_moe_qkb_kernel(
    tc, dq_words, dq_scales, dk_words, dk_scales, dv_words, dv_scales,
    wq_words, wq_scales, wk, wv_words, wv_scales, gate, offs, pos1, pos2, out,
):
    nc = tc.nc
    with ExitStack() as ctx:
        lists = ctx.enter_context(tc.tile_pool(name="lists", bufs=1))
        sb = ctx.enter_context(tc.tile_pool(name="sb", bufs=1))
        shared = ctx.enter_context(tc.tile_pool(name="shared", bufs=1))
        ps = ctx.enter_context(tc.psum_pool(name="ps", bufs=1))

        raw_bytes = 4 * 4 * K
        shared_offsets = {
            "wk_raw%d" % (E - 1): 0, "second_words_k": 0,
            "wk_bf1": raw_bytes, "late_words_k": raw_bytes, "late_scales_k": raw_bytes + 4 * (S - LATE),
        }

        def held(name, shape, dtype):
            if name in shared_offsets:
                return shared.tile(shape, dtype, name=name, align_bytes=64, offset=shared_offsets[name])
            return sb.tile(shape, dtype, name=name, align_bytes=64)

        offs_sb = lists.tile([P, S // PER_COLUMN], U16, name="offs_sb")
        pos_sb = [lists.tile([P, T // PER_COLUMN], U16, name="pos%d_sb" % r) for r in (1, 2)]

        packed = ("q", "v")
        word_columns = {"q": WHOLE_WINDOW, "v": WHOLE_WINDOW, "k": RUN_WINDOW}
        scale_columns = {"q": WHOLE_WINDOW, "v": WHOLE_WINDOW, "k": EARLY_WINDOW}
        tok_words = {g: held("tok_words_" + g, [P, width], I32) for g, width in word_columns.items()}
        tok_scales = {g: held("tok_scales_" + g, [P, width], U8) for g, width in scale_columns.items()}
        slot_scales_q = held("slot_plane_q", [P, S], U8)
        slot_words = {}
        slot_scales = {}
        w4_words = {g: held("w4_words_" + g, [P, E, 2 * K], U8) for g in packed}
        w4_scales = {g: held("w4_scales_" + g, [P, E, K], U8) for g in packed}

        calls = [[(e, h) for e in experts for h in range(2)] for experts in (range(2), range(2, E))]
        wk_words = [held("wk_words%d" % i, [P, len(panels), P], U32) for i, panels in enumerate(calls)]
        wk_scales = [held("wk_scales%d" % i, [P, len(panels), P], U8) for i, panels in enumerate(calls)]
        wk_bf = [held("wk_bf%d" % i, [P, len(panels), P, 4], BF16) for i, panels in enumerate(calls)]
        wk_place = {panel: (call, i) for call, panels in enumerate(calls) for i, panel in enumerate(panels)}
        wk_three = held("wk_three", [P, 3, 4, K], F32)
        wk_raw = [wk_three[:, e - 2] if e in (2, 3, 4) else held("wk_raw%d" % e, [P, 4, K], F32)[:] for e in range(E)]
        gate_sb = held("gate_sb", [P, S], F32)
        turned_blocks = list(range(TURNED, LATE, P))
        gate_columns = held("gate_columns", [P, len(turned_blocks)], F32)
        identity = held("identity", [P, P], F32)
        dx = [held("dx%d" % h, [P, S], F32) for h in range(2)]
        picked = [held("picked%d" % h, [P, T], F32) for h in range(2)]

        first_spans = [(h, 0, FIRST) for h in range(2)]
        second_spans = [(0, FIRST, FILLER), (1, FIRST, TURNED)]
        filler_span = (0, FILLER, LATE)
        turned_spans = [(1, a, a + P) for a in turned_blocks]
        late_spans = [(0, LATE, LAST), (1, LATE, LAST), (0, LAST, S), (1, LAST, S)]
        groups = [[span] for span in first_spans + second_spans[1:] + late_spans[0::3]]
        groups = groups + [turned_spans + second_spans[:1], late_spans[1:3], [filler_span]]
        sums = {}
        for i, group in enumerate(groups):
            bank = ps.tile([P, sum(b - a for h, a, b in group)], F32, name="bank%d" % i)
            column = 0
            for h, a, b in group:
                sums[h, a, b] = bank[:, column : column + b - a]
                column = column + b - a
        opens = [group[0] for group in groups]
        closes = [group[-1] for group in groups]

        tok_words_hbm = {"q": dq_words, "k": dk_words, "v": dv_words}
        tok_scales_hbm = {"q": dq_scales, "k": dk_scales, "v": dv_scales}
        w4_words_hbm = {"q": wq_words, "v": wv_words}
        w4_scales_hbm = {"q": wq_scales, "v": wv_scales}

        def load_tok_scales(g, rs):
            rows = tok_scales_hbm[g][0].rearrange("(m r) t -> r m t", r=4)
            for r in rs:
                nc.sync.dma_start(out=tok_scales[g][r:P:32, :T].bitcast(I32), in_=rows[r].bitcast(I32))

        def load_tok_words(g):
            nc.sync.dma_start(out=tok_words[g][:, :T],
                              in_=tok_words_hbm[g][0].rearrange("p t d -> p (t d)").bitcast(I32))

        def load_w4_scales(g, rs):
            rows = w4_scales_hbm[g].rearrange("e s (m r) c -> r m (e s) c", r=4)
            for r in rs:
                nc.sync.dma_start(out=w4_scales[g][r:P:32, :, :].bitcast(I32), in_=rows[r].bitcast(I32))

        def load_w4_words(g):
            nc.sync.dma_start(out=w4_words[g][:].bitcast(I32),
                              in_=w4_words_hbm[g].rearrange("e s p b -> p (e s) b").bitcast(I32))

        def load_wk(e):
            nc.sync.dma_start(out=wk_raw[e], in_=wk[e].rearrange("(p j) c -> p j c", j=4))

        def round_wk(e):
            for h in range(2):
                call, i = wk_place[e, h]
                nc.scalar.copy(out=wk_bf[call][:, i].rearrange("p (c i) j -> p c j i", i=4),
                               in_=wk_raw[e][:, :, h * P : (h + 1) * P].rearrange("p j (c i) -> p c j i", i=4))

        def quantize_wk(call):
            nc.vector.quantize_mx(
                out=wk_words[call][:].rearrange("p e c -> p (e c)").bitcast(FP8X4),
                scales=wk_scales[call][:].rearrange("p e c -> p (e c)"),
                in_=wk_bf[call][:].rearrange("p e c j -> p (e c j)"),
            )

        def entries(list_sb, a, b):
            return list_sb[:, a // PER_COLUMN : b // PER_COLUMN]

        def gather(window, dtype, name, cuts):
            first = cuts[0]
            tile = held(name, [P, cuts[-1] - first], dtype)
            for a, b in pieces(cuts):
                nc.vector.tensor_copy(out=tile[:, a - first : b - first], in_=window.indirect(entries(offs_sb, a, b)))
            return tile

        def file_slots(places, g, tile, first, last):
            for a in range(first, last, P):
                places[g, a // P] = (tile, first)

        def gather_words(g, name, cuts):
            file_slots(slot_words, g, gather(tok_words[g][:].bitcast(U32), U32, name, cuts), cuts[0], cuts[-1])

        def gather_scales(g, name, cuts):
            file_slots(slot_scales, g, gather(tok_scales[g][:], U8, name, cuts), cuts[0], cuts[-1])

        def weights(g, e, h):
            if g in packed:
                return w4_words[g][:, e, 2 * h * P : 2 * (h + 1) * P].bitcast(FP4X4), w4_scales[g][:, e, h * P : (h + 1) * P]
            call, i = wk_place[e, h]
            return wk_words[call][:, i].bitcast(FP8X4), wk_scales[call][:, i]

        def passes(g, span):
            h, first, last = span
            for a, b in pieces([first] + [x for x in range(0, S, C) if first < x < last] + [last]):
                (words, first_word), (scales, first_scale) = slot_words[g, a // P], slot_scales[g, a // P]
                tokens = (words[:, a - first_word : b - first_word].bitcast(FP8X4),
                          scales[:, a - first_scale : b - first_scale])
                matrix = weights(g, a // C, h)
                still, moving = (tokens, matrix) if span in turned_spans else (matrix, tokens)
                nc.tensor.matmul_mx(
                    out=sums[span][:, a - first : b - first], lhsT=still[0], lhsT_scale=still[1],
                    rhs=moving[0], rhs_scale=moving[1],
                    start=(g == ("v" if span in first_spans else "q") and a == first and span in opens),
                    stop=(g == "k" and b == last and span in closes))

        def staged_name(span):
            return "staged%d_%d" % span[:2]

        def stage(span):
            staged = held(staged_name(span), [P, span[2] - span[1]], F32)
            nc.scalar.copy(out=staged[:], in_=sums[span])
            return staged

        def gate_by_gpsimd(span):
            h, a, b = span
            nc.gpsimd.tensor_tensor(out=dx[h][:, a:b], in0=stage(span)[:], in1=gate_sb[:, a:b], op=MULT)

        def gate_by_vector(span):
            h, a, b = span
            nc.vector.tensor_tensor(out=dx[h][:, a:b], in0=sums[span], in1=gate_sb[:, a:b], op=MULT)

        for first, last in ((32, 64), (64, P)):
            nc.vector.memset(tok_scales["q"][first:last, :T].bitcast(I32), 0)
        for g in ("v", "k"):
            nc.vector.memset(tok_scales[g][:, :T].bitcast(I32), 0)
        make_identity(nc, identity[:])

        nc.sync.dma_start(out=tok_scales["q"][: 2 * BLOCKS, :T].bitcast(I32),
                          in_=dq_scales[0].bitcast(I32).unsqueeze(1).to_broadcast([BLOCKS, 2, T // 4]))
        nc.sync.dma_start(out=offs_sb[:], in_=offs)
        load_tok_words("q")
        load_tok_scales("v", range(4))
        load_tok_words("v")
        load_wk(0)
        load_tok_scales("k", range(4))
        load_tok_words("k")
        load_wk(1)
        nc.sync.dma_start(out=wk_three[:], in_=wk[2:5].rearrange("e (p j) c -> p e j c", j=4))
        load_w4_scales("v", range(4))
        load_wk(5)
        load_w4_scales("q", range(4))
        load_w4_words("v")
        load_w4_words("q")

        for e in range(E):
            round_wk(e)

        slot_rows_q = gather(tok_scales["q"][:], U8, "slot_rows_q", (0, S))
        for quadrant in range(4):
            nc.sync.dma_start(out=slot_scales_q[32 * quadrant : 32 * quadrant + 4, :].bitcast(I32),
                              in_=slot_rows_q[8 * quadrant : 8 * quadrant + 8 : 2, :].bitcast(I32))
        nc.sync.dma_start(out=gate_sb[:], in_=gate)
        nc.sync.dma_start(out=pos_sb[0][:], in_=pos1)
        nc.sync.dma_start(out=pos_sb[1][:], in_=pos2)
        with nc.allow_non_contiguous_dma(reason="one weight a partition"):
            nc.sync.dma_start(out=gate_columns[:], in_=gate[0, TURNED:LATE].rearrange("(b p) -> p b", p=P))
        file_slots(slot_scales, "q", slot_scales_q, 0, S)
        gather_words("q", "slot_words_q", (0, S))
        gather_scales("v", "slot_scales_v", (0, S))
        gather_words("v", "slot_words_v", (0, S))
        gather_scales("k", "early_scales_k", (0, LATE))
        quantize_wk(0)
        gather_words("k", "wk_raw1", (0, FIRST))
        quantize_wk(1)
        gather_words("k", "second_words_k", (FIRST, LATE))
        gather_scales("k", "late_scales_k", (LATE, S))
        gather_words("k", "late_words_k", (LATE, LAST, S))

        middle_spans = turned_spans + second_spans + [filler_span]
        for g in packed[::-1]:
            for span in first_spans:
                passes(g, span)
        for span in middle_spans:
            passes("q", span)
        for span in first_spans:
            passes("k", span)
            gate_by_gpsimd(span)
        for span in middle_spans:
            passes("v", span)
        for g in packed:
            for span in late_spans:
                passes(g, span)
        for span in middle_spans:
            passes("k", span)
        gated = held("gated", [P, len(turned_spans), P], F32)
        for i, span in enumerate(turned_spans):
            nc.scalar.activation(out=gated[:, i], in_=sums[span], func=COPY, scale=gate_columns[:, i : i + 1])
        gate_by_gpsimd(second_spans[0])
        gate_by_gpsimd(second_spans[1])
        for span in late_spans[:3]:
            passes("k", span)
        turned_back = ps.tile([P, len(turned_spans), P], F32, name="bank0")
        for i in range(len(turned_spans)):
            nc.tensor.transpose(turned_back[:, i], gated[:, i], identity[:])
        passes("k", late_spans[3])
        nc.scalar.copy(out=dx[1][:, TURNED:LATE], in_=turned_back[:].rearrange("p b s -> p (b s)"))
        for span in (filler_span, late_spans[0], late_spans[2], late_spans[1], late_spans[3]):
            gate_by_vector(span)

        summed = [held("summed%d" % h, [P, T], F32) for h in range(2)]
        other = held("other", [P, T - FUSED_END], F32)

        def pick_on_scalar(tile, h, r, a, b):
            nc.scalar.activation(out=tile, in_=dx[h][:].indirect(entries(pos_sb[r], a, b)), func=COPY)

        def pick_and_add(h, a, b):
            nc.vector.tensor_tensor(out=summed[h][:, a:b], in0=dx[h][:].indirect(entries(pos_sb[1], a, b)),
                                    in1=picked[h][:, a:b], op=ADD)

        def store(h, a, b):
            nc.sync.dma_start(out=out[h * P : (h + 1) * P, a:b], in_=summed[h][:, a:b])

        pick_on_scalar(picked[0][:, :SCALAR_FIRST], 0, 0, 0, SCALAR_FIRST)
        nc.vector.tensor_copy(out=picked[0][:, SCALAR_FIRST:], in_=dx[0][:].indirect(entries(pos_sb[0], SCALAR_FIRST, T)))
        pick_on_scalar(picked[1][:], 1, 0, 0, T)
        for a, b in pieces(PLAIN_CUTS):
            pick_on_scalar(other[:, a - FUSED_END : b - FUSED_END], 1, 1, a, b)
        for a, b in pieces((0, SCALAR_FIRST, T)):
            pick_and_add(0, a, b)
            store(0, a, b)
        pick_and_add(1, 0, FUSED_END)
        store(1, 0, FUSED_END)
        for a, b in pieces(PLAIN_CUTS):
            nc.vector.tensor_tensor(out=summed[1][:, a:b], in0=other[:, a - FUSED_END : b - FUSED_END],
                                    in1=picked[1][:, a:b], op=ADD)
            store(1, a, b)
